import numpy as np
import ml_dtypes


def mxq(x, axis, fmt="e4m3"):
    dtype, down = {"e4m3": (ml_dtypes.float8_e4m3fn, 7), "e5m2": (ml_dtypes.float8_e5m2, 14)}[fmt]
    v = np.moveaxis(np.asarray(x, np.float32).astype(ml_dtypes.bfloat16).astype(np.float64), axis, -1)
    blocks = v.reshape(v.shape[:-1] + (-1, 32))
    amax = np.abs(blocks).max(-1, keepdims=True)
    byte = np.maximum(np.where(amax > 0, np.frexp(amax)[1] - 1 + 127, 0) - down, 1)
    scale = np.exp2(byte - 127.0)
    codes = (blocks / scale).astype(np.float32).astype(dtype).astype(np.float64)
    return np.moveaxis((codes * scale).reshape(v.shape), -1, axis)


WIDE = False


def mx_kscale(k):
    if not WIDE:
        return np.ones(k)
    levels = np.array([10, -10, 5, -5, 0])
    if k % 512:
        return np.exp2(np.random.permutation(np.resize(levels, k // 32))).repeat(32)
    a = np.empty((k // 512, 16))
    for p in range(k // 512):
        a[p, :8] = np.random.permutation(np.resize(levels, 8))
        for g in range(8):
            far = levels[np.abs(levels - a[p, g]) >= 10]
            a[p, g + 8] = far[np.random.randint(len(far))]
    return np.exp2(a.ravel()).repeat(32)


def f64(x):
    return np.asarray(x).astype(np.float64)


def striped(idx):
    return np.tile(idx.reshape(-1, 16).T, (8, 1)).astype(np.uint16)


def unstriped(offs):
    return offs[:16].T.reshape(-1).astype(np.int64)


def pack_weight(w):
    k, n = w.shape
    w = f64(np.asarray(w, np.float32).astype(ml_dtypes.bfloat16)).reshape(k // 32, 32, n)
    amax = np.abs(w).max(1)
    byte = np.clip(np.where(amax > 0, np.frexp(amax)[1] - 1 + 127 - 7, 1), 1, 254)
    scaled = (w * np.exp2(127.0 - byte)[:, None, :]).reshape(k, n).astype(np.float32)
    words = np.ascontiguousarray(scaled.reshape(k // 512, 128, 4, n).transpose(0, 1, 3, 2)).astype(ml_dtypes.float8_e4m3fn).view(np.uint8)
    return words, np.ascontiguousarray(byte.astype(np.uint8).reshape(k // 512, 16, n))


def unpack_weight(words, scales):
    g, p, n, _ = words.shape
    vals = np.ascontiguousarray(words).view(ml_dtypes.float8_e4m3fn).astype(np.float64) * np.repeat(np.exp2(scales.astype(np.float64) - 127.0), 8, axis=1)[..., None]
    return vals.transpose(0, 1, 3, 2).reshape(g * 512, n)


K, T, S, H, D, W, U = 1024, 1024, 512, 512, 4, 2048, 512
P = 2 ** 7


def setup_inputs():
    n = np.random.standard_normal
    s = mx_kscale(K)[:, None]
    u = mx_kscale(H)
    packed_xT = pack_weight(n((K, T)) * s)
    packed_eT = pack_weight(n((H, W)) / np.sqrt(H) / u[:, None])
    return {
        "x_words": packed_xT[0],
        "x_scales": packed_xT[1],
        "w1": (n((K, H)) / np.sqrt(K) / s * u).astype(np.float32),
        "e_words": packed_eT[0],
        "e_scales": packed_eT[1],
        "half": (np.tile(np.random.uniform(0.2, 1.0, W), (P, 1))).astype(np.float32),
        "own": (-np.random.uniform(0.2, 1.0, (S, 1))).astype(np.float32),
        "alpha": (np.tile(n(W), (P, 1))).astype(np.float32),
        "offs": striped(np.random.permutation(T)[:S]),
        "sv": striped(np.random.permutation(W)[:U]),
    }


def reference(x_words, x_scales, w1, e_words, e_scales, half, own, alpha, offs, sv):
    xq = unpack_weight(x_words, x_scales)[:, unstriped(offs)]
    h = mxq(f64(w1), 0, "e4m3").T @ xq
    e_sv = unpack_weight(e_words, e_scales)[:, unstriped(sv)]
    y = mxq(h, 0, "e4m3").T @ e_sv
    ee = np.exp(0.5 * y + f64(own) - (f64(half)[:1][:, unstriped(sv)]))
    gg = ee * (f64(alpha)[:1][:, unstriped(sv)])
    return gg.reshape(len(gg), -1, D).sum(axis=2)

@@ -1,0 +1,204 @@
+from contextlib import ExitStack
+
+import concourse.mybir as mybir
+from concourse.masks import make_identity
+
+F32 = mybir.dt.float32
+BF16 = mybir.dt.bfloat16
+I32 = mybir.dt.int32
+U32 = mybir.dt.uint32
+U16 = mybir.dt.uint16
+U8 = mybir.dt.uint8
+FP8X4 = mybir.dt.float8_e4m3fn_x4
+ALU = mybir.AluOpType
+ACT = mybir.ActivationFunctionType
+
+P = 128
+K, T, S, H, D, W, U = 1024, 1024, 512, 512, 4, 2048, 512
+FLOPS = 2 * K * H * S + 2 * H * S * U
+
+
+def tile_picked_yrbf_sum_p_kernel(
+    tc, x_words, x_scales, w1, e_words, e_scales, half, own, alpha, offs, sv, out
+):
+    nc = tc.nc
+    with ExitStack() as ctx:
+        keep = ctx.enter_context(tc.tile_pool(name="keep", bufs=1))
+        psum = ctx.enter_context(tc.psum_pool(name="psum", bufs=1))
+
+        offs_sb = keep.tile([P, S // 16], U16, name="offs_sb")
+        sv_sb = keep.tile([P, U // 16], U16, name="sv_sb")
+        xs = keep.tile([P, T], U8, name="xs", tag="xs", align_bytes=64)
+        es = keep.tile([P, W], U8, name="es", tag="es", align_bytes=64)
+        ha = keep.tile([P, W], F32, name="ha", tag="ha", align_bytes=64)
+        xw = [keep.tile([P, T], I32, name="xw%d" % o, tag="xw%d" % o, align_bytes=64) for o in range(2)]
+        ew = keep.tile([P, W], I32, name="ew", tag="ew", align_bytes=64)
+        cut = ((0, 256, 512), (0, 384, 512))
+        raw = [[keep.tile([P, 4, cut[o][c + 1] - cut[o][c]], F32, name="raw%d%d" % (o, c), tag="raw%d%d" % (o, c), align_bytes=64) for c in range(2)] for o in range(2)]
+        own_c = keep.tile([P, 4], F32, name="own_c")
+        ident = keep.tile([P, P], F32, name="ident")
+        warm = keep.tile([P, 1], F32, name="warm")
+        warm2 = keep.tile([P, 1], F32, name="warm2")
+
+        nc.gpsimd.memset(xs[:].bitcast(I32), 0)
+        nc.vector.memset(warm[:], 0.0)
+        nc.vector.memset(ha[:, 0:1024], 0.0)
+        nc.gpsimd.memset(ha[:, 1024:W], 0.0)
+        nc.vector.memset(es[:].bitcast(I32), 0)
+        nc.scalar.activation(warm2[:], warm[:], ACT.Exp)
+
+        def load_w(o, c):
+            rows = w1[512 * o : 512 * (o + 1), cut[o][c] : cut[o][c + 1]]
+            nc.sync.dma_start(raw[o][c][:], rows.rearrange("(p j) c -> p j c", j=4))
+
+        def load_words(tile, words):
+            nc.sync.dma_start(tile[:], words.rearrange("p c r -> p (c r)").bitcast(I32))
+
+        def load_xs(q):
+            nc.sync.dma_start(xs[32 * q : 32 * q + 8, :].bitcast(I32), x_scales[:, 4 * q : 4 * q + 4, :].bitcast(I32))
+
+        def load_es(q):
+            nc.sync.dma_start(es[32 * q : 32 * q + 4, :].bitcast(I32), e_scales[0, 4 * q : 4 * q + 4, :].bitcast(I32))
+
+        nc.sync.dma_start(offs_sb[:], offs)
+        for q in range(4):
+            load_xs(q)
+        nc.sync.dma_start(sv_sb[:], sv)
+        nc.scalar.dma_start(ha[0:1, :], half[0:1, :])
+        nc.scalar.dma_start(ha[64:65, :], alpha[0:1, :])
+        load_w(0, 0)
+        load_w(0, 1)
+        for q in range(4):
+            load_es(q)
+        load_w(1, 0)
+        load_words(xw[0], x_words[0])
+        load_w(1, 1)
+        load_words(xw[1], x_words[1])
+        load_words(ew, e_words[0])
+        nc.gpsimd.dma_start(own_c[:], own.rearrange("(p s) o -> p (s o)", s=4))
+        make_identity(nc, ident[:])
+
+        xs_g = keep.tile([P, S], U8, name="xs_g", align_bytes=64)
+        nc.vector.tensor_copy(xs_g[:], xs[:].indirect(offs_sb[:]))
+        ha_g = keep.tile([P, U], F32, name="ha_g", tag="xs", align_bytes=64)
+        nc.vector.tensor_copy(ha_g[:], ha[:].indirect(sv_sb[:]))
+
+        w_bf = [keep.tile([P, 4 * H], BF16, name="w_bf%d" % o, tag="w_bf%d" % o, align_bytes=64) for o in range(2)]
+        w_q = [keep.tile([P, H], U32, name="w_q%d" % o, tag=("es", "xw0")[o], align_bytes=64) for o in range(2)]
+        w_s = [keep.tile([P, H], U8, name="w_s%d" % o, align_bytes=64) for o in range(2)]
+        for o in range(2):
+            for c in range(2):
+                nc.scalar.copy(
+                    w_bf[o][:].rearrange("p (r m j) -> p m j r", r=4, j=4)[:, cut[o][c] // 4 : cut[o][c + 1] // 4],
+                    raw[o][c][:].rearrange("p j (m r) -> p m j r", r=4),
+                )
+        es_g = keep.tile([P, U], U8, name="es_g", tag="ha", align_bytes=64)
+        nc.vector.tensor_copy(es_g[:], es[:].indirect(sv_sb[:]))
+        nc.vector.quantize_mx(out=w_q[0][:].bitcast(FP8X4), scales=w_s[0][:], in_=w_bf[0][:])
+        es_p = keep.tile([P, D, P], U8, name="es_p", tag="w_bf0", align_bytes=64)
+        nc.vector.tensor_copy(es_p[:], es_g[:].rearrange("p (v d) -> p d v", d=D))
+        x_a = [keep.tile([P, P], U32, name="x_a%d" % o, tag=("ha", "w_bf1")[o], align_bytes=64) for o in range(2)]
+        x_b = [keep.tile([P, S - P], U32, name="x_b%d" % o, align_bytes=64) for o in range(2)]
+
+        def gather_x(o):
+            nc.vector.tensor_copy(x_a[o][:], xw[o][:].bitcast(U32).indirect(offs_sb[:, 0 : P // 16]))
+            nc.vector.tensor_copy(x_b[o][:], xw[o][:].bitcast(U32).indirect(offs_sb[:, P // 16 : S // 16]))
+
+        gather_x(0)
+        nc.vector.quantize_mx(out=w_q[1][:].bitcast(FP8X4), scales=w_s[1][:], in_=w_bf[1][:])
+        gather_x(1)
+
+        ha_ps = psum.tile([P, D, P], F32, name="ha_ps", tag="y0")
+        for d in range(D):
+            nc.tensor.transpose(ha_ps[:, d, :], ha_g[:, d:U:D], ident[:])
+        coef = keep.tile([P, 2, D], F32, name="coef", tag="raw10", align_bytes=64)
+        neg_half = coef[:, 0, :]
+        alpha_c = coef[:, 1, :]
+        nc.scalar.activation(neg_half, ha_ps[:, :, 0], ACT.Copy, scale=-1.0)
+        nc.scalar.copy(alpha_c, ha_ps[:, :, 64])
+        own_ps = psum.tile([P, 4, P], F32, name="own_ps", tag="y1")
+        for s in range(4):
+            nc.tensor.transpose(own_ps[:, s, :], own_c[:, s : s + 1].to_broadcast([P, P]), ident[:])
+        own_b = keep.tile([P, S], F32, name="own_b", tag="raw11", align_bytes=64)
+        nc.scalar.copy(own_b[:].rearrange("m (p s) -> m p s", s=4), own_ps[:].rearrange("m s p -> m p s"))
+
+        junk = psum.tile([P, 512], F32, name="junk", tag="y2")
+        for rep in range(3):
+            nc.tensor.matmul_mx(out=junk[:], lhsT=x_a[0][:].bitcast(FP8X4), lhsT_scale=xs_g[:, 0:P], rhs=w_q[0][:].bitcast(FP8X4), rhs_scale=w_s[0][:], start=True, stop=True)
+        h_bf = [keep.tile([P, 256, 4], BF16, name="h_bf%d" % th, align_bytes=64) for th in range(2)]
+        for tb in range(4):
+            cols = slice(P * tb, P * (tb + 1))
+            h_ps = psum.tile([P, 4, P], F32, name="h_ps%d" % tb, tag="h%d" % tb)
+            for r in range(4):
+                ch = slice(P * r, P * (r + 1))
+                for o in range(2):
+                    nc.tensor.matmul_mx(
+                        out=h_ps[:, r, :],
+                        lhsT=w_q[o][:, ch].bitcast(FP8X4),
+                        lhsT_scale=w_s[o][:, ch],
+                        rhs=(x_a[o][:] if tb == 0 else x_b[o][:, P * (tb - 1) : P * tb]).bitcast(FP8X4),
+                        rhs_scale=xs_g[4 * o : P, cols],
+                        start=(o == 0),
+                        stop=(o == 1),
+                    )
+            nc.scalar.copy(h_bf[tb // 2][:, P * (tb % 2) : P * (tb % 2 + 1), :], h_ps[:].rearrange("p r t -> p t r"))
+
+        e_g = keep.tile([P, D, P], U32, name="e_g", tag="xw1", align_bytes=64)
+        nc.vector.tensor_copy(e_g[:].rearrange("p d v -> p v d"), ew[:].bitcast(U32).indirect(sv_sb[:]))
+
+        h_q = [keep.tile([P, 256], U32, name="h_q0", tag="ew", align_bytes=64), keep.tile([P, 256], U32, name="h_q1", align_bytes=64)]
+        h_s = [keep.tile([P, 256], U8, name="h_s%d" % th, align_bytes=64) for th in range(2)]
+        for th in range(2):
+            nc.vector.quantize_mx(out=h_q[th][:].bitcast(FP8X4), scales=h_s[th][:], in_=h_bf[th][:].rearrange("p t r -> p (t r)"))
+
+        for th in range(2):
+            tcols = slice(256 * th, 256 * (th + 1))
+            if th == 0:
+                o_both = psum.tile([P, 2, P], F32, name="o_both", tag="h0")
+            else:
+                o_ps = [psum.tile([P, P], F32, name="o_ps%d" % s, tag="h%d" % (2 + s)) for s in range(2)]
+            ggs = []
+            for dp in range(2):
+                u = 2 * th + dp
+                y_ps = psum.tile([P, 2, 256], F32, name="y_ps%d" % u, tag="y%d" % u)
+                for dd in range(2):
+                    d = 2 * dp + dd
+                    nc.tensor.matmul_mx(
+                        out=y_ps[:, dd, :],
+                        lhsT=e_g[:, d, :].bitcast(FP8X4),
+                        lhsT_scale=es_p[:, d, :],
+                        rhs=h_q[th][:].bitcast(FP8X4),
+                        rhs_scale=h_s[th][:],
+                        start=True,
+                        stop=True,
+                    )
+                arg = keep.tile([P, 2, 256], F32, name="arg%d" % u)
+                nc.vector.scalar_tensor_tensor(
+                    arg[:], y_ps[:], 0.5, own_b[:, tcols].unsqueeze(1).to_broadcast([P, 2, 256]), ALU.mult, ALU.add
+                )
+                for dd in range(2):
+                    d = 2 * dp + dd
+                    ee = keep.tile([P, 256], F32, name="ee%d%d" % (u, dd))
+                    nc.scalar.activation(ee[:], arg[:, dd, :], ACT.Exp, bias=neg_half[:, d : d + 1])
+                    gg = keep.tile([P, 256], F32, name="gg%d%d" % (u, dd))
+                    if th == 0:
+                        nc.gpsimd.tensor_scalar(gg[:], ee[:], alpha_c[:, d : d + 1], 0.0, ALU.mult, ALU.add)
+                        ggs.append(gg)
+                    else:
+                        nc.vector.tensor_scalar(gg[:], ee[:], alpha_c[:, d : d + 1], None, ALU.mult)
+                        for s in range(2):
+                            nc.tensor.matmul(
+                                o_ps[s][:], gg[:, P * s : P * (s + 1)], ident[:], start=(d == 0), stop=(d == D - 1), is_transpose=True
+                            )
+            res = keep.tile([P, 2, P], F32, name="res%d" % th)
+            if th == 0:
+                for s in range(2):
+                    for d in range(D):
+                        nc.tensor.matmul(
+                            o_both[:, s, :], ggs[d][:, P * s : P * (s + 1)], ident[:], start=(d == 0), stop=(d == D - 1), is_transpose=True
+                        )
+                nc.vector.tensor_copy(res[:], o_both[:])
+            else:
+                nc.scalar.copy(res[:, 0, :], o_ps[0][:])
+                nc.vector.tensor_copy(res[:, 1, :], o_ps[1][:])
+            nc.sync.dma_start(out[tcols, :].rearrange("(s p) v -> p s v", s=2), res[:])

@@ -33,8 +33,7 @@ def tile_picked_yrbf_sum_p_kernel(
         ha = keep.tile([P, W], F32, name="ha", tag="ha", align_bytes=64)
         xw = [keep.tile([P, T], I32, name="xw%d" % o, tag="xw%d" % o, align_bytes=64) for o in range(2)]
         ew = keep.tile([P, W], I32, name="ew", tag="ew", align_bytes=64)
-        cut = ((0, 256, 512), (0, 384, 512))
-        raw = [[keep.tile([P, 4, cut[o][c + 1] - cut[o][c]], F32, name="raw%d%d" % (o, c), tag="raw%d%d" % (o, c), align_bytes=64) for c in range(2)] for o in range(2)]
+        raw = [keep.tile([P, 4, H], F32, name="raw%d" % o, tag="raw%d" % o, align_bytes=64) for o in range(2)]
         own_c = keep.tile([P, 4], F32, name="own_c")
         ident = keep.tile([P, P], F32, name="ident")
         warm = keep.tile([P, 1], F32, name="warm")
@@ -47,9 +46,9 @@ def tile_picked_yrbf_sum_p_kernel(
         nc.vector.memset(es[:].bitcast(I32), 0)
         nc.scalar.activation(warm2[:], warm[:], ACT.Exp)
 
-        def load_w(o, c):
-            rows = w1[512 * o : 512 * (o + 1), cut[o][c] : cut[o][c + 1]]
-            nc.sync.dma_start(raw[o][c][:], rows.rearrange("(p j) c -> p j c", j=4))
+        def load_w(o):
+            rows = w1[512 * o : 512 * (o + 1), :]
+            nc.sync.dma_start(raw[o][:], rows.rearrange("(p j) c -> p j c", j=4))
 
         def load_words(tile, words):
             nc.sync.dma_start(tile[:], words.rearrange("p c r -> p (c r)").bitcast(I32))
@@ -58,7 +57,7 @@ def tile_picked_yrbf_sum_p_kernel(
             nc.sync.dma_start(xs[32 * q : 32 * q + 8, :].bitcast(I32), x_scales[:, 4 * q : 4 * q + 4, :].bitcast(I32))
 
         def load_es(q):
-            nc.sync.dma_start(es[32 * q : 32 * q + 4, :].bitcast(I32), e_scales[0, 4 * q : 4 * q + 4, :].bitcast(I32))
+            nc.scalar.dma_start(es[32 * q : 32 * q + 4, :].bitcast(I32), e_scales[0, 4 * q : 4 * q + 4, :].bitcast(I32))
 
         nc.sync.dma_start(offs_sb[:], offs)
         for q in range(4):
@@ -66,13 +65,11 @@ def tile_picked_yrbf_sum_p_kernel(
         nc.sync.dma_start(sv_sb[:], sv)
         nc.scalar.dma_start(ha[0:1, :], half[0:1, :])
         nc.scalar.dma_start(ha[64:65, :], alpha[0:1, :])
-        load_w(0, 0)
-        load_w(0, 1)
         for q in range(4):
             load_es(q)
-        load_w(1, 0)
+        load_w(0)
+        load_w(1)
         load_words(xw[0], x_words[0])
-        load_w(1, 1)
         load_words(xw[1], x_words[1])
         load_words(ew, e_words[0])
         nc.gpsimd.dma_start(own_c[:], own.rearrange("(p s) o -> p (s o)", s=4))
@@ -87,11 +84,10 @@ def tile_picked_yrbf_sum_p_kernel(
         w_q = [keep.tile([P, H], U32, name="w_q%d" % o, tag=("es", "xw0")[o], align_bytes=64) for o in range(2)]
         w_s = [keep.tile([P, H], U8, name="w_s%d" % o, align_bytes=64) for o in range(2)]
         for o in range(2):
-            for c in range(2):
-                nc.scalar.copy(
-                    w_bf[o][:].rearrange("p (r m j) -> p m j r", r=4, j=4)[:, cut[o][c] // 4 : cut[o][c + 1] // 4],
-                    raw[o][c][:].rearrange("p j (m r) -> p m j r", r=4),
-                )
+            nc.scalar.copy(
+                w_bf[o][:].rearrange("p (r m j) -> p m j r", r=4, j=4),
+                raw[o][:].rearrange("p j (m r) -> p m j r", r=4),
+            )
         es_g = keep.tile([P, U], U8, name="es_g", tag="ha", align_bytes=64)
         nc.vector.tensor_copy(es_g[:], es[:].indirect(sv_sb[:]))
         nc.vector.quantize_mx(out=w_q[0][:].bitcast(FP8X4), scales=w_s[0][:], in_=w_bf[0][:])
@@ -111,16 +107,16 @@ def tile_picked_yrbf_sum_p_kernel(
         ha_ps = psum.tile([P, D, P], F32, name="ha_ps", tag="y0")
         for d in range(D):
             nc.tensor.transpose(ha_ps[:, d, :], ha_g[:, d:U:D], ident[:])
-        coef = keep.tile([P, 2, D], F32, name="coef", tag="raw10", align_bytes=64)
-        neg_half = coef[:, 0, :]
-        alpha_c = coef[:, 1, :]
+        terms = keep.tile([P, S + 2 * D], F32, name="terms", tag="raw1", align_bytes=64)
+        own_b = terms[:, 0:S]
+        neg_half = terms[:, S : S + D]
+        alpha_c = terms[:, S + D : S + 2 * D]
         nc.scalar.activation(neg_half, ha_ps[:, :, 0], ACT.Copy, scale=-1.0)
         nc.scalar.copy(alpha_c, ha_ps[:, :, 64])
         own_ps = psum.tile([P, 4, P], F32, name="own_ps", tag="y1")
         for s in range(4):
             nc.tensor.transpose(own_ps[:, s, :], own_c[:, s : s + 1].to_broadcast([P, P]), ident[:])
-        own_b = keep.tile([P, S], F32, name="own_b", tag="raw11", align_bytes=64)
-        nc.scalar.copy(own_b[:].rearrange("m (p s) -> m p s", s=4), own_ps[:].rearrange("m s p -> m p s"))
+        nc.scalar.copy(own_b.rearrange("m (p s) -> m p s", s=4), own_ps[:].rearrange("m s p -> m p s"))
 
         junk = psum.tile([P, 512], F32, name="junk", tag="y2")
         for rep in range(3):
@@ -182,7 +178,7 @@ def tile_picked_yrbf_sum_p_kernel(
                     nc.scalar.activation(ee[:], arg[:, dd, :], ACT.Exp, bias=neg_half[:, d : d + 1])
                     gg = keep.tile([P, 256], F32, name="gg%d%d" % (u, dd))
                     if th == 0:
-                        nc.gpsimd.tensor_scalar(gg[:], ee[:], alpha_c[:, d : d + 1], 0.0, ALU.mult, ALU.add)
+                        nc.vector.tensor_scalar(gg[:], ee[:], alpha_c[:, d : d + 1], None, ALU.mult)
                         ggs.append(gg)
                     else:
                         nc.vector.tensor_scalar(gg[:], ee[:], alpha_c[:, d : d + 1], None, ALU.mult)
@@ -197,7 +193,7 @@ def tile_picked_yrbf_sum_p_kernel(
                         nc.tensor.matmul(
                             o_both[:, s, :], ggs[d][:, P * s : P * (s + 1)], ident[:], start=(d == 0), stop=(d == D - 1), is_transpose=True
                         )
-                nc.vector.tensor_copy(res[:], o_both[:])
+                nc.scalar.copy(res[:], o_both[:])
             else:
                 nc.scalar.copy(res[:, 0, :], o_ps[0][:])
                 nc.vector.tensor_copy(res[:, 1, :], o_ps[1][:])

@@ -57,17 +57,17 @@ def tile_picked_yrbf_sum_p_kernel(
             nc.sync.dma_start(xs[32 * q : 32 * q + 8, :].bitcast(I32), x_scales[:, 4 * q : 4 * q + 4, :].bitcast(I32))
 
         def load_es(q):
-            nc.scalar.dma_start(es[32 * q : 32 * q + 4, :].bitcast(I32), e_scales[0, 4 * q : 4 * q + 4, :].bitcast(I32))
+            nc.sync.dma_start(es[32 * q : 32 * q + 4, :].bitcast(I32), e_scales[0, 4 * q : 4 * q + 4, :].bitcast(I32))
 
         nc.sync.dma_start(offs_sb[:], offs)
         for q in range(4):
             load_xs(q)
         nc.sync.dma_start(sv_sb[:], sv)
-        nc.scalar.dma_start(ha[0:1, :], half[0:1, :])
-        nc.scalar.dma_start(ha[64:65, :], alpha[0:1, :])
+        load_w(0)
+        nc.sync.dma_start(ha[0:1, :], half[0:1, :])
+        nc.sync.dma_start(ha[64:65, :], alpha[0:1, :])
         for q in range(4):
             load_es(q)
-        load_w(0)
         load_w(1)
         load_words(xw[0], x_words[0])
         load_words(xw[1], x_words[1])
@@ -80,28 +80,35 @@ def tile_picked_yrbf_sum_p_kernel(
         ha_g = keep.tile([P, U], F32, name="ha_g", tag="xs", align_bytes=64)
         nc.vector.tensor_copy(ha_g[:], ha[:].indirect(sv_sb[:]))
 
-        w_bf = [keep.tile([P, 4 * H], BF16, name="w_bf%d" % o, tag="w_bf%d" % o, align_bytes=64) for o in range(2)]
+        w_bf = [[keep.tile([P, 2 * H], BF16, name="w_bf%d%d" % (o, c), tag="w_bf%d%d" % (o, c), align_bytes=64) for c in range(2)] for o in range(2)]
         w_q = [keep.tile([P, H], U32, name="w_q%d" % o, tag=("es", "xw0")[o], align_bytes=64) for o in range(2)]
         w_s = [keep.tile([P, H], U8, name="w_s%d" % o, align_bytes=64) for o in range(2)]
         for o in range(2):
-            nc.scalar.copy(
-                w_bf[o][:].rearrange("p (r m j) -> p m j r", r=4, j=4),
-                raw[o][:].rearrange("p j (m r) -> p m j r", r=4),
-            )
+            for c in range(2):
+                nc.scalar.copy(
+                    w_bf[o][c][:].rearrange("p (r m j) -> p m j r", r=2, j=4),
+                    raw[o][:].rearrange("p j (m r) -> p m j r", r=4)[:, :, :, 2 * c : 2 * c + 2],
+                )
+
+        def quantize_w(o):
+            for c in range(2):
+                half_cols = slice(256 * c, 256 * (c + 1))
+                nc.vector.quantize_mx(out=w_q[o][:, half_cols].bitcast(FP8X4), scales=w_s[o][:, half_cols], in_=w_bf[o][c][:])
+
         es_g = keep.tile([P, U], U8, name="es_g", tag="ha", align_bytes=64)
         nc.vector.tensor_copy(es_g[:], es[:].indirect(sv_sb[:]))
-        nc.vector.quantize_mx(out=w_q[0][:].bitcast(FP8X4), scales=w_s[0][:], in_=w_bf[0][:])
-        es_p = keep.tile([P, D, P], U8, name="es_p", tag="w_bf0", align_bytes=64)
+        quantize_w(0)
+        es_p = keep.tile([P, D, P], U8, name="es_p", tag="w_bf01", align_bytes=64)
         nc.vector.tensor_copy(es_p[:], es_g[:].rearrange("p (v d) -> p d v", d=D))
-        x_a = [keep.tile([P, P], U32, name="x_a%d" % o, tag=("ha", "w_bf1")[o], align_bytes=64) for o in range(2)]
-        x_b = [keep.tile([P, S - P], U32, name="x_b%d" % o, align_bytes=64) for o in range(2)]
+        x_a = [keep.tile([P, P], U32, name="x_a%d" % o, tag=("ha", "w_bf10")[o], align_bytes=64) for o in range(2)]
+        x_b = [keep.tile([P, S - P], U32, name="x_b%d" % o, tag=("x_b0", "w_bf11")[o], align_bytes=64) for o in range(2)]
 
         def gather_x(o):
             nc.vector.tensor_copy(x_a[o][:], xw[o][:].bitcast(U32).indirect(offs_sb[:, 0 : P // 16]))
             nc.vector.tensor_copy(x_b[o][:], xw[o][:].bitcast(U32).indirect(offs_sb[:, P // 16 : S // 16]))
 
         gather_x(0)
-        nc.vector.quantize_mx(out=w_q[1][:].bitcast(FP8X4), scales=w_s[1][:], in_=w_bf[1][:])
+        quantize_w(1)
         gather_x(1)
 
         ha_ps = psum.tile([P, D, P], F32, name="ha_ps", tag="y0")
@@ -120,32 +127,40 @@ def tile_picked_yrbf_sum_p_kernel(
 
         junk = psum.tile([P, 512], F32, name="junk", tag="y2")
         for rep in range(3):
-            nc.tensor.matmul_mx(out=junk[:], lhsT=x_a[0][:].bitcast(FP8X4), lhsT_scale=xs_g[:, 0:P], rhs=w_q[0][:].bitcast(FP8X4), rhs_scale=w_s[0][:], start=True, stop=True)
+            nc.tensor.matmul_mx(out=junk[:], lhsT=w_q[0][:, 0:P].bitcast(FP8X4), lhsT_scale=w_s[0][:, 0:P], rhs=w_q[0][:].bitcast(FP8X4), rhs_scale=w_s[0][:], start=(rep == 0), stop=(rep == 2))
         h_bf = [keep.tile([P, 256, 4], BF16, name="h_bf%d" % th, align_bytes=64) for th in range(2)]
+        h_ps = [psum.tile([P, 4, P], F32, name="h_ps%d" % tb, tag="h%d" % tb) for tb in range(4)]
+
+        def project(tb, r, o):
+            ch = slice(P * r, P * (r + 1))
+            nc.tensor.matmul_mx(
+                out=h_ps[tb][:, r, :],
+                lhsT=w_q[o][:, ch].bitcast(FP8X4),
+                lhsT_scale=w_s[o][:, ch],
+                rhs=(x_a[o][:] if tb == 0 else x_b[o][:, P * (tb - 1) : P * tb]).bitcast(FP8X4),
+                rhs_scale=xs_g[4 * o : P, P * tb : P * (tb + 1)],
+                start=(o == 0),
+                stop=(o == 1),
+            )
+
         for tb in range(4):
-            cols = slice(P * tb, P * (tb + 1))
-            h_ps = psum.tile([P, 4, P], F32, name="h_ps%d" % tb, tag="h%d" % tb)
-            for r in range(4):
-                ch = slice(P * r, P * (r + 1))
+            project(tb, 0, 0)
+        for tb in range(4):
+            project(tb, 0, 1)
+            for r in range(1, 4):
                 for o in range(2):
-                    nc.tensor.matmul_mx(
-                        out=h_ps[:, r, :],
-                        lhsT=w_q[o][:, ch].bitcast(FP8X4),
-                        lhsT_scale=w_s[o][:, ch],
-                        rhs=(x_a[o][:] if tb == 0 else x_b[o][:, P * (tb - 1) : P * tb]).bitcast(FP8X4),
-                        rhs_scale=xs_g[4 * o : P, cols],
-                        start=(o == 0),
-                        stop=(o == 1),
-                    )
-            nc.scalar.copy(h_bf[tb // 2][:, P * (tb % 2) : P * (tb % 2 + 1), :], h_ps[:].rearrange("p r t -> p t r"))
+                    project(tb, r, o)
+            nc.scalar.copy(h_bf[tb // 2][:, P * (tb % 2) : P * (tb % 2 + 1), :], h_ps[tb][:].rearrange("p r t -> p t r"))
 
         e_g = keep.tile([P, D, P], U32, name="e_g", tag="xw1", align_bytes=64)
         nc.vector.tensor_copy(e_g[:].rearrange("p d v -> p v d"), ew[:].bitcast(U32).indirect(sv_sb[:]))
 
-        h_q = [keep.tile([P, 256], U32, name="h_q0", tag="ew", align_bytes=64), keep.tile([P, 256], U32, name="h_q1", align_bytes=64)]
-        h_s = [keep.tile([P, 256], U8, name="h_s%d" % th, align_bytes=64) for th in range(2)]
+        h_mx = []
         for th in range(2):
-            nc.vector.quantize_mx(out=h_q[th][:].bitcast(FP8X4), scales=h_s[th][:], in_=h_bf[th][:].rearrange("p t r -> p (t r)"))
+            h_q = keep.tile([P, 256], U32, name="h_q%d" % th, tag=("ew", "h_q1")[th], align_bytes=64)
+            h_s = keep.tile([P, 256], U8, name="h_s%d" % th, align_bytes=64)
+            nc.vector.quantize_mx(out=h_q[:].bitcast(FP8X4), scales=h_s[:], in_=h_bf[th][:].rearrange("p t r -> p (t r)"))
+            h_mx.append((h_q, h_s))
 
         for th in range(2):
             tcols = slice(256 * th, 256 * (th + 1))
@@ -154,6 +169,8 @@ def tile_picked_yrbf_sum_p_kernel(
             else:
                 o_ps = [psum.tile([P, P], F32, name="o_ps%d" % s, tag="h%d" % (2 + s)) for s in range(2)]
             ggs = []
+            h_q, h_s = h_mx[th]
+            args = []
             for dp in range(2):
                 u = 2 * th + dp
                 y_ps = psum.tile([P, 2, 256], F32, name="y_ps%d" % u, tag="y%d" % u)
@@ -163,15 +180,19 @@ def tile_picked_yrbf_sum_p_kernel(
                         out=y_ps[:, dd, :],
                         lhsT=e_g[:, d, :].bitcast(FP8X4),
                         lhsT_scale=es_p[:, d, :],
-                        rhs=h_q[th][:].bitcast(FP8X4),
-                        rhs_scale=h_s[th][:],
+                        rhs=h_q[:].bitcast(FP8X4),
+                        rhs_scale=h_s[:],
                         start=True,
                         stop=True,
                     )
-                arg = keep.tile([P, 2, 256], F32, name="arg%d" % u)
+                arg = keep.tile([P, 2, 256], F32, name="arg%d" % u, tag="arg%d" % u, align_bytes=64)
                 nc.vector.scalar_tensor_tensor(
                     arg[:], y_ps[:], 0.5, own_b[:, tcols].unsqueeze(1).to_broadcast([P, 2, 256]), ALU.mult, ALU.add
                 )
+                args.append(arg)
+            for dp in range(2):
+                u = 2 * th + dp
+                arg = args[dp]
                 for dd in range(2):
                     d = 2 * dp + dd
                     ee = keep.tile([P, 256], F32, name="ee%d%d" % (u, dd))

@@ -14,7 +14,16 @@ ALU = mybir.AluOpType
 ACT = mybir.ActivationFunctionType
 
 P = 128
-K, T, S, H, D, W, U = 1024, 1024, 512, 512, 4, 2048, 512
+PACK = 4
+QUADS = 4
+LIST_ROWS = 16
+K, T, S = 1024, 1024, 512
+H, W, U, D = 512, 2048, 512, 4
+PASSES = K // (P * PACK)
+BLOCKS = S // P
+HALF = S // 2
+ALPHA_ROW = 64
+WARM_PASSES = 3
 FLOPS = 2 * K * H * S + 2 * H * S * U
 
 
@@ -26,196 +35,217 @@ def tile_picked_yrbf_sum_p_kernel(
         keep = ctx.enter_context(tc.tile_pool(name="keep", bufs=1))
         psum = ctx.enter_context(tc.psum_pool(name="psum", bufs=1))
 
-        offs_sb = keep.tile([P, S // 16], U16, name="offs_sb")
-        sv_sb = keep.tile([P, U // 16], U16, name="sv_sb")
-        xs = keep.tile([P, T], U8, name="xs", tag="xs", align_bytes=64)
-        es = keep.tile([P, W], U8, name="es", tag="es", align_bytes=64)
-        ha = keep.tile([P, W], F32, name="ha", tag="ha", align_bytes=64)
-        xw = [keep.tile([P, T], I32, name="xw%d" % o, tag="xw%d" % o, align_bytes=64) for o in range(2)]
-        ew = keep.tile([P, W], I32, name="ew", tag="ew", align_bytes=64)
-        raw = [keep.tile([P, 4, H], F32, name="raw%d" % o, tag="raw%d" % o, align_bytes=64) for o in range(2)]
-        own_c = keep.tile([P, 4], F32, name="own_c")
-        ident = keep.tile([P, P], F32, name="ident")
-        warm = keep.tile([P, 1], F32, name="warm")
-        warm2 = keep.tile([P, 1], F32, name="warm2")
+        def sbuf(name, shape, dtype, after=None):
+            return keep.tile(shape, dtype, name=name, tag=after or name, align_bytes=64)
 
-        nc.gpsimd.memset(xs[:].bitcast(I32), 0)
-        nc.vector.memset(warm[:], 0.0)
-        nc.vector.memset(ha[:, 0:1024], 0.0)
-        nc.gpsimd.memset(ha[:, 1024:W], 0.0)
-        nc.vector.memset(es[:].bitcast(I32), 0)
-        nc.scalar.activation(warm2[:], warm[:], ACT.Exp)
+        offs_sb = keep.tile([P, S // LIST_ROWS], U16, name="offs_sb")
+        sv_sb = keep.tile([P, U // LIST_ROWS], U16, name="sv_sb")
+        x_scale_table = sbuf("x_scale_table", [P, T], U8)
+        e_scale_table = sbuf("e_scale_table", [P, W], U8)
+        row_table = sbuf("row_table", [P, W], F32)
+        x_table = [sbuf("x_table%d" % o, [P, T], I32) for o in range(PASSES)]
+        e_table = sbuf("e_table", [P, W], I32)
+        w_raw = [sbuf("w_raw%d" % o, [P, PACK, H], F32) for o in range(PASSES)]
+        own_cols = sbuf("own_cols", [P, BLOCKS], F32)
+        ident = sbuf("ident", [P, P], F32)
+        exp_in = sbuf("exp_in", [P, 1], F32)
+        exp_out = sbuf("exp_out", [P, 1], F32)
 
-        def load_w(o):
-            rows = w1[512 * o : 512 * (o + 1), :]
-            nc.sync.dma_start(raw[o][:], rows.rearrange("(p j) c -> p j c", j=4))
+        nc.gpsimd.memset(x_scale_table[:].bitcast(I32), 0)
+        nc.vector.memset(exp_in[:], 0.0)
+        nc.vector.memset(row_table[:, 0 : W // 2], 0.0)
+        nc.gpsimd.memset(row_table[:, W // 2 : W], 0.0)
+        nc.vector.memset(e_scale_table[:].bitcast(I32), 0)
+        nc.scalar.activation(exp_out[:], exp_in[:], ACT.Exp)
 
         def load_words(tile, words):
-            nc.sync.dma_start(tile[:], words.rearrange("p c r -> p (c r)").bitcast(I32))
+            nc.sync.dma_start(tile[:], words.rearrange("p c j -> p (c j)").bitcast(I32))
 
-        def load_xs(q):
-            nc.sync.dma_start(xs[32 * q : 32 * q + 8, :].bitcast(I32), x_scales[:, 4 * q : 4 * q + 4, :].bitcast(I32))
+        def load_scales(tile, scales):
+            passes = scales.shape[0]
+            for q in range(QUADS):
+                rows = tile[32 * q : 32 * q + 4 * passes, :]
+                nc.sync.dma_start(rows.bitcast(I32), scales[:, 4 * q : 4 * q + 4, :].bitcast(I32))
 
-        def load_es(q):
-            nc.sync.dma_start(es[32 * q : 32 * q + 4, :].bitcast(I32), e_scales[0, 4 * q : 4 * q + 4, :].bitcast(I32))
+        def load_weights(o):
+            rows = w1[P * PACK * o : P * PACK * (o + 1), :]
+            nc.sync.dma_start(w_raw[o][:], rows.rearrange("(p j) c -> p j c", j=PACK))
 
         nc.sync.dma_start(offs_sb[:], offs)
-        for q in range(4):
-            load_xs(q)
+        load_scales(x_scale_table, x_scales)
         nc.sync.dma_start(sv_sb[:], sv)
-        load_w(0)
-        nc.sync.dma_start(ha[0:1, :], half[0:1, :])
-        nc.sync.dma_start(ha[64:65, :], alpha[0:1, :])
-        for q in range(4):
-            load_es(q)
-        load_w(1)
-        load_words(xw[0], x_words[0])
-        load_words(xw[1], x_words[1])
-        load_words(ew, e_words[0])
-        nc.gpsimd.dma_start(own_c[:], own.rearrange("(p s) o -> p (s o)", s=4))
+        load_words(x_table[0], x_words[0])
+        nc.sync.dma_start(row_table[0:1, :], half[0:1, :])
+        nc.sync.dma_start(row_table[ALPHA_ROW : ALPHA_ROW + 1, :], alpha[0:1, :])
+        load_weights(0)
+        load_scales(e_scale_table, e_scales)
+        load_weights(1)
+        load_words(x_table[1], x_words[1])
+        load_words(e_table, e_words[0])
+        nc.gpsimd.dma_start(own_cols[:], own.rearrange("(p s) o -> p (s o)", s=BLOCKS))
         make_identity(nc, ident[:])
 
-        xs_g = keep.tile([P, S], U8, name="xs_g", align_bytes=64)
-        nc.vector.tensor_copy(xs_g[:], xs[:].indirect(offs_sb[:]))
-        ha_g = keep.tile([P, U], F32, name="ha_g", tag="xs", align_bytes=64)
-        nc.vector.tensor_copy(ha_g[:], ha[:].indirect(sv_sb[:]))
+        x_scale = sbuf("x_scale", [P, S], U8)
+        nc.vector.tensor_copy(x_scale[:], x_scale_table[:].indirect(offs_sb[:]))
+        x_first = sbuf("x_first", [P, S], U32)
+        nc.vector.tensor_copy(x_first[:], x_table[0][:].bitcast(U32).indirect(offs_sb[:]))
+        rows_picked = sbuf("rows_picked", [P, U], F32)
+        nc.vector.tensor_copy(rows_picked[:], row_table[:].indirect(sv_sb[:]))
+        e_scale_listed = sbuf("e_scale_listed", [P, U], U8)
+        nc.vector.tensor_copy(e_scale_listed[:], e_scale_table[:].indirect(sv_sb[:]))
+        e_scale = sbuf("e_scale", [P, D, P], U8)
+        nc.vector.tensor_copy(e_scale[:], e_scale_listed[:].rearrange("p (v d) -> p d v", d=D))
 
-        w_bf = [[keep.tile([P, 2 * H], BF16, name="w_bf%d%d" % (o, c), tag="w_bf%d%d" % (o, c), align_bytes=64) for c in range(2)] for o in range(2)]
-        w_q = [keep.tile([P, H], U32, name="w_q%d" % o, tag=("es", "xw0")[o], align_bytes=64) for o in range(2)]
-        w_s = [keep.tile([P, H], U8, name="w_s%d" % o, align_bytes=64) for o in range(2)]
-        for o in range(2):
-            for c in range(2):
-                nc.scalar.copy(
-                    w_bf[o][c][:].rearrange("p (r m j) -> p m j r", r=2, j=4),
-                    raw[o][:].rearrange("p j (m r) -> p m j r", r=4)[:, :, :, 2 * c : 2 * c + 2],
-                )
+        w_codes = [sbuf("w_codes0", [P, H], U32, after="e_scale_table"), sbuf("w_codes1", [P, H], U32)]
+        w_scale = [sbuf("w_scale%d" % o, [P, H], U8) for o in range(PASSES)]
+        w_bf = [[sbuf("w_bf%d%d" % (o, c), [P, 2 * H], BF16) for c in range(2)] for o in range(PASSES)]
 
-        def quantize_w(o):
-            for c in range(2):
-                half_cols = slice(256 * c, 256 * (c + 1))
-                nc.vector.quantize_mx(out=w_q[o][:, half_cols].bitcast(FP8X4), scales=w_s[o][:, half_cols], in_=w_bf[o][c][:])
-
-        es_g = keep.tile([P, U], U8, name="es_g", tag="ha", align_bytes=64)
-        nc.vector.tensor_copy(es_g[:], es[:].indirect(sv_sb[:]))
-        quantize_w(0)
-        es_p = keep.tile([P, D, P], U8, name="es_p", tag="w_bf01", align_bytes=64)
-        nc.vector.tensor_copy(es_p[:], es_g[:].rearrange("p (v d) -> p d v", d=D))
-        x_a = [keep.tile([P, P], U32, name="x_a%d" % o, tag=("ha", "w_bf10")[o], align_bytes=64) for o in range(2)]
-        x_b = [keep.tile([P, S - P], U32, name="x_b%d" % o, tag=("x_b0", "w_bf11")[o], align_bytes=64) for o in range(2)]
-
-        def gather_x(o):
-            nc.vector.tensor_copy(x_a[o][:], xw[o][:].bitcast(U32).indirect(offs_sb[:, 0 : P // 16]))
-            nc.vector.tensor_copy(x_b[o][:], xw[o][:].bitcast(U32).indirect(offs_sb[:, P // 16 : S // 16]))
-
-        gather_x(0)
-        quantize_w(1)
-        gather_x(1)
-
-        ha_ps = psum.tile([P, D, P], F32, name="ha_ps", tag="y0")
-        for d in range(D):
-            nc.tensor.transpose(ha_ps[:, d, :], ha_g[:, d:U:D], ident[:])
-        terms = keep.tile([P, S + 2 * D], F32, name="terms", tag="raw1", align_bytes=64)
-        own_b = terms[:, 0:S]
-        neg_half = terms[:, S : S + D]
-        alpha_c = terms[:, S + D : S + 2 * D]
-        nc.scalar.activation(neg_half, ha_ps[:, :, 0], ACT.Copy, scale=-1.0)
-        nc.scalar.copy(alpha_c, ha_ps[:, :, 64])
-        own_ps = psum.tile([P, 4, P], F32, name="own_ps", tag="y1")
-        for s in range(4):
-            nc.tensor.transpose(own_ps[:, s, :], own_c[:, s : s + 1].to_broadcast([P, P]), ident[:])
-        nc.scalar.copy(own_b.rearrange("m (p s) -> m p s", s=4), own_ps[:].rearrange("m s p -> m p s"))
-
-        junk = psum.tile([P, 512], F32, name="junk", tag="y2")
-        for rep in range(3):
-            nc.tensor.matmul_mx(out=junk[:], lhsT=w_q[0][:, 0:P].bitcast(FP8X4), lhsT_scale=w_s[0][:, 0:P], rhs=w_q[0][:].bitcast(FP8X4), rhs_scale=w_s[0][:], start=(rep == 0), stop=(rep == 2))
-        h_bf = [keep.tile([P, 256, 4], BF16, name="h_bf%d" % th, align_bytes=64) for th in range(2)]
-        h_ps = [psum.tile([P, 4, P], F32, name="h_ps%d" % tb, tag="h%d" % tb) for tb in range(4)]
-
-        def project(tb, r, o):
-            ch = slice(P * r, P * (r + 1))
-            nc.tensor.matmul_mx(
-                out=h_ps[tb][:, r, :],
-                lhsT=w_q[o][:, ch].bitcast(FP8X4),
-                lhsT_scale=w_s[o][:, ch],
-                rhs=(x_a[o][:] if tb == 0 else x_b[o][:, P * (tb - 1) : P * tb]).bitcast(FP8X4),
-                rhs_scale=xs_g[4 * o : P, P * tb : P * (tb + 1)],
-                start=(o == 0),
-                stop=(o == 1),
+        def round_weights(copy, o, c):
+            copy(
+                w_bf[o][c][:].rearrange("p (r m j) -> p m j r", r=2, j=PACK),
+                w_raw[o][:].rearrange("p j (m r) -> p m j r", r=PACK)[:, :, :, 2 * c : 2 * c + 2],
             )
 
-        for tb in range(4):
+        def quantize_weights(o, c):
+            cols = slice(2 * P * c, 2 * P * (c + 1))
+            nc.vector.quantize_mx(out=w_codes[o][:, cols].bitcast(FP8X4), scales=w_scale[o][:, cols], in_=w_bf[o][c][:])
+
+        round_weights(nc.scalar.copy, 0, 0)
+        round_weights(nc.scalar.copy, 0, 1)
+        round_weights(nc.scalar.copy, 1, 0)
+        quantize_weights(0, 0)
+        quantize_weights(0, 1)
+        round_weights(nc.vector.tensor_copy, 1, 1)
+        quantize_weights(1, 1)
+        quantize_weights(1, 0)
+
+        x_second = x_table[1][:].bitcast(U32)
+        x_head = sbuf("x_head", [P, P], U32)
+        nc.vector.tensor_copy(x_head[:], x_second.indirect(offs_sb[:, 0 : P // LIST_ROWS]))
+        x_rest = sbuf("x_rest", [P, S - P], U32, after="w_bf10")
+        nc.vector.tensor_copy(x_rest[:], x_second.indirect(offs_sb[:, P // LIST_ROWS : S // LIST_ROWS]))
+
+        rows_ps = psum.tile([P, D, P], F32, name="rows_ps", tag="y0")
+        for d in range(D):
+            nc.tensor.transpose(rows_ps[:, d, :], rows_picked[:, d:U:D], ident[:])
+        terms = sbuf("terms", [P, HALF + 2 * D], F32, after="w_raw1")
+        own_first = sbuf("own_first", [P, HALF], F32, after="w_bf11")
+        own_rows = [own_first[:], terms[:, 0:HALF]]
+        neg_half = terms[:, HALF : HALF + D]
+        alpha_cols = terms[:, HALF + D : HALF + 2 * D]
+        nc.scalar.activation(neg_half, rows_ps[:, :, 0], ACT.Copy, scale=-1.0)
+        nc.scalar.copy(alpha_cols, rows_ps[:, :, ALPHA_ROW])
+        own_ps = psum.tile([P, BLOCKS, P], F32, name="own_ps", tag="y1")
+        for s in range(BLOCKS):
+            nc.tensor.transpose(own_ps[:, s, :], own_cols[:, s : s + 1].to_broadcast([P, P]), ident[:])
+        for th in range(2):
+            own_part = own_ps[:, :, P // 2 * th : P // 2 * (th + 1)]
+            nc.scalar.copy(own_rows[th].rearrange("m (p s) -> m p s", s=BLOCKS), own_part.rearrange("m s p -> m p s"))
+
+        h_ps = [psum.tile([P, PACK, P], F32, name="h_ps%d" % tb, tag="h%d" % tb) for tb in range(BLOCKS)]
+
+        def project(tb, r, o):
+            samples = slice(P * tb, P * (tb + 1))
+            hidden = slice(P * r, P * (r + 1))
+            if o == 0:
+                x_codes = x_first[:, samples]
+            elif tb == 0:
+                x_codes = x_head[:]
+            else:
+                x_codes = x_rest[:, P * (tb - 1) : P * tb]
+            nc.tensor.matmul_mx(
+                out=h_ps[tb][:, r, :],
+                lhsT=w_codes[o][:, hidden].bitcast(FP8X4),
+                lhsT_scale=w_scale[o][:, hidden],
+                rhs=x_codes.bitcast(FP8X4),
+                rhs_scale=x_scale[4 * o : P, samples],
+                start=(o == 0),
+                stop=(o == PASSES - 1),
+            )
+
+        for tb in range(BLOCKS):
             project(tb, 0, 0)
-        for tb in range(4):
+        warm_ps = psum.tile([P, H], F32, name="warm_ps", tag="y2")
+        for n in range(WARM_PASSES):
+            nc.tensor.matmul_mx(
+                out=warm_ps[:],
+                lhsT=w_codes[0][:, 0:P].bitcast(FP8X4),
+                lhsT_scale=w_scale[0][:, 0:P],
+                rhs=w_codes[0][:].bitcast(FP8X4),
+                rhs_scale=w_scale[0][:],
+                start=(n == 0),
+                stop=(n == WARM_PASSES - 1),
+            )
+        h_bf = [sbuf("h_bf%d" % th, [P, HALF, PACK], BF16) for th in range(2)]
+        for tb in range(BLOCKS):
             project(tb, 0, 1)
-            for r in range(1, 4):
-                for o in range(2):
+            for r in range(1, PACK):
+                for o in range(PASSES):
                     project(tb, r, o)
             nc.scalar.copy(h_bf[tb // 2][:, P * (tb % 2) : P * (tb % 2 + 1), :], h_ps[tb][:].rearrange("p r t -> p t r"))
 
-        e_g = keep.tile([P, D, P], U32, name="e_g", tag="xw1", align_bytes=64)
-        nc.vector.tensor_copy(e_g[:].rearrange("p d v -> p v d"), ew[:].bitcast(U32).indirect(sv_sb[:]))
+        e_codes = sbuf("e_codes", [P, D, P], U32)
+        nc.vector.tensor_copy(e_codes[:].rearrange("p d v -> p v d"), e_table[:].bitcast(U32).indirect(sv_sb[:]))
 
-        h_mx = []
-        for th in range(2):
-            h_q = keep.tile([P, 256], U32, name="h_q%d" % th, tag=("ew", "h_q1")[th], align_bytes=64)
-            h_s = keep.tile([P, 256], U8, name="h_s%d" % th, align_bytes=64)
-            nc.vector.quantize_mx(out=h_q[:].bitcast(FP8X4), scales=h_s[:], in_=h_bf[th][:].rearrange("p t r -> p (t r)"))
-            h_mx.append((h_q, h_s))
+        def quantize_hidden(th, after):
+            codes = sbuf("h_codes%d" % th, [P, HALF], U32, after=after)
+            scale = sbuf("h_scale%d" % th, [P, HALF], U8)
+            nc.vector.quantize_mx(out=codes[:].bitcast(FP8X4), scales=scale[:], in_=h_bf[th][:].rearrange("p t r -> p (t r)"))
+            return codes, scale
 
-        for th in range(2):
-            tcols = slice(256 * th, 256 * (th + 1))
-            if th == 0:
-                o_both = psum.tile([P, 2, P], F32, name="o_both", tag="h0")
-            else:
-                o_ps = [psum.tile([P, P], F32, name="o_ps%d" % s, tag="h%d" % (2 + s)) for s in range(2)]
-            ggs = []
-            h_q, h_s = h_mx[th]
-            args = []
-            for dp in range(2):
-                u = 2 * th + dp
-                y_ps = psum.tile([P, 2, 256], F32, name="y_ps%d" % u, tag="y%d" % u)
-                for dd in range(2):
-                    d = 2 * dp + dd
-                    nc.tensor.matmul_mx(
-                        out=y_ps[:, dd, :],
-                        lhsT=e_g[:, d, :].bitcast(FP8X4),
-                        lhsT_scale=es_p[:, d, :],
-                        rhs=h_q[:].bitcast(FP8X4),
-                        rhs_scale=h_s[:],
-                        start=True,
-                        stop=True,
-                    )
-                arg = keep.tile([P, 2, 256], F32, name="arg%d" % u, tag="arg%d" % u, align_bytes=64)
-                nc.vector.scalar_tensor_tensor(
-                    arg[:], y_ps[:], 0.5, own_b[:, tcols].unsqueeze(1).to_broadcast([P, 2, 256]), ALU.mult, ALU.add
+        def exponents(th, pair, h_codes, h_scale):
+            unit = 2 * th + pair
+            y_ps = psum.tile([P, 2, HALF], F32, name="y_ps%d" % unit, tag="y%d" % unit)
+            for dd in range(2):
+                nc.tensor.matmul_mx(
+                    out=y_ps[:, dd, :],
+                    lhsT=e_codes[:, 2 * pair + dd, :].bitcast(FP8X4),
+                    lhsT_scale=e_scale[:, 2 * pair + dd, :],
+                    rhs=h_codes[:].bitcast(FP8X4),
+                    rhs_scale=h_scale[:],
+                    start=True,
+                    stop=True,
                 )
-                args.append(arg)
-            for dp in range(2):
-                u = 2 * th + dp
-                arg = args[dp]
-                for dd in range(2):
-                    d = 2 * dp + dd
-                    ee = keep.tile([P, 256], F32, name="ee%d%d" % (u, dd))
-                    nc.scalar.activation(ee[:], arg[:, dd, :], ACT.Exp, bias=neg_half[:, d : d + 1])
-                    gg = keep.tile([P, 256], F32, name="gg%d%d" % (u, dd))
-                    if th == 0:
-                        nc.vector.tensor_scalar(gg[:], ee[:], alpha_c[:, d : d + 1], None, ALU.mult)
-                        ggs.append(gg)
-                    else:
-                        nc.vector.tensor_scalar(gg[:], ee[:], alpha_c[:, d : d + 1], None, ALU.mult)
-                        for s in range(2):
-                            nc.tensor.matmul(
-                                o_ps[s][:], gg[:, P * s : P * (s + 1)], ident[:], start=(d == 0), stop=(d == D - 1), is_transpose=True
-                            )
-            res = keep.tile([P, 2, P], F32, name="res%d" % th)
-            if th == 0:
-                for s in range(2):
-                    for d in range(D):
-                        nc.tensor.matmul(
-                            o_both[:, s, :], ggs[d][:, P * s : P * (s + 1)], ident[:], start=(d == 0), stop=(d == D - 1), is_transpose=True
-                        )
-                nc.scalar.copy(res[:], o_both[:])
-            else:
-                nc.scalar.copy(res[:, 0, :], o_ps[0][:])
-                nc.vector.tensor_copy(res[:, 1, :], o_ps[1][:])
-            nc.sync.dma_start(out[tcols, :].rearrange("(s p) v -> p s v", s=2), res[:])
+            arg = sbuf("arg%d" % unit, [P, 2, HALF], F32)
+            own_twice = own_rows[th].unsqueeze(1).to_broadcast([P, 2, HALF])
+            nc.vector.scalar_tensor_tensor(arg[:], y_ps[:], 0.5, own_twice, ALU.mult, ALU.add)
+            return arg
+
+        def weighted(th, d, arg):
+            value = sbuf("value%d%d" % (th, d), [P, HALF], F32)
+            nc.scalar.activation(value[:], arg[:, d % 2, :], ACT.Exp, bias=neg_half[:, d : d + 1])
+            term = sbuf("term%d%d" % (th, d), [P, HALF], F32)
+            nc.vector.tensor_scalar(term[:], value[:], alpha_cols[:, d : d + 1], None, ALU.mult)
+            return term
+
+        def add_transposed(acc, term, s, d):
+            nc.tensor.matmul(
+                acc, term[:, P * s : P * (s + 1)], ident[:], start=(d == 0), stop=(d == D - 1), is_transpose=True
+            )
+
+        def store(th, result):
+            nc.sync.dma_start(out[HALF * th : HALF * (th + 1), :].rearrange("(s p) v -> p s v", s=2), result[:])
+
+        args = []
+        for th, after in enumerate(("e_table", "w_bf11")):
+            h_codes, h_scale = quantize_hidden(th, after)
+            args.append([exponents(th, pair, h_codes, h_scale) for pair in range(2)])
+
+        first_terms = [weighted(0, d, args[0][d // 2]) for d in range(D)]
+        first_ps = psum.tile([P, 2, P], F32, name="first_ps", tag="h0")
+        for s in range(2):
+            for d in range(D):
+                add_transposed(first_ps[:, s, :], first_terms[d], s, d)
+        first_out = sbuf("first_out", [P, 2, P], F32)
+        nc.scalar.copy(first_out[:], first_ps[:])
+        store(0, first_out)
+
+        last_ps = [psum.tile([P, P], F32, name="last_ps%d" % s, tag="h%d" % (2 + s)) for s in range(2)]
+        for d in range(D):
+            term = weighted(1, d, args[1][d // 2])
+            for s in range(2):
+                add_transposed(last_ps[s][:], term, s, d)
+        last_out = sbuf("last_out", [P, 2, P], F32)
+        nc.scalar.copy(last_out[:, 0, :], last_ps[0][:])
+        nc.vector.tensor_copy(last_out[:, 1, :], last_ps[1][:])
+        store(1, last_out)

@@ -23,6 +23,7 @@ PASSES = K // (P * PACK)
 BLOCKS = S // P
 HALF = S // 2
 ALPHA_ROW = 64
+POOL_TERMS = 3
 WARM_PASSES = 3
 FLOPS = 2 * K * H * S + 2 * H * S * U
 
@@ -48,22 +49,17 @@ def tile_picked_yrbf_sum_p_kernel(
         w_raw = [sbuf("w_raw%d" % o, [P, PACK, H], F32) for o in range(PASSES)]
         own_cols = sbuf("own_cols", [P, BLOCKS], F32)
         ident = sbuf("ident", [P, P], F32)
-        exp_in = sbuf("exp_in", [P, 1], F32)
-        exp_out = sbuf("exp_out", [P, 1], F32)
 
-        nc.gpsimd.memset(x_scale_table[:].bitcast(I32), 0)
-        nc.vector.memset(exp_in[:], 0.0)
-        nc.vector.memset(row_table[:, 0 : W // 2], 0.0)
-        nc.gpsimd.memset(row_table[:, W // 2 : W], 0.0)
         nc.vector.memset(e_scale_table[:].bitcast(I32), 0)
-        nc.scalar.activation(exp_out[:], exp_in[:], ACT.Exp)
+        nc.vector.memset(x_scale_table[:].bitcast(I32), 0)
+        nc.vector.memset(row_table[:], 0.0)
 
         def load_words(tile, words):
             nc.sync.dma_start(tile[:], words.rearrange("p c j -> p (c j)").bitcast(I32))
 
-        def load_scales(tile, scales):
+        def load_scales(tile, scales, quads):
             passes = scales.shape[0]
-            for q in range(QUADS):
+            for q in quads:
                 rows = tile[32 * q : 32 * q + 4 * passes, :]
                 nc.sync.dma_start(rows.bitcast(I32), scales[:, 4 * q : 4 * q + 4, :].bitcast(I32))
 
@@ -71,100 +67,97 @@ def tile_picked_yrbf_sum_p_kernel(
             rows = w1[P * PACK * o : P * PACK * (o + 1), :]
             nc.sync.dma_start(w_raw[o][:], rows.rearrange("(p j) c -> p j c", j=PACK))
 
-        nc.sync.dma_start(offs_sb[:], offs)
-        load_scales(x_scale_table, x_scales)
         nc.sync.dma_start(sv_sb[:], sv)
-        load_words(x_table[0], x_words[0])
+        nc.sync.dma_start(offs_sb[:], offs)
+        load_scales(e_scale_table, e_scales, range(QUADS))
+        load_weights(0)
+        load_scales(x_scale_table, x_scales, range(QUADS))
         nc.sync.dma_start(row_table[0:1, :], half[0:1, :])
         nc.sync.dma_start(row_table[ALPHA_ROW : ALPHA_ROW + 1, :], alpha[0:1, :])
-        load_weights(0)
-        load_scales(e_scale_table, e_scales)
         load_weights(1)
+        load_words(x_table[0], x_words[0])
         load_words(x_table[1], x_words[1])
         load_words(e_table, e_words[0])
-        nc.gpsimd.dma_start(own_cols[:], own.rearrange("(p s) o -> p (s o)", s=BLOCKS))
         make_identity(nc, ident[:])
+        nc.gpsimd.dma_start(own_cols[:], own.rearrange("(p s) o -> p (s o)", s=BLOCKS))
 
-        x_scale = sbuf("x_scale", [P, S], U8)
-        nc.vector.tensor_copy(x_scale[:], x_scale_table[:].indirect(offs_sb[:]))
-        x_first = sbuf("x_first", [P, S], U32)
-        nc.vector.tensor_copy(x_first[:], x_table[0][:].bitcast(U32).indirect(offs_sb[:]))
-        rows_picked = sbuf("rows_picked", [P, U], F32)
-        nc.vector.tensor_copy(rows_picked[:], row_table[:].indirect(sv_sb[:]))
         e_scale_listed = sbuf("e_scale_listed", [P, U], U8)
         nc.vector.tensor_copy(e_scale_listed[:], e_scale_table[:].indirect(sv_sb[:]))
         e_scale = sbuf("e_scale", [P, D, P], U8)
         nc.vector.tensor_copy(e_scale[:], e_scale_listed[:].rearrange("p (v d) -> p d v", d=D))
+        x_scale = sbuf("x_scale", [P, S], U8)
+        nc.vector.tensor_copy(x_scale[:], x_scale_table[:].indirect(offs_sb[:]))
+        rows_picked = sbuf("rows_picked", [P, U], F32)
+        nc.vector.tensor_copy(rows_picked[:], row_table[:].indirect(sv_sb[:]))
 
-        w_codes = [sbuf("w_codes0", [P, H], U32, after="e_scale_table"), sbuf("w_codes1", [P, H], U32)]
+        w_codes = [sbuf("w_codes0", [P, H], U32, after="row_table"), sbuf("w_codes1", [P, H], U32)]
         w_scale = [sbuf("w_scale%d" % o, [P, H], U8) for o in range(PASSES)]
-        w_bf = [[sbuf("w_bf%d%d" % (o, c), [P, 2 * H], BF16) for c in range(2)] for o in range(PASSES)]
+        w_bf_first = sbuf("w_bf_first", [P, 2, 2 * H], BF16)
+        w_bf_second = [sbuf("w_bf1%d" % c, [P, 2 * H], BF16) for c in range(2)]
+        w_bf = [[w_bf_first[:, c, :] for c in range(2)], [w_bf_second[c][:] for c in range(2)]]
 
-        def round_weights(copy, o, c):
-            copy(
-                w_bf[o][c][:].rearrange("p (r m j) -> p m j r", r=2, j=PACK),
+        def round_weights(o, c):
+            nc.scalar.activation(
+                w_bf[o][c].rearrange("p (r m j) -> p m j r", r=2, j=PACK),
                 w_raw[o][:].rearrange("p j (m r) -> p m j r", r=PACK)[:, :, :, 2 * c : 2 * c + 2],
+                ACT.Copy,
             )
 
-        def quantize_weights(o, c):
+        for o in range(PASSES):
+            for c in range(2):
+                round_weights(o, c)
+        nc.vector.quantize_mx(
+            out=w_codes[0][:].bitcast(FP8X4), scales=w_scale[0][:], in_=w_bf_first[:].rearrange("p c n -> p (c n)")
+        )
+
+        def quantize_second(c):
             cols = slice(2 * P * c, 2 * P * (c + 1))
-            nc.vector.quantize_mx(out=w_codes[o][:, cols].bitcast(FP8X4), scales=w_scale[o][:, cols], in_=w_bf[o][c][:])
+            nc.vector.quantize_mx(out=w_codes[1][:, cols].bitcast(FP8X4), scales=w_scale[1][:, cols], in_=w_bf[1][c])
 
-        round_weights(nc.scalar.copy, 0, 0)
-        round_weights(nc.scalar.copy, 0, 1)
-        round_weights(nc.scalar.copy, 1, 0)
-        quantize_weights(0, 0)
-        quantize_weights(0, 1)
-        round_weights(nc.vector.tensor_copy, 1, 1)
-        quantize_weights(1, 1)
-        quantize_weights(1, 0)
+        def gather_x(o, first, last, after=None):
+            codes = sbuf("x_codes%d%d" % (o, first), [P, P * (last - first)], U32, after=after)
+            entries = offs_sb[:, first * P // LIST_ROWS : last * P // LIST_ROWS]
+            nc.vector.tensor_copy(codes[:], x_table[o][:].bitcast(U32).indirect(entries))
+            for tb in range(first, last):
+                x_codes[o, tb] = codes[:, P * (tb - first) : P * (tb - first + 1)]
 
-        x_second = x_table[1][:].bitcast(U32)
-        x_head = sbuf("x_head", [P, P], U32)
-        nc.vector.tensor_copy(x_head[:], x_second.indirect(offs_sb[:, 0 : P // LIST_ROWS]))
-        x_rest = sbuf("x_rest", [P, S - P], U32, after="w_bf10")
-        nc.vector.tensor_copy(x_rest[:], x_second.indirect(offs_sb[:, P // LIST_ROWS : S // LIST_ROWS]))
+        x_codes = {}
+        gather_x(0, 0, 2)
+        quantize_second(0)
+        gather_x(1, 0, 1)
+        quantize_second(1)
+        gather_x(1, 1, BLOCKS)
+        gather_x(0, 2, BLOCKS, after="w_bf11")
 
         rows_ps = psum.tile([P, D, P], F32, name="rows_ps", tag="y0")
         for d in range(D):
             nc.tensor.transpose(rows_ps[:, d, :], rows_picked[:, d:U:D], ident[:])
-        terms = sbuf("terms", [P, HALF + 2 * D], F32, after="w_raw1")
-        own_first = sbuf("own_first", [P, HALF], F32, after="w_bf11")
-        own_rows = [own_first[:], terms[:, 0:HALF]]
-        neg_half = terms[:, HALF : HALF + D]
-        alpha_cols = terms[:, HALF + D : HALF + 2 * D]
+        terms = sbuf("terms", [P, S + 2 * D], F32, after="w_raw1")
+        own_rows = [terms[:, HALF * th : HALF * (th + 1)] for th in range(2)]
+        neg_half = terms[:, S : S + D]
+        alpha_cols = terms[:, S + D : S + 2 * D]
         nc.scalar.activation(neg_half, rows_ps[:, :, 0], ACT.Copy, scale=-1.0)
         nc.scalar.copy(alpha_cols, rows_ps[:, :, ALPHA_ROW])
         own_ps = psum.tile([P, BLOCKS, P], F32, name="own_ps", tag="y1")
         for s in range(BLOCKS):
             nc.tensor.transpose(own_ps[:, s, :], own_cols[:, s : s + 1].to_broadcast([P, P]), ident[:])
-        for th in range(2):
-            own_part = own_ps[:, :, P // 2 * th : P // 2 * (th + 1)]
-            nc.scalar.copy(own_rows[th].rearrange("m (p s) -> m p s", s=BLOCKS), own_part.rearrange("m s p -> m p s"))
+        nc.scalar.copy(terms[:, 0:S].rearrange("m (p s) -> m p s", s=BLOCKS), own_ps[:].rearrange("m s p -> m p s"))
 
         h_ps = [psum.tile([P, PACK, P], F32, name="h_ps%d" % tb, tag="h%d" % tb) for tb in range(BLOCKS)]
 
         def project(tb, r, o):
             samples = slice(P * tb, P * (tb + 1))
             hidden = slice(P * r, P * (r + 1))
-            if o == 0:
-                x_codes = x_first[:, samples]
-            elif tb == 0:
-                x_codes = x_head[:]
-            else:
-                x_codes = x_rest[:, P * (tb - 1) : P * tb]
             nc.tensor.matmul_mx(
                 out=h_ps[tb][:, r, :],
                 lhsT=w_codes[o][:, hidden].bitcast(FP8X4),
                 lhsT_scale=w_scale[o][:, hidden],
-                rhs=x_codes.bitcast(FP8X4),
+                rhs=x_codes[o, tb].bitcast(FP8X4),
                 rhs_scale=x_scale[4 * o : P, samples],
                 start=(o == 0),
                 stop=(o == PASSES - 1),
             )
 
-        for tb in range(BLOCKS):
-            project(tb, 0, 0)
         warm_ps = psum.tile([P, H], F32, name="warm_ps", tag="y2")
         for n in range(WARM_PASSES):
             nc.tensor.matmul_mx(
@@ -177,23 +170,29 @@ def tile_picked_yrbf_sum_p_kernel(
                 stop=(n == WARM_PASSES - 1),
             )
         h_bf = [sbuf("h_bf%d" % th, [P, HALF, PACK], BF16) for th in range(2)]
-        for tb in range(BLOCKS):
-            project(tb, 0, 1)
-            for r in range(1, PACK):
-                for o in range(PASSES):
-                    project(tb, r, o)
+
+        def copy_hidden(tb):
             nc.scalar.copy(h_bf[tb // 2][:, P * (tb % 2) : P * (tb % 2 + 1), :], h_ps[tb][:].rearrange("p r t -> p t r"))
+
+        for tb in range(2):
+            project(tb, 0, 0)
+        for tb in range(BLOCKS):
+            for r in range(PACK):
+                for o in range(PASSES):
+                    if tb >= 2 or (r, o) != (0, 0):
+                        project(tb, r, o)
+            copy_hidden(tb)
 
         e_codes = sbuf("e_codes", [P, D, P], U32)
         nc.vector.tensor_copy(e_codes[:].rearrange("p d v -> p v d"), e_table[:].bitcast(U32).indirect(sv_sb[:]))
 
-        def quantize_hidden(th, after):
-            codes = sbuf("h_codes%d" % th, [P, HALF], U32, after=after)
+        def quantize_hidden(th):
+            codes = sbuf("h_codes%d" % th, [P, HALF], U32, after="e_table")[:]
             scale = sbuf("h_scale%d" % th, [P, HALF], U8)
-            nc.vector.quantize_mx(out=codes[:].bitcast(FP8X4), scales=scale[:], in_=h_bf[th][:].rearrange("p t r -> p (t r)"))
+            nc.vector.quantize_mx(out=codes.bitcast(FP8X4), scales=scale[:], in_=h_bf[th][:].rearrange("p t r -> p (t r)"))
             return codes, scale
 
-        def exponents(th, pair, h_codes, h_scale):
+        def products(th, pair, h_codes, h_scale):
             unit = 2 * th + pair
             y_ps = psum.tile([P, 2, HALF], F32, name="y_ps%d" % unit, tag="y%d" % unit)
             for dd in range(2):
@@ -201,21 +200,30 @@ def tile_picked_yrbf_sum_p_kernel(
                     out=y_ps[:, dd, :],
                     lhsT=e_codes[:, 2 * pair + dd, :].bitcast(FP8X4),
                     lhsT_scale=e_scale[:, 2 * pair + dd, :],
-                    rhs=h_codes[:].bitcast(FP8X4),
+                    rhs=h_codes.bitcast(FP8X4),
                     rhs_scale=h_scale[:],
                     start=True,
                     stop=True,
                 )
-            arg = sbuf("arg%d" % unit, [P, 2, HALF], F32)
+            return y_ps
+
+        def add_own(th, pair, y_ps):
+            arg = sbuf("arg%d%d" % (th, pair), [P, 2, HALF], F32)
             own_twice = own_rows[th].unsqueeze(1).to_broadcast([P, 2, HALF])
             nc.vector.scalar_tensor_tensor(arg[:], y_ps[:], 0.5, own_twice, ALU.mult, ALU.add)
             return arg
+
+        def exponents(th, pair, h_codes, h_scale):
+            return add_own(th, pair, products(th, pair, h_codes, h_scale))
 
         def weighted(th, d, arg):
             value = sbuf("value%d%d" % (th, d), [P, HALF], F32)
             nc.scalar.activation(value[:], arg[:, d % 2, :], ACT.Exp, bias=neg_half[:, d : d + 1])
             term = sbuf("term%d%d" % (th, d), [P, HALF], F32)
-            nc.vector.tensor_scalar(term[:], value[:], alpha_cols[:, d : d + 1], None, ALU.mult)
+            if th == 0 and d < POOL_TERMS:
+                nc.gpsimd.tensor_scalar(term[:], value[:], alpha_cols[:, d : d + 1], 0.0, ALU.mult, ALU.add)
+            else:
+                nc.vector.tensor_scalar(term[:], value[:], alpha_cols[:, d : d + 1], None, ALU.mult)
             return term
 
         def add_transposed(acc, term, s, d):
@@ -226,26 +234,21 @@ def tile_picked_yrbf_sum_p_kernel(
         def store(th, result):
             nc.sync.dma_start(out[HALF * th : HALF * (th + 1), :].rearrange("(s p) v -> p s v", s=2), result[:])
 
-        args = []
-        for th, after in enumerate(("e_table", "w_bf11")):
-            h_codes, h_scale = quantize_hidden(th, after)
-            args.append([exponents(th, pair, h_codes, h_scale) for pair in range(2)])
+        first = quantize_hidden(0)
+        args = [[exponents(0, 0, *first)], []]
+        first_rest = products(0, 1, *first)
+        second = quantize_hidden(1)
+        args[0].append(add_own(0, 1, first_rest))
+        args[1] = [exponents(1, pair, *second) for pair in range(2)]
 
-        first_terms = [weighted(0, d, args[0][d // 2]) for d in range(D)]
-        first_ps = psum.tile([P, 2, P], F32, name="first_ps", tag="h0")
-        for s in range(2):
+        sums = [psum.tile([P, P], F32, name="sum%d" % tb, tag="h%d" % tb) for tb in range(BLOCKS)]
+        for th in range(2):
             for d in range(D):
-                add_transposed(first_ps[:, s, :], first_terms[d], s, d)
-        first_out = sbuf("first_out", [P, 2, P], F32)
-        nc.scalar.copy(first_out[:], first_ps[:])
-        store(0, first_out)
-
-        last_ps = [psum.tile([P, P], F32, name="last_ps%d" % s, tag="h%d" % (2 + s)) for s in range(2)]
-        for d in range(D):
-            term = weighted(1, d, args[1][d // 2])
-            for s in range(2):
-                add_transposed(last_ps[s][:], term, s, d)
-        last_out = sbuf("last_out", [P, 2, P], F32)
-        nc.scalar.copy(last_out[:, 0, :], last_ps[0][:])
-        nc.vector.tensor_copy(last_out[:, 1, :], last_ps[1][:])
-        store(1, last_out)
+                term = weighted(th, d, args[th][d // 2])
+                for s in range(2):
+                    add_transposed(sums[2 * th + s][:], term, s, d)
+        for th in range(2):
+            result = sbuf("result%d" % th, [P, 2, P], F32)
+            nc.scalar.copy(result[:, 0, :], sums[2 * th][:])
+            nc.vector.tensor_copy(result[:, 1, :], sums[2 * th + 1][:])
+            store(th, result)

@@ -22,7 +22,8 @@ H, W, U, D = 512, 2048, 512, 4
 PASSES = K // (P * PACK)
 BLOCKS = S // P
 HALF = S // 2
-ALPHA_ROW = 64
+HALF_ROW, ALPHA_ROW = 16, 80
+E_PLANE = 8
 POOL_TERMS = 3
 WARM_PASSES = 3
 FLOPS = 2 * K * H * S + 2 * H * S * U
@@ -51,17 +52,17 @@ def tile_picked_yrbf_sum_p_kernel(
         ident = sbuf("ident", [P, P], F32)
 
         nc.vector.memset(e_scale_table[:].bitcast(I32), 0)
-        nc.vector.memset(x_scale_table[:].bitcast(I32), 0)
         nc.vector.memset(row_table[:], 0.0)
+        nc.vector.memset(x_scale_table[:].bitcast(I32), 0)
 
         def load_words(tile, words):
             nc.sync.dma_start(tile[:], words.rearrange("p c j -> p (c j)").bitcast(I32))
 
-        def load_scales(tile, scales, quads):
+        def load_scales(tile, scales, first, queues):
             passes = scales.shape[0]
-            for q in quads:
-                rows = tile[32 * q : 32 * q + 4 * passes, :]
-                nc.sync.dma_start(rows.bitcast(I32), scales[:, 4 * q : 4 * q + 4, :].bitcast(I32))
+            for q, queue in enumerate(queues):
+                rows = tile[32 * q + first : 32 * q + first + 4 * passes, :]
+                queue.dma_start(rows.bitcast(I32), scales[:, 4 * q : 4 * q + 4, :].bitcast(I32))
 
         def load_weights(o):
             rows = w1[P * PACK * o : P * PACK * (o + 1), :]
@@ -69,11 +70,11 @@ def tile_picked_yrbf_sum_p_kernel(
 
         nc.sync.dma_start(sv_sb[:], sv)
         nc.sync.dma_start(offs_sb[:], offs)
-        load_scales(e_scale_table, e_scales, range(QUADS))
+        load_scales(e_scale_table, e_scales, E_PLANE, (nc.sync, nc.scalar, nc.sync, nc.scalar))
         load_weights(0)
-        load_scales(x_scale_table, x_scales, range(QUADS))
-        nc.sync.dma_start(row_table[0:1, :], half[0:1, :])
+        nc.sync.dma_start(row_table[HALF_ROW : HALF_ROW + 1, :], half[0:1, :])
         nc.sync.dma_start(row_table[ALPHA_ROW : ALPHA_ROW + 1, :], alpha[0:1, :])
+        load_scales(x_scale_table, x_scales, 0, (nc.sync,) * QUADS)
         load_weights(1)
         load_words(x_table[0], x_words[0])
         load_words(x_table[1], x_words[1])
@@ -85,12 +86,12 @@ def tile_picked_yrbf_sum_p_kernel(
         nc.vector.tensor_copy(e_scale_listed[:], e_scale_table[:].indirect(sv_sb[:]))
         e_scale = sbuf("e_scale", [P, D, P], U8)
         nc.vector.tensor_copy(e_scale[:], e_scale_listed[:].rearrange("p (v d) -> p d v", d=D))
-        x_scale = sbuf("x_scale", [P, S], U8)
-        nc.vector.tensor_copy(x_scale[:], x_scale_table[:].indirect(offs_sb[:]))
         rows_picked = sbuf("rows_picked", [P, U], F32)
         nc.vector.tensor_copy(rows_picked[:], row_table[:].indirect(sv_sb[:]))
+        x_scale = sbuf("x_scale", [P, S], U8)
+        nc.vector.tensor_copy(x_scale[:], x_scale_table[:].indirect(offs_sb[:]))
 
-        w_codes = [sbuf("w_codes0", [P, H], U32, after="row_table"), sbuf("w_codes1", [P, H], U32)]
+        w_codes = [sbuf("w_codes0", [P, H], U32, after="x_scale_table"), sbuf("w_codes1", [P, H], U32)]
         w_scale = [sbuf("w_scale%d" % o, [P, H], U8) for o in range(PASSES)]
         w_bf_first = sbuf("w_bf_first", [P, 2, 2 * H], BF16)
         w_bf_second = [sbuf("w_bf1%d" % c, [P, 2 * H], BF16) for c in range(2)]
@@ -122,12 +123,12 @@ def tile_picked_yrbf_sum_p_kernel(
                 x_codes[o, tb] = codes[:, P * (tb - first) : P * (tb - first + 1)]
 
         x_codes = {}
-        gather_x(0, 0, 2)
+        gather_x(0, 0, BLOCKS - 1)
         quantize_second(0)
         gather_x(1, 0, 1)
         quantize_second(1)
         gather_x(1, 1, BLOCKS)
-        gather_x(0, 2, BLOCKS, after="w_bf11")
+        gather_x(0, BLOCKS - 1, BLOCKS, after="w_bf11")
 
         rows_ps = psum.tile([P, D, P], F32, name="rows_ps", tag="y0")
         for d in range(D):
@@ -136,7 +137,7 @@ def tile_picked_yrbf_sum_p_kernel(
         own_rows = [terms[:, HALF * th : HALF * (th + 1)] for th in range(2)]
         neg_half = terms[:, S : S + D]
         alpha_cols = terms[:, S + D : S + 2 * D]
-        nc.scalar.activation(neg_half, rows_ps[:, :, 0], ACT.Copy, scale=-1.0)
+        nc.scalar.activation(neg_half, rows_ps[:, :, HALF_ROW], ACT.Copy, scale=-1.0)
         nc.scalar.copy(alpha_cols, rows_ps[:, :, ALPHA_ROW])
         own_ps = psum.tile([P, BLOCKS, P], F32, name="own_ps", tag="y1")
         for s in range(BLOCKS):
@@ -174,12 +175,12 @@ def tile_picked_yrbf_sum_p_kernel(
         def copy_hidden(tb):
             nc.scalar.copy(h_bf[tb // 2][:, P * (tb % 2) : P * (tb % 2 + 1), :], h_ps[tb][:].rearrange("p r t -> p t r"))
 
-        for tb in range(2):
+        for tb in range(BLOCKS - 1):
             project(tb, 0, 0)
         for tb in range(BLOCKS):
             for r in range(PACK):
                 for o in range(PASSES):
-                    if tb >= 2 or (r, o) != (0, 0):
+                    if tb == BLOCKS - 1 or (r, o) != (0, 0):
                         project(tb, r, o)
             copy_hidden(tb)
 
@@ -199,7 +200,7 @@ def tile_picked_yrbf_sum_p_kernel(
                 nc.tensor.matmul_mx(
                     out=y_ps[:, dd, :],
                     lhsT=e_codes[:, 2 * pair + dd, :].bitcast(FP8X4),
-                    lhsT_scale=e_scale[:, 2 * pair + dd, :],
+                    lhsT_scale=e_scale[E_PLANE:P, 2 * pair + dd, :],
                     rhs=h_codes.bitcast(FP8X4),
                     rhs_scale=h_scale[:],
                     start=True,

@@ -24,7 +24,7 @@ BLOCKS = S // P
 HALF = S // 2
 HALF_ROW, ALPHA_ROW = 16, 80
 E_PLANE = 8
-POOL_TERMS = 3
+POOL_TERMS = 2
 WARM_PASSES = 3
 FLOPS = 2 * K * H * S + 2 * H * S * U
 
@@ -58,11 +58,11 @@ def tile_picked_yrbf_sum_p_kernel(
         def load_words(tile, words):
             nc.sync.dma_start(tile[:], words.rearrange("p c j -> p (c j)").bitcast(I32))
 
-        def load_scales(tile, scales, first, queues):
+        def load_scales(tile, scales, first):
             passes = scales.shape[0]
-            for q, queue in enumerate(queues):
+            for q in range(QUADS):
                 rows = tile[32 * q + first : 32 * q + first + 4 * passes, :]
-                queue.dma_start(rows.bitcast(I32), scales[:, 4 * q : 4 * q + 4, :].bitcast(I32))
+                nc.sync.dma_start(rows.bitcast(I32), scales[:, 4 * q : 4 * q + 4, :].bitcast(I32))
 
         def load_weights(o):
             rows = w1[P * PACK * o : P * PACK * (o + 1), :]
@@ -70,11 +70,11 @@ def tile_picked_yrbf_sum_p_kernel(
 
         nc.sync.dma_start(sv_sb[:], sv)
         nc.sync.dma_start(offs_sb[:], offs)
-        load_scales(e_scale_table, e_scales, E_PLANE, (nc.sync, nc.scalar, nc.sync, nc.scalar))
+        load_scales(e_scale_table, e_scales, E_PLANE)
         load_weights(0)
         nc.sync.dma_start(row_table[HALF_ROW : HALF_ROW + 1, :], half[0:1, :])
         nc.sync.dma_start(row_table[ALPHA_ROW : ALPHA_ROW + 1, :], alpha[0:1, :])
-        load_scales(x_scale_table, x_scales, 0, (nc.sync,) * QUADS)
+        load_scales(x_scale_table, x_scales, 0)
         load_weights(1)
         load_words(x_table[0], x_words[0])
         load_words(x_table[1], x_words[1])
@@ -187,18 +187,24 @@ def tile_picked_yrbf_sum_p_kernel(
         e_codes = sbuf("e_codes", [P, D, P], U32)
         nc.vector.tensor_copy(e_codes[:].rearrange("p d v -> p v d"), e_table[:].bitcast(U32).indirect(sv_sb[:]))
 
-        def quantize_hidden(th):
-            codes = sbuf("h_codes%d" % th, [P, HALF], U32, after="e_table")[:]
-            scale = sbuf("h_scale%d" % th, [P, HALF], U8)
-            nc.vector.quantize_mx(out=codes.bitcast(FP8X4), scales=scale[:], in_=h_bf[th][:].rearrange("p t r -> p (t r)"))
+        h_words = sbuf("h_words", [P, S], U32, after="e_table")
+
+        def quantize_hidden(first, last, after=None):
+            codes = h_words[:, P * first : P * last]
+            scale = sbuf("h_scale%d" % first, [P, P * (last - first)], U8, after=after)
+            values = h_bf[first // 2][:, P * (first % 2) : P * (first % 2 + last - first), :]
+            nc.vector.quantize_mx(out=codes.bitcast(FP8X4), scales=scale[:], in_=values.rearrange("p t r -> p (t r)"))
             return codes, scale
 
-        def products(th, pair, h_codes, h_scale):
+        y_ps = {}
+
+        def products(th, pair, cols, h_codes, h_scale):
             unit = 2 * th + pair
-            y_ps = psum.tile([P, 2, HALF], F32, name="y_ps%d" % unit, tag="y%d" % unit)
+            if unit not in y_ps:
+                y_ps[unit] = psum.tile([P, 2, HALF], F32, name="y_ps%d" % unit, tag="y%d" % unit)
             for dd in range(2):
                 nc.tensor.matmul_mx(
-                    out=y_ps[:, dd, :],
+                    out=y_ps[unit][:, dd, cols],
                     lhsT=e_codes[:, 2 * pair + dd, :].bitcast(FP8X4),
                     lhsT_scale=e_scale[E_PLANE:P, 2 * pair + dd, :],
                     rhs=h_codes.bitcast(FP8X4),
@@ -206,48 +212,54 @@ def tile_picked_yrbf_sum_p_kernel(
                     start=True,
                     stop=True,
                 )
-            return y_ps
 
-        def add_own(th, pair, y_ps):
+        def add_own(th, pair):
             arg = sbuf("arg%d%d" % (th, pair), [P, 2, HALF], F32)
             own_twice = own_rows[th].unsqueeze(1).to_broadcast([P, 2, HALF])
-            nc.vector.scalar_tensor_tensor(arg[:], y_ps[:], 0.5, own_twice, ALU.mult, ALU.add)
+            nc.vector.scalar_tensor_tensor(arg[:], y_ps[2 * th + pair][:], 0.5, own_twice, ALU.mult, ALU.add)
             return arg
 
-        def exponents(th, pair, h_codes, h_scale):
-            return add_own(th, pair, products(th, pair, h_codes, h_scale))
-
-        def weighted(th, d, arg):
-            value = sbuf("value%d%d" % (th, d), [P, HALF], F32)
-            nc.scalar.activation(value[:], arg[:, d % 2, :], ACT.Exp, bias=neg_half[:, d : d + 1])
-            term = sbuf("term%d%d" % (th, d), [P, HALF], F32)
+        def weighted(th, d, arg, cols):
+            name = "%d%d%d" % (th, d, cols.start)
+            value = sbuf("value" + name, [P, cols.stop - cols.start], F32)
+            nc.scalar.activation(value[:], arg[:, d % 2, cols], ACT.Exp, bias=neg_half[:, d : d + 1])
+            term = sbuf("term" + name, [P, cols.stop - cols.start], F32)
             if th == 0 and d < POOL_TERMS:
                 nc.gpsimd.tensor_scalar(term[:], value[:], alpha_cols[:, d : d + 1], 0.0, ALU.mult, ALU.add)
             else:
                 nc.vector.tensor_scalar(term[:], value[:], alpha_cols[:, d : d + 1], None, ALU.mult)
             return term
 
-        def add_transposed(acc, term, s, d):
-            nc.tensor.matmul(
-                acc, term[:, P * s : P * (s + 1)], ident[:], start=(d == 0), stop=(d == D - 1), is_transpose=True
-            )
+        def add_transposed(acc, term, d):
+            nc.tensor.matmul(acc, term, ident[:], start=(d == 0), stop=(d == D - 1), is_transpose=True)
 
         def store(th, result):
             nc.sync.dma_start(out[HALF * th : HALF * (th + 1), :].rearrange("(s p) v -> p s v", s=2), result[:])
 
-        first = quantize_hidden(0)
-        args = [[exponents(0, 0, *first)], []]
-        first_rest = products(0, 1, *first)
-        second = quantize_hidden(1)
-        args[0].append(add_own(0, 1, first_rest))
-        args[1] = [exponents(1, pair, *second) for pair in range(2)]
+        first = quantize_hidden(0, 2)
+        third = quantize_hidden(2, 3)
+        for pair in range(2):
+            products(0, pair, slice(0, HALF), *first)
+        for pair in range(2):
+            products(1, pair, slice(0, P), *third)
+        args = [[add_own(0, 0)], []]
+        last = quantize_hidden(3, 4, after="h_scale0")
+        for pair in range(2):
+            products(1, pair, slice(P, HALF), *last)
+        args[0].append(add_own(0, 1))
+        args[1] = [add_own(1, pair) for pair in range(2)]
 
         sums = [psum.tile([P, P], F32, name="sum%d" % tb, tag="h%d" % tb) for tb in range(BLOCKS)]
         for th in range(2):
             for d in range(D):
-                term = weighted(th, d, args[th][d // 2])
-                for s in range(2):
-                    add_transposed(sums[2 * th + s][:], term, s, d)
+                if (th, d) == (1, D - 1):
+                    for s in range(2):
+                        term = weighted(th, d, args[th][d // 2], slice(P * s, P * (s + 1)))
+                        add_transposed(sums[2 * th + s][:], term[:], d)
+                else:
+                    term = weighted(th, d, args[th][d // 2], slice(0, HALF))
+                    for s in range(2):
+                        add_transposed(sums[2 * th + s][:], term[:, P * s : P * (s + 1)], d)
         for th in range(2):
             result = sbuf("result%d" % th, [P, 2, P], F32)
             nc.scalar.copy(result[:, 0, :], sums[2 * th][:])

@@ -24,6 +24,8 @@ BLOCKS = S // P
 HALF = S // 2
 HALF_ROW, ALPHA_ROW = 16, 80
 E_PLANE = 8
+ROW_SPLIT = 1536
+W_HEAD = 768
 POOL_TERMS = 2
 WARM_PASSES = 3
 FLOPS = 2 * K * H * S + 2 * H * S * U
@@ -50,9 +52,12 @@ def tile_picked_yrbf_sum_p_kernel(
         w_raw = [sbuf("w_raw%d" % o, [P, PACK, H], F32) for o in range(PASSES)]
         own_cols = sbuf("own_cols", [P, BLOCKS], F32)
         ident = sbuf("ident", [P, P], F32)
+        zero = sbuf("zero", [P, 1], F32)
 
         nc.vector.memset(e_scale_table[:].bitcast(I32), 0)
-        nc.vector.memset(row_table[:], 0.0)
+        nc.vector.memset(zero[:], 0.0)
+        nc.vector.memset(row_table[:, 0:ROW_SPLIT], 0.0)
+        nc.scalar.activation(row_table[:, ROW_SPLIT:W], zero[:].to_broadcast([P, W - ROW_SPLIT]), ACT.Copy)
         nc.vector.memset(x_scale_table[:].bitcast(I32), 0)
 
         def load_words(tile, words):
@@ -64,18 +69,19 @@ def tile_picked_yrbf_sum_p_kernel(
                 rows = tile[32 * q + first : 32 * q + first + 4 * passes, :]
                 nc.sync.dma_start(rows.bitcast(I32), scales[:, 4 * q : 4 * q + 4, :].bitcast(I32))
 
-        def load_weights(o):
-            rows = w1[P * PACK * o : P * PACK * (o + 1), :]
-            nc.sync.dma_start(w_raw[o][:], rows.rearrange("(p j) c -> p j c", j=PACK))
+        def load_weights(o, cols):
+            rows = w1[P * PACK * o : P * PACK * (o + 1), :].rearrange("(p j) c -> p (j c)", j=PACK)
+            nc.sync.dma_start(w_raw[o][:].rearrange("p j c -> p (j c)")[:, cols], rows[:, cols])
 
         nc.sync.dma_start(sv_sb[:], sv)
         nc.sync.dma_start(offs_sb[:], offs)
+        load_weights(0, slice(0, W_HEAD))
         load_scales(e_scale_table, e_scales, E_PLANE)
-        load_weights(0)
+        load_weights(0, slice(W_HEAD, PACK * H))
         nc.sync.dma_start(row_table[HALF_ROW : HALF_ROW + 1, :], half[0:1, :])
         nc.sync.dma_start(row_table[ALPHA_ROW : ALPHA_ROW + 1, :], alpha[0:1, :])
         load_scales(x_scale_table, x_scales, 0)
-        load_weights(1)
+        load_weights(1, slice(0, PACK * H))
         load_words(x_table[0], x_words[0])
         load_words(x_table[1], x_words[1])
         load_words(e_table, e_words[0])

@@ -73,9 +73,9 @@ def tile_picked_yrbf_sum_p_kernel(
             rows = w1[P * PACK * o : P * PACK * (o + 1), :].rearrange("(p j) c -> p (j c)", j=PACK)
             nc.sync.dma_start(w_raw[o][:].rearrange("p j c -> p (j c)")[:, cols], rows[:, cols])
 
+        load_weights(0, slice(0, W_HEAD))
         nc.sync.dma_start(sv_sb[:], sv)
         nc.sync.dma_start(offs_sb[:], offs)
-        load_weights(0, slice(0, W_HEAD))
         load_scales(e_scale_table, e_scales, E_PLANE)
         load_weights(0, slice(W_HEAD, PACK * H))
         nc.sync.dma_start(row_table[HALF_ROW : HALF_ROW + 1, :], half[0:1, :])
@@ -239,9 +239,6 @@ def tile_picked_yrbf_sum_p_kernel(
         def add_transposed(acc, term, d):
             nc.tensor.matmul(acc, term, ident[:], start=(d == 0), stop=(d == D - 1), is_transpose=True)
 
-        def store(th, result):
-            nc.sync.dma_start(out[HALF * th : HALF * (th + 1), :].rearrange("(s p) v -> p s v", s=2), result[:])
-
         first = quantize_hidden(0, 2)
         third = quantize_hidden(2, 3)
         for pair in range(2):
@@ -266,8 +263,11 @@ def tile_picked_yrbf_sum_p_kernel(
                     term = weighted(th, d, args[th][d // 2], slice(0, HALF))
                     for s in range(2):
                         add_transposed(sums[2 * th + s][:], term[:, P * s : P * (s + 1)], d)
-        for th in range(2):
-            result = sbuf("result%d" % th, [P, 2, P], F32)
-            nc.scalar.copy(result[:, 0, :], sums[2 * th][:])
-            nc.vector.tensor_copy(result[:, 1, :], sums[2 * th + 1][:])
-            store(th, result)
+        first_out = sbuf("first_out", [P, 2, P], F32)
+        nc.scalar.copy(first_out[:, 0, :], sums[0][:])
+        nc.vector.tensor_copy(first_out[:, 1, :], sums[1][:])
+        nc.sync.dma_start(out[0:HALF, :].rearrange("(s p) v -> p s v", s=2), first_out[:])
+        for tb, copy in ((2, nc.scalar.copy), (3, nc.vector.tensor_copy)):
+            block_out = sbuf("block_out%d" % tb, [P, P], F32)
+            copy(block_out[:], sums[tb][:])
+            nc.sync.dma_start(out[P * tb : P * (tb + 1), :], block_out[:])

@@ -23,11 +23,10 @@ PASSES = K // (P * PACK)
 BLOCKS = S // P
 HALF = S // 2
 HALF_ROW, ALPHA_ROW = 16, 80
-E_PLANE = 8
+E_FIRST = 8
 ROW_SPLIT = 1536
 W_HEAD = 768
 POOL_TERMS = 2
-WARM_PASSES = 3
 FLOPS = 2 * K * H * S + 2 * H * S * U
 
 
@@ -76,7 +75,7 @@ def tile_picked_yrbf_sum_p_kernel(
         load_weights(0, slice(0, W_HEAD))
         nc.sync.dma_start(sv_sb[:], sv)
         nc.sync.dma_start(offs_sb[:], offs)
-        load_scales(e_scale_table, e_scales, E_PLANE)
+        load_scales(e_scale_table, e_scales, E_FIRST)
         load_weights(0, slice(W_HEAD, PACK * H))
         nc.sync.dma_start(row_table[HALF_ROW : HALF_ROW + 1, :], half[0:1, :])
         nc.sync.dma_start(row_table[ALPHA_ROW : ALPHA_ROW + 1, :], alpha[0:1, :])
@@ -121,6 +120,8 @@ def tile_picked_yrbf_sum_p_kernel(
             cols = slice(2 * P * c, 2 * P * (c + 1))
             nc.vector.quantize_mx(out=w_codes[1][:, cols].bitcast(FP8X4), scales=w_scale[1][:, cols], in_=w_bf[1][c])
 
+        x_codes = {}
+
         def gather_x(o, first, last, after=None):
             codes = sbuf("x_codes%d%d" % (o, first), [P, P * (last - first)], U32, after=after)
             entries = offs_sb[:, first * P // LIST_ROWS : last * P // LIST_ROWS]
@@ -128,7 +129,6 @@ def tile_picked_yrbf_sum_p_kernel(
             for tb in range(first, last):
                 x_codes[o, tb] = codes[:, P * (tb - first) : P * (tb - first + 1)]
 
-        x_codes = {}
         gather_x(0, 0, BLOCKS - 1)
         quantize_second(0)
         gather_x(1, 0, 1)
@@ -165,17 +165,6 @@ def tile_picked_yrbf_sum_p_kernel(
                 stop=(o == PASSES - 1),
             )
 
-        warm_ps = psum.tile([P, H], F32, name="warm_ps", tag="y2")
-        for n in range(WARM_PASSES):
-            nc.tensor.matmul_mx(
-                out=warm_ps[:],
-                lhsT=w_codes[0][:, 0:P].bitcast(FP8X4),
-                lhsT_scale=w_scale[0][:, 0:P],
-                rhs=w_codes[0][:].bitcast(FP8X4),
-                rhs_scale=w_scale[0][:],
-                start=(n == 0),
-                stop=(n == WARM_PASSES - 1),
-            )
         h_bf = [sbuf("h_bf%d" % th, [P, HALF, PACK], BF16) for th in range(2)]
 
         def copy_hidden(tb):
@@ -205,14 +194,14 @@ def tile_picked_yrbf_sum_p_kernel(
         y_ps = {}
 
         def products(th, pair, cols, h_codes, h_scale):
-            unit = 2 * th + pair
-            if unit not in y_ps:
-                y_ps[unit] = psum.tile([P, 2, HALF], F32, name="y_ps%d" % unit, tag="y%d" % unit)
+            bank = 2 * th + pair
+            if bank not in y_ps:
+                y_ps[bank] = psum.tile([P, 2, HALF], F32, name="y_ps%d" % bank, tag="y%d" % bank)
             for dd in range(2):
                 nc.tensor.matmul_mx(
-                    out=y_ps[unit][:, dd, cols],
+                    out=y_ps[bank][:, dd, cols],
                     lhsT=e_codes[:, 2 * pair + dd, :].bitcast(FP8X4),
-                    lhsT_scale=e_scale[E_PLANE:P, 2 * pair + dd, :],
+                    lhsT_scale=e_scale[E_FIRST:P, 2 * pair + dd, :],
                     rhs=h_codes.bitcast(FP8X4),
                     rhs_scale=h_scale[:],
                     start=True,
@@ -239,16 +228,16 @@ def tile_picked_yrbf_sum_p_kernel(
         def add_transposed(acc, term, d):
             nc.tensor.matmul(acc, term, ident[:], start=(d == 0), stop=(d == D - 1), is_transpose=True)
 
-        first = quantize_hidden(0, 2)
-        third = quantize_hidden(2, 3)
+        first_half = quantize_hidden(0, 2)
+        third_block = quantize_hidden(2, 3)
         for pair in range(2):
-            products(0, pair, slice(0, HALF), *first)
+            products(0, pair, slice(0, HALF), *first_half)
         for pair in range(2):
-            products(1, pair, slice(0, P), *third)
+            products(1, pair, slice(0, P), *third_block)
         args = [[add_own(0, 0)], []]
-        last = quantize_hidden(3, 4, after="h_scale0")
+        last_block = quantize_hidden(3, 4, after="h_scale0")
         for pair in range(2):
-            products(1, pair, slice(P, HALF), *last)
+            products(1, pair, slice(P, HALF), *last_block)
         args[0].append(add_own(0, 1))
         args[1] = [add_own(1, pair) for pair in range(2)]
 

@@ -22,11 +22,10 @@ H, W, U, D = 512, 2048, 512, 4
 PASSES = K // (P * PACK)
 BLOCKS = S // P
 HALF = S // 2
+POOL_TERMS = 3
 HALF_ROW, ALPHA_ROW = 16, 80
 E_FIRST = 8
 ROW_SPLIT = 1536
-W_HEAD = 768
-POOL_TERMS = 2
 FLOPS = 2 * K * H * S + 2 * H * S * U
 
 
@@ -37,8 +36,11 @@ def tile_picked_yrbf_sum_p_kernel(
     with ExitStack() as ctx:
         keep = ctx.enter_context(tc.tile_pool(name="keep", bufs=1))
         psum = ctx.enter_context(tc.psum_pool(name="psum", bufs=1))
+        shared = ctx.enter_context(tc.tile_pool(name="shared", bufs=1))
 
-        def sbuf(name, shape, dtype, after=None):
+        def sbuf(name, shape, dtype, after=None, at=None):
+            if at is not None:
+                return shared.tile(shape, dtype, name=name, offset=at, align_bytes=64)
             return keep.tile(shape, dtype, name=name, tag=after or name, align_bytes=64)
 
         offs_sb = keep.tile([P, S // LIST_ROWS], U16, name="offs_sb")
@@ -48,16 +50,16 @@ def tile_picked_yrbf_sum_p_kernel(
         row_table = sbuf("row_table", [P, W], F32)
         x_table = [sbuf("x_table%d" % o, [P, T], I32) for o in range(PASSES)]
         e_table = sbuf("e_table", [P, W], I32)
-        w_raw = [sbuf("w_raw%d" % o, [P, PACK, H], F32) for o in range(PASSES)]
+        w_raw = [sbuf("w_raw0", [P, PACK, H], F32), sbuf("w_raw1", [P, PACK, H], F32, at=0)]
         own_cols = sbuf("own_cols", [P, BLOCKS], F32)
         ident = sbuf("ident", [P, P], F32)
         zero = sbuf("zero", [P, 1], F32)
 
-        nc.vector.memset(e_scale_table[:].bitcast(I32), 0)
+        nc.vector.memset(x_scale_table[:].bitcast(I32), 0)
         nc.vector.memset(zero[:], 0.0)
+        nc.vector.memset(e_scale_table[:].bitcast(I32), 0)
         nc.vector.memset(row_table[:, 0:ROW_SPLIT], 0.0)
         nc.scalar.activation(row_table[:, ROW_SPLIT:W], zero[:].to_broadcast([P, W - ROW_SPLIT]), ACT.Copy)
-        nc.vector.memset(x_scale_table[:].bitcast(I32), 0)
 
         def load_words(tile, words):
             nc.sync.dma_start(tile[:], words.rearrange("p c j -> p (c j)").bitcast(I32))
@@ -68,89 +70,85 @@ def tile_picked_yrbf_sum_p_kernel(
                 rows = tile[32 * q + first : 32 * q + first + 4 * passes, :]
                 nc.sync.dma_start(rows.bitcast(I32), scales[:, 4 * q : 4 * q + 4, :].bitcast(I32))
 
-        def load_weights(o, cols):
+        def load_weights(o):
             rows = w1[P * PACK * o : P * PACK * (o + 1), :].rearrange("(p j) c -> p (j c)", j=PACK)
-            nc.sync.dma_start(w_raw[o][:].rearrange("p j c -> p (j c)")[:, cols], rows[:, cols])
+            nc.sync.dma_start(w_raw[o][:].rearrange("p j c -> p (j c)"), rows)
 
-        load_weights(0, slice(0, W_HEAD))
-        nc.sync.dma_start(sv_sb[:], sv)
+        load_words(x_table[0], x_words[0])
         nc.sync.dma_start(offs_sb[:], offs)
-        load_scales(e_scale_table, e_scales, E_FIRST)
-        load_weights(0, slice(W_HEAD, PACK * H))
+        nc.sync.dma_start(sv_sb[:], sv)
+        load_scales(x_scale_table, x_scales, 0)
+        load_weights(0)
         nc.sync.dma_start(row_table[HALF_ROW : HALF_ROW + 1, :], half[0:1, :])
         nc.sync.dma_start(row_table[ALPHA_ROW : ALPHA_ROW + 1, :], alpha[0:1, :])
-        load_scales(x_scale_table, x_scales, 0)
-        load_weights(1, slice(0, PACK * H))
-        load_words(x_table[0], x_words[0])
+        load_scales(e_scale_table, e_scales, E_FIRST)
+        load_weights(1)
         load_words(x_table[1], x_words[1])
         load_words(e_table, e_words[0])
         make_identity(nc, ident[:])
         nc.gpsimd.dma_start(own_cols[:], own.rearrange("(p s) o -> p (s o)", s=BLOCKS))
 
-        e_scale_listed = sbuf("e_scale_listed", [P, U], U8)
-        nc.vector.tensor_copy(e_scale_listed[:], e_scale_table[:].indirect(sv_sb[:]))
-        e_scale = sbuf("e_scale", [P, D, P], U8)
-        nc.vector.tensor_copy(e_scale[:], e_scale_listed[:].rearrange("p (v d) -> p d v", d=D))
-        rows_picked = sbuf("rows_picked", [P, U], F32)
-        nc.vector.tensor_copy(rows_picked[:], row_table[:].indirect(sv_sb[:]))
         x_scale = sbuf("x_scale", [P, S], U8)
         nc.vector.tensor_copy(x_scale[:], x_scale_table[:].indirect(offs_sb[:]))
-
-        w_codes = [sbuf("w_codes0", [P, H], U32, after="x_scale_table"), sbuf("w_codes1", [P, H], U32)]
-        w_scale = [sbuf("w_scale%d" % o, [P, H], U8) for o in range(PASSES)]
-        w_bf_first = sbuf("w_bf_first", [P, 2, 2 * H], BF16)
-        w_bf_second = [sbuf("w_bf1%d" % c, [P, 2 * H], BF16) for c in range(2)]
-        w_bf = [[w_bf_first[:, c, :] for c in range(2)], [w_bf_second[c][:] for c in range(2)]]
-
-        def round_weights(o, c):
-            nc.scalar.activation(
-                w_bf[o][c].rearrange("p (r m j) -> p m j r", r=2, j=PACK),
-                w_raw[o][:].rearrange("p j (m r) -> p m j r", r=PACK)[:, :, :, 2 * c : 2 * c + 2],
-                ACT.Copy,
-            )
-
-        for o in range(PASSES):
-            for c in range(2):
-                round_weights(o, c)
-        nc.vector.quantize_mx(
-            out=w_codes[0][:].bitcast(FP8X4), scales=w_scale[0][:], in_=w_bf_first[:].rearrange("p c n -> p (c n)")
-        )
-
-        def quantize_second(c):
-            cols = slice(2 * P * c, 2 * P * (c + 1))
-            nc.vector.quantize_mx(out=w_codes[1][:, cols].bitcast(FP8X4), scales=w_scale[1][:, cols], in_=w_bf[1][c])
-
         x_codes = {}
 
-        def gather_x(o, first, last, after=None):
-            codes = sbuf("x_codes%d%d" % (o, first), [P, P * (last - first)], U32, after=after)
+        def gather_x(o, first, last, at=None):
+            codes = sbuf("x_codes%d%d" % (o, first), [P, P * (last - first)], U32, at=at)
             entries = offs_sb[:, first * P // LIST_ROWS : last * P // LIST_ROWS]
             nc.vector.tensor_copy(codes[:], x_table[o][:].bitcast(U32).indirect(entries))
             for tb in range(first, last):
                 x_codes[o, tb] = codes[:, P * (tb - first) : P * (tb - first + 1)]
 
-        gather_x(0, 0, BLOCKS - 1)
-        quantize_second(0)
-        gather_x(1, 0, 1)
-        quantize_second(1)
-        gather_x(1, 1, BLOCKS)
-        gather_x(0, BLOCKS - 1, BLOCKS, after="w_bf11")
+        gather_x(0, 0, BLOCKS)
 
-        rows_ps = psum.tile([P, D, P], F32, name="rows_ps", tag="y0")
-        for d in range(D):
-            nc.tensor.transpose(rows_ps[:, d, :], rows_picked[:, d:U:D], ident[:])
-        terms = sbuf("terms", [P, S + 2 * D], F32, after="w_raw1")
-        own_rows = [terms[:, HALF * th : HALF * (th + 1)] for th in range(2)]
-        neg_half = terms[:, S : S + D]
-        alpha_cols = terms[:, S + D : S + 2 * D]
-        nc.scalar.activation(neg_half, rows_ps[:, :, HALF_ROW], ACT.Copy, scale=-1.0)
-        nc.scalar.copy(alpha_cols, rows_ps[:, :, ALPHA_ROW])
-        own_ps = psum.tile([P, BLOCKS, P], F32, name="own_ps", tag="y1")
+        w_codes = [sbuf("w_codes0", [P, H], U32, after="e_scale_table"), sbuf("w_codes1", [P, H], U32)]
+        w_scale = [sbuf("w_scale%d" % o, [P, H], U8) for o in range(PASSES)]
+        w_bf = [sbuf("w_bf%d" % o, [P, 2, 2 * H], BF16) for o in range(PASSES)]
+
+        def round_weights(o):
+            def views(c):
+                return (
+                    w_bf[o][:, c, :].rearrange("p (r m j) -> p m j r", r=2, j=PACK),
+                    w_raw[o][:].rearrange("p j (m r) -> p m j r", r=PACK)[:, :, :, 2 * c : 2 * c + 2],
+                )
+
+            nc.scalar.activation(*views(0), ACT.Copy)
+            nc.vector.tensor_copy(*views(1))
+
+        round_weights(0)
+        e_scale = sbuf("e_scale", [P, D, P], U8)
+        nc.vector.tensor_copy(e_scale[:].rearrange("p d v -> p v d"), e_scale_table[:].indirect(sv_sb[:]))
+        rows_picked = sbuf("rows_picked", [P, U], F32)
+        nc.scalar.activation(rows_picked[:], row_table[:].indirect(sv_sb[:]), ACT.Copy)
+        half_cols = sbuf("half_cols", [P, D], F32)
+        alpha_cols = sbuf("alpha_cols", [P, D], F32)
+        for cols, row in ((half_cols, HALF_ROW), (alpha_cols, ALPHA_ROW)):
+            nc.sync.dma_start(cols[:], rows_picked[row : row + 1, :].rearrange("o (v d) -> o v d", d=D))
+        neg_half = sbuf("neg_half", [P, D], F32)
+        nc.gpsimd.tensor_scalar(neg_half[:], half_cols[:], -1.0, 0.0, ALU.mult, ALU.add)
+        nc.vector.quantize_mx(
+            out=w_codes[0][:].bitcast(FP8X4), scales=w_scale[0][:], in_=w_bf[0][:].rearrange("p c n -> p (c n)")
+        )
+
+        def quantize_second(c):
+            cols = slice(2 * P * c, 2 * P * (c + 1))
+            nc.vector.quantize_mx(out=w_codes[1][:, cols].bitcast(FP8X4), scales=w_scale[1][:, cols], in_=w_bf[1][:, c, :])
+
+        round_weights(1)
+        quantize_second(1)
+        gather_x(1, 0, 1)
+        quantize_second(0)
+        own_rows = sbuf("own_rows", [P, S], F32, at=0)
+        gather_x(1, 1, 2, at=4 * S)
+        gather_x(1, 2, BLOCKS, at=8 * S)
+
+        own_ps = psum.tile([P, BLOCKS, P], F32, name="own_ps", tag="h3")
         for s in range(BLOCKS):
             nc.tensor.transpose(own_ps[:, s, :], own_cols[:, s : s + 1].to_broadcast([P, P]), ident[:])
-        nc.scalar.copy(terms[:, 0:S].rearrange("m (p s) -> m p s", s=BLOCKS), own_ps[:].rearrange("m s p -> m p s"))
+        nc.scalar.copy(own_rows[:].rearrange("m (p s) -> m p s", s=BLOCKS), own_ps[:].rearrange("m s p -> m p s"))
 
         h_ps = [psum.tile([P, PACK, P], F32, name="h_ps%d" % tb, tag="h%d" % tb) for tb in range(BLOCKS)]
+        second_order = (2, 3, 0, 1)
 
         def project(tb, r, o):
             samples = slice(P * tb, P * (tb + 1))
@@ -161,100 +159,94 @@ def tile_picked_yrbf_sum_p_kernel(
                 lhsT_scale=w_scale[o][:, hidden],
                 rhs=x_codes[o, tb].bitcast(FP8X4),
                 rhs_scale=x_scale[4 * o : P, samples],
-                start=(o == 0),
-                stop=(o == PASSES - 1),
+                start=(o, r) == (0, 0),
+                stop=(o, r) == (1, second_order[-1]),
             )
 
         h_bf = [sbuf("h_bf%d" % th, [P, HALF, PACK], BF16) for th in range(2)]
 
-        def copy_hidden(tb):
+        def second_pass(tb):
+            for r in second_order:
+                project(tb, r, 1)
             nc.scalar.copy(h_bf[tb // 2][:, P * (tb % 2) : P * (tb % 2 + 1), :], h_ps[tb][:].rearrange("p r t -> p t r"))
 
-        for tb in range(BLOCKS - 1):
-            project(tb, 0, 0)
         for tb in range(BLOCKS):
+            if tb == BLOCKS - 1:
+                second_pass(0)
             for r in range(PACK):
-                for o in range(PASSES):
-                    if tb == BLOCKS - 1 or (r, o) != (0, 0):
-                        project(tb, r, o)
-            copy_hidden(tb)
+                project(tb, r, 0)
+        for tb in range(1, BLOCKS):
+            second_pass(tb)
 
         e_codes = sbuf("e_codes", [P, D, P], U32)
         nc.vector.tensor_copy(e_codes[:].rearrange("p d v -> p v d"), e_table[:].bitcast(U32).indirect(sv_sb[:]))
 
-        h_words = sbuf("h_words", [P, S], U32, after="e_table")
+        y_ps = [psum.tile([P, 2, HALF], F32, name="y_ps%d" % bank, tag="y%d" % bank) for bank in range(D)]
 
-        def quantize_hidden(first, last, after=None):
-            codes = h_words[:, P * first : P * last]
-            scale = sbuf("h_scale%d" % first, [P, P * (last - first)], U8, after=after)
-            values = h_bf[first // 2][:, P * (first % 2) : P * (first % 2 + last - first), :]
-            nc.vector.quantize_mx(out=codes.bitcast(FP8X4), scales=scale[:], in_=values.rearrange("p t r -> p (t r)"))
-            return codes, scale
-
-        y_ps = {}
-
-        def products(th, pair, cols, h_codes, h_scale):
-            bank = 2 * th + pair
-            if bank not in y_ps:
-                y_ps[bank] = psum.tile([P, 2, HALF], F32, name="y_ps%d" % bank, tag="y%d" % bank)
-            for dd in range(2):
+        def products(th):
+            codes = sbuf("h_codes%d" % th, [P, HALF], U32, after="rows_picked" if th == 0 else None)
+            scale = sbuf("h_scale%d" % th, [P, HALF], U8, after="h_scale0")
+            nc.vector.quantize_mx(
+                out=codes[:].bitcast(FP8X4), scales=scale[:], in_=h_bf[th][:].rearrange("p t r -> p (t r)")
+            )
+            for d in range(D):
                 nc.tensor.matmul_mx(
-                    out=y_ps[bank][:, dd, cols],
-                    lhsT=e_codes[:, 2 * pair + dd, :].bitcast(FP8X4),
-                    lhsT_scale=e_scale[E_FIRST:P, 2 * pair + dd, :],
-                    rhs=h_codes.bitcast(FP8X4),
-                    rhs_scale=h_scale[:],
+                    out=y_ps[2 * th + d // 2][:, d % 2, :],
+                    lhsT=e_codes[:, d, :].bitcast(FP8X4),
+                    lhsT_scale=e_scale[E_FIRST:P, d, :],
+                    rhs=codes[:].bitcast(FP8X4),
+                    rhs_scale=scale[:],
                     start=True,
                     stop=True,
                 )
 
-        def add_own(th, pair):
-            arg = sbuf("arg%d%d" % (th, pair), [P, 2, HALF], F32)
-            own_twice = own_rows[th].unsqueeze(1).to_broadcast([P, 2, HALF])
-            nc.vector.scalar_tensor_tensor(arg[:], y_ps[2 * th + pair][:], 0.5, own_twice, ALU.mult, ALU.add)
-            return arg
+        args = {}
 
-        def weighted(th, d, arg, cols):
-            name = "%d%d%d" % (th, d, cols.start)
-            value = sbuf("value" + name, [P, cols.stop - cols.start], F32)
-            nc.scalar.activation(value[:], arg[:, d % 2, cols], ACT.Exp, bias=neg_half[:, d : d + 1])
-            term = sbuf("term" + name, [P, cols.stop - cols.start], F32)
-            if th == 0 and d < POOL_TERMS:
+        def add_own(th, first, last):
+            count = last - first
+            arg = sbuf("arg%d%d" % (th, first), [P, count, HALF], F32)
+            own_view = own_rows[:, HALF * th : HALF * (th + 1)].unsqueeze(1).to_broadcast([P, count, HALF])
+            y = y_ps[2 * th + first // 2][:, first % 2 : first % 2 + count, :]
+            nc.vector.scalar_tensor_tensor(arg[:], y, 0.5, own_view, ALU.mult, ALU.add)
+            for d in range(first, last):
+                args[th, d] = arg[:, d - first, :]
+
+        products(0)
+        add_own(0, 0, 1)
+        products(1)
+        add_own(0, 1, 2)
+        add_own(0, 2, 4)
+        add_own(1, 0, 2)
+        add_own(1, 2, 3)
+        add_own(1, 3, 4)
+
+        sums = [psum.tile([P, P], F32, name="sum%d" % tb, tag="h%d" % tb) for tb in range(BLOCKS)]
+
+        def weighted(d, first, last):
+            name = "%d%d" % (d, first)
+            th = first // 2
+            arg = args[th, d][:, P * (first % 2) : P * (first % 2 + last - first)]
+            value = sbuf("value" + name, [P, P * (last - first)], F32)
+            nc.scalar.activation(value[:], arg, ACT.Exp, bias=neg_half[:, d : d + 1])
+            term = sbuf("term" + name, [P, P * (last - first)], F32)
+            if D * th + d < POOL_TERMS:
                 nc.gpsimd.tensor_scalar(term[:], value[:], alpha_cols[:, d : d + 1], 0.0, ALU.mult, ALU.add)
             else:
                 nc.vector.tensor_scalar(term[:], value[:], alpha_cols[:, d : d + 1], None, ALU.mult)
-            return term
+            for tb in range(first, last):
+                block = term[:, P * (tb - first) : P * (tb - first + 1)]
+                nc.tensor.matmul(sums[tb][:], block, ident[:], start=(d == 0), stop=(d == D - 1), is_transpose=True)
 
-        def add_transposed(acc, term, d):
-            nc.tensor.matmul(acc, term, ident[:], start=(d == 0), stop=(d == D - 1), is_transpose=True)
+        for d in range(D):
+            weighted(d, 0, 2)
+        for d in range(D - 1):
+            weighted(d, 2, BLOCKS)
+        weighted(D - 1, 2, 3)
+        weighted(D - 1, 3, BLOCKS)
 
-        first_half = quantize_hidden(0, 2)
-        third_block = quantize_hidden(2, 3)
-        for pair in range(2):
-            products(0, pair, slice(0, HALF), *first_half)
-        for pair in range(2):
-            products(1, pair, slice(0, P), *third_block)
-        args = [[add_own(0, 0)], []]
-        last_block = quantize_hidden(3, 4, after="h_scale0")
-        for pair in range(2):
-            products(1, pair, slice(P, HALF), *last_block)
-        args[0].append(add_own(0, 1))
-        args[1] = [add_own(1, pair) for pair in range(2)]
-
-        sums = [psum.tile([P, P], F32, name="sum%d" % tb, tag="h%d" % tb) for tb in range(BLOCKS)]
-        for th in range(2):
-            for d in range(D):
-                if (th, d) == (1, D - 1):
-                    for s in range(2):
-                        term = weighted(th, d, args[th][d // 2], slice(P * s, P * (s + 1)))
-                        add_transposed(sums[2 * th + s][:], term[:], d)
-                else:
-                    term = weighted(th, d, args[th][d // 2], slice(0, HALF))
-                    for s in range(2):
-                        add_transposed(sums[2 * th + s][:], term[:, P * s : P * (s + 1)], d)
-        first_out = sbuf("first_out", [P, 2, P], F32)
-        nc.scalar.copy(first_out[:, 0, :], sums[0][:])
-        nc.vector.tensor_copy(first_out[:, 1, :], sums[1][:])
+        first_out = sbuf("first_out", [P, 2, P], F32, after="arg13")
+        for tb in range(2):
+            nc.scalar.copy(first_out[:, tb, :], sums[tb][:])
         nc.sync.dma_start(out[0:HALF, :].rearrange("(s p) v -> p s v", s=2), first_out[:])
         for tb, copy in ((2, nc.scalar.copy), (3, nc.vector.tensor_copy)):
             block_out = sbuf("block_out%d" % tb, [P, P], F32)

@@ -24,7 +24,7 @@ BLOCKS = S // P
 HALF = S // 2
 POOL_TERMS = 3
 HALF_ROW, ALPHA_ROW = 16, 80
-E_FIRST = 8
+E_ROWS = 96
 ROW_SPLIT = 1536
 FLOPS = 2 * K * H * S + 2 * H * S * U
 
@@ -54,11 +54,13 @@ def tile_picked_yrbf_sum_p_kernel(
         own_cols = sbuf("own_cols", [P, BLOCKS], F32)
         ident = sbuf("ident", [P, P], F32)
         zero = sbuf("zero", [P, 1], F32)
+        e_scale = sbuf("e_scale", [P, D, P], U8)
 
         nc.vector.memset(x_scale_table[:].bitcast(I32), 0)
         nc.vector.memset(zero[:], 0.0)
         nc.vector.memset(e_scale_table[:].bitcast(I32), 0)
         nc.vector.memset(row_table[:, 0:ROW_SPLIT], 0.0)
+        nc.vector.memset(e_scale[:].bitcast(I32), 0)
         nc.scalar.activation(row_table[:, ROW_SPLIT:W], zero[:].to_broadcast([P, W - ROW_SPLIT]), ACT.Copy)
 
         def load_words(tile, words):
@@ -79,9 +81,10 @@ def tile_picked_yrbf_sum_p_kernel(
         nc.sync.dma_start(sv_sb[:], sv)
         load_scales(x_scale_table, x_scales, 0)
         load_weights(0)
+        e_rows = e_scale_table[E_ROWS : E_ROWS + 4 * QUADS, :]
+        nc.sync.dma_start(e_rows.bitcast(I32), e_scales[0].bitcast(I32))
         nc.sync.dma_start(row_table[HALF_ROW : HALF_ROW + 1, :], half[0:1, :])
         nc.sync.dma_start(row_table[ALPHA_ROW : ALPHA_ROW + 1, :], alpha[0:1, :])
-        load_scales(e_scale_table, e_scales, E_FIRST)
         load_weights(1)
         load_words(x_table[1], x_words[1])
         load_words(e_table, e_words[0])
@@ -101,7 +104,7 @@ def tile_picked_yrbf_sum_p_kernel(
 
         gather_x(0, 0, BLOCKS)
 
-        w_codes = [sbuf("w_codes0", [P, H], U32, after="e_scale_table"), sbuf("w_codes1", [P, H], U32)]
+        w_codes = [sbuf("w_codes%d" % o, [P, H], U32) for o in range(PASSES)]
         w_scale = [sbuf("w_scale%d" % o, [P, H], U8) for o in range(PASSES)]
         w_bf = [sbuf("w_bf%d" % o, [P, 2, 2 * H], BF16) for o in range(PASSES)]
 
@@ -115,29 +118,27 @@ def tile_picked_yrbf_sum_p_kernel(
             nc.scalar.activation(*views(0), ACT.Copy)
             nc.vector.tensor_copy(*views(1))
 
-        round_weights(0)
-        e_scale = sbuf("e_scale", [P, D, P], U8)
-        nc.vector.tensor_copy(e_scale[:].rearrange("p d v -> p v d"), e_scale_table[:].indirect(sv_sb[:]))
-        rows_picked = sbuf("rows_picked", [P, U], F32)
-        nc.scalar.activation(rows_picked[:], row_table[:].indirect(sv_sb[:]), ACT.Copy)
-        half_cols = sbuf("half_cols", [P, D], F32)
-        alpha_cols = sbuf("alpha_cols", [P, D], F32)
-        for cols, row in ((half_cols, HALF_ROW), (alpha_cols, ALPHA_ROW)):
-            nc.sync.dma_start(cols[:], rows_picked[row : row + 1, :].rearrange("o (v d) -> o v d", d=D))
-        neg_half = sbuf("neg_half", [P, D], F32)
-        nc.gpsimd.tensor_scalar(neg_half[:], half_cols[:], -1.0, 0.0, ALU.mult, ALU.add)
-        nc.vector.quantize_mx(
-            out=w_codes[0][:].bitcast(FP8X4), scales=w_scale[0][:], in_=w_bf[0][:].rearrange("p c n -> p (c n)")
-        )
+        def quantize_weights(o):
+            values = w_bf[o][:].rearrange("p c n -> p (c n)")
+            nc.vector.quantize_mx(out=w_codes[o][:].bitcast(FP8X4), scales=w_scale[o][:], in_=values)
 
-        def quantize_second(c):
-            cols = slice(2 * P * c, 2 * P * (c + 1))
-            nc.vector.quantize_mx(out=w_codes[1][:, cols].bitcast(FP8X4), scales=w_scale[1][:, cols], in_=w_bf[1][:, c, :])
+        round_weights(0)
+        e_scale_rows = sbuf("e_scale_rows", [P, D, P], U8)
+        nc.vector.tensor_copy(e_scale_rows[:].rearrange("p d v -> p v d"), e_scale_table[:].indirect(sv_sb[:]))
+        for q in range(QUADS):
+            rows = e_scale_rows[E_ROWS + 4 * q : E_ROWS + 4 * q + 4, :, :]
+            nc.sync.dma_start(e_scale[32 * q : 32 * q + 4, :, :].bitcast(I32), rows.bitcast(I32))
+        rows_picked = sbuf("rows_picked", [P, U], F32)
+        nc.scalar.activation(rows_picked[:], row_table[:].indirect(sv_sb[:]), ACT.Copy, scale=-1.0)
+        neg_half = sbuf("neg_half", [P, D], F32)
+        neg_alpha = sbuf("neg_alpha", [P, D], F32)
+        for cols, row in ((neg_half, HALF_ROW), (neg_alpha, ALPHA_ROW)):
+            nc.sync.dma_start(cols[:], rows_picked[row : row + 1, :].rearrange("o (v d) -> o v d", d=D))
+        quantize_weights(0)
 
         round_weights(1)
-        quantize_second(1)
         gather_x(1, 0, 1)
-        quantize_second(0)
+        quantize_weights(1)
         own_rows = sbuf("own_rows", [P, S], F32, at=0)
         gather_x(1, 1, 2, at=4 * S)
         gather_x(1, 2, BLOCKS, at=8 * S)
@@ -148,7 +149,6 @@ def tile_picked_yrbf_sum_p_kernel(
         nc.scalar.copy(own_rows[:].rearrange("m (p s) -> m p s", s=BLOCKS), own_ps[:].rearrange("m s p -> m p s"))
 
         h_ps = [psum.tile([P, PACK, P], F32, name="h_ps%d" % tb, tag="h%d" % tb) for tb in range(BLOCKS)]
-        second_order = (2, 3, 0, 1)
 
         def project(tb, r, o):
             samples = slice(P * tb, P * (tb + 1))
@@ -160,13 +160,13 @@ def tile_picked_yrbf_sum_p_kernel(
                 rhs=x_codes[o, tb].bitcast(FP8X4),
                 rhs_scale=x_scale[4 * o : P, samples],
                 start=(o, r) == (0, 0),
-                stop=(o, r) == (1, second_order[-1]),
+                stop=(o, r) == (PASSES - 1, PACK - 1),
             )
 
         h_bf = [sbuf("h_bf%d" % th, [P, HALF, PACK], BF16) for th in range(2)]
 
         def second_pass(tb):
-            for r in second_order:
+            for r in range(PACK):
                 project(tb, r, 1)
             nc.scalar.copy(h_bf[tb // 2][:, P * (tb % 2) : P * (tb % 2 + 1), :], h_ps[tb][:].rearrange("p r t -> p t r"))
 
@@ -181,7 +181,13 @@ def tile_picked_yrbf_sum_p_kernel(
         e_codes = sbuf("e_codes", [P, D, P], U32)
         nc.vector.tensor_copy(e_codes[:].rearrange("p d v -> p v d"), e_table[:].bitcast(U32).indirect(sv_sb[:]))
 
+        y_first = psum.tile([P, HALF], F32, name="y_first", tag="h0")
         y_ps = [psum.tile([P, 2, HALF], F32, name="y_ps%d" % bank, tag="y%d" % bank) for bank in range(D)]
+
+        def y_of(th, first, last):
+            if (th, first) == (0, 0):
+                return y_first[:].unsqueeze(1)
+            return y_ps[2 * th + first // 2][:, first % 2 : first % 2 + last - first, :]
 
         def products(th):
             codes = sbuf("h_codes%d" % th, [P, HALF], U32, after="rows_picked" if th == 0 else None)
@@ -191,9 +197,9 @@ def tile_picked_yrbf_sum_p_kernel(
             )
             for d in range(D):
                 nc.tensor.matmul_mx(
-                    out=y_ps[2 * th + d // 2][:, d % 2, :],
+                    out=y_of(th, d, d + 1)[:, 0, :],
                     lhsT=e_codes[:, d, :].bitcast(FP8X4),
-                    lhsT_scale=e_scale[E_FIRST:P, d, :],
+                    lhsT_scale=e_scale[:, d, :],
                     rhs=codes[:].bitcast(FP8X4),
                     rhs_scale=scale[:],
                     start=True,
@@ -206,8 +212,7 @@ def tile_picked_yrbf_sum_p_kernel(
             count = last - first
             arg = sbuf("arg%d%d" % (th, first), [P, count, HALF], F32)
             own_view = own_rows[:, HALF * th : HALF * (th + 1)].unsqueeze(1).to_broadcast([P, count, HALF])
-            y = y_ps[2 * th + first // 2][:, first % 2 : first % 2 + count, :]
-            nc.vector.scalar_tensor_tensor(arg[:], y, 0.5, own_view, ALU.mult, ALU.add)
+            nc.vector.scalar_tensor_tensor(arg[:], y_of(th, first, last), 0.5, own_view, ALU.mult, ALU.add)
             for d in range(first, last):
                 args[th, d] = arg[:, d - first, :]
 
@@ -230,9 +235,9 @@ def tile_picked_yrbf_sum_p_kernel(
             nc.scalar.activation(value[:], arg, ACT.Exp, bias=neg_half[:, d : d + 1])
             term = sbuf("term" + name, [P, P * (last - first)], F32)
             if D * th + d < POOL_TERMS:
-                nc.gpsimd.tensor_scalar(term[:], value[:], alpha_cols[:, d : d + 1], 0.0, ALU.mult, ALU.add)
+                nc.gpsimd.tensor_scalar(term[:], value[:], neg_alpha[:, d : d + 1], 0.0, ALU.mult, ALU.add)
             else:
-                nc.vector.tensor_scalar(term[:], value[:], alpha_cols[:, d : d + 1], None, ALU.mult)
+                nc.vector.tensor_scalar(term[:], value[:], neg_alpha[:, d : d + 1], None, ALU.mult)
             for tb in range(first, last):
                 block = term[:, P * (tb - first) : P * (tb - first + 1)]
                 nc.tensor.matmul(sums[tb][:], block, ident[:], start=(d == 0), stop=(d == D - 1), is_transpose=True)
@@ -246,9 +251,11 @@ def tile_picked_yrbf_sum_p_kernel(
 
         first_out = sbuf("first_out", [P, 2, P], F32, after="arg13")
         for tb in range(2):
-            nc.scalar.copy(first_out[:, tb, :], sums[tb][:])
+            nc.scalar.activation(first_out[:, tb, :], sums[tb][:], ACT.Copy, scale=-1.0)
         nc.sync.dma_start(out[0:HALF, :].rearrange("(s p) v -> p s v", s=2), first_out[:])
-        for tb, copy in ((2, nc.scalar.copy), (3, nc.vector.tensor_copy)):
-            block_out = sbuf("block_out%d" % tb, [P, P], F32)
-            copy(block_out[:], sums[tb][:])
-            nc.sync.dma_start(out[P * tb : P * (tb + 1), :], block_out[:])
+        third_out = sbuf("third_out", [P, P], F32)
+        nc.scalar.activation(third_out[:], sums[2][:], ACT.Copy, scale=-1.0)
+        nc.sync.dma_start(out[2 * P : 3 * P, :], third_out[:])
+        last_out = sbuf("last_out", [P, P], F32)
+        nc.vector.tensor_scalar(last_out[:], sums[3][:], -1.0, None, ALU.mult)
+        nc.sync.dma_start(out[3 * P : S, :], last_out[:])

@@ -24,7 +24,8 @@ BLOCKS = S // P
 HALF = S // 2
 POOL_TERMS = 3
 HALF_ROW, ALPHA_ROW = 16, 80
-E_ROWS = 96
+E_ROWS = range(32, 96, 4)
+PICKED_AT = 4 * PACK * H
 ROW_SPLIT = 1536
 FLOPS = 2 * K * H * S + 2 * H * S * U
 
@@ -81,7 +82,7 @@ def tile_picked_yrbf_sum_p_kernel(
         nc.sync.dma_start(sv_sb[:], sv)
         load_scales(x_scale_table, x_scales, 0)
         load_weights(0)
-        e_rows = e_scale_table[E_ROWS : E_ROWS + 4 * QUADS, :]
+        e_rows = e_scale_table[E_ROWS.start : E_ROWS.stop : E_ROWS.step, :]
         nc.sync.dma_start(e_rows.bitcast(I32), e_scales[0].bitcast(I32))
         nc.sync.dma_start(row_table[HALF_ROW : HALF_ROW + 1, :], half[0:1, :])
         nc.sync.dma_start(row_table[ALPHA_ROW : ALPHA_ROW + 1, :], alpha[0:1, :])
@@ -126,9 +127,9 @@ def tile_picked_yrbf_sum_p_kernel(
         e_scale_rows = sbuf("e_scale_rows", [P, D, P], U8)
         nc.vector.tensor_copy(e_scale_rows[:].rearrange("p d v -> p v d"), e_scale_table[:].indirect(sv_sb[:]))
         for q in range(QUADS):
-            rows = e_scale_rows[E_ROWS + 4 * q : E_ROWS + 4 * q + 4, :, :]
+            rows = e_scale_rows[E_ROWS[4 * q] : E_ROWS[4 * q + 3] + 1 : E_ROWS.step, :, :]
             nc.sync.dma_start(e_scale[32 * q : 32 * q + 4, :, :].bitcast(I32), rows.bitcast(I32))
-        rows_picked = sbuf("rows_picked", [P, U], F32)
+        rows_picked = sbuf("rows_picked", [P, U], F32, at=PICKED_AT)
         nc.scalar.activation(rows_picked[:], row_table[:].indirect(sv_sb[:]), ACT.Copy, scale=-1.0)
         neg_half = sbuf("neg_half", [P, D], F32)
         neg_alpha = sbuf("neg_alpha", [P, D], F32)
@@ -189,22 +190,27 @@ def tile_picked_yrbf_sum_p_kernel(
                 return y_first[:].unsqueeze(1)
             return y_ps[2 * th + first // 2][:, first % 2 : first % 2 + last - first, :]
 
-        def products(th):
-            codes = sbuf("h_codes%d" % th, [P, HALF], U32, after="rows_picked" if th == 0 else None)
-            scale = sbuf("h_scale%d" % th, [P, HALF], U8, after="h_scale0")
+        def products(first, last, codes_at=None, scale_after=None):
+            th, cols = first // 2, slice(P * (first % 2), P * (first % 2 + last - first))
+            codes = sbuf("h_codes%d" % first, [P, P * (last - first)], U32, at=codes_at)
+            scale = sbuf("h_scale%d" % first, [P, P * (last - first)], U8, after=scale_after)
             nc.vector.quantize_mx(
-                out=codes[:].bitcast(FP8X4), scales=scale[:], in_=h_bf[th][:].rearrange("p t r -> p (t r)")
+                out=codes[:].bitcast(FP8X4), scales=scale[:], in_=h_bf[th][:, cols, :].rearrange("p t r -> p (t r)")
             )
-            for d in range(D):
-                nc.tensor.matmul_mx(
-                    out=y_of(th, d, d + 1)[:, 0, :],
-                    lhsT=e_codes[:, d, :].bitcast(FP8X4),
-                    lhsT_scale=e_scale[:, d, :],
-                    rhs=codes[:].bitcast(FP8X4),
-                    rhs_scale=scale[:],
-                    start=True,
-                    stop=True,
-                )
+
+            def multiply():
+                for d in range(D):
+                    nc.tensor.matmul_mx(
+                        out=y_of(th, d, d + 1)[:, 0, cols],
+                        lhsT=e_codes[:, d, :].bitcast(FP8X4),
+                        lhsT_scale=e_scale[:, d, :],
+                        rhs=codes[:].bitcast(FP8X4),
+                        rhs_scale=scale[:],
+                        start=True,
+                        stop=True,
+                    )
+
+            return multiply
 
         args = {}
 
@@ -216,9 +222,12 @@ def tile_picked_yrbf_sum_p_kernel(
             for d in range(first, last):
                 args[th, d] = arg[:, d - first, :]
 
-        products(0)
+        first_half = products(0, 2, codes_at=PICKED_AT)
+        third_block = products(2, 3, codes_at=PICKED_AT + 4 * HALF)
+        first_half()
+        third_block()
         add_own(0, 0, 1)
-        products(1)
+        products(3, 4, scale_after="h_scale0")()
         add_own(0, 1, 2)
         add_own(0, 2, 4)
         add_own(1, 0, 2)

@@ -26,6 +26,8 @@ POOL_TERMS = 3
 HALF_ROW, ALPHA_ROW = 16, 80
 E_ROWS = range(32, 96, 4)
 PICKED_AT = 4 * PACK * H
+Y_BANKS = ((3, 4), (1, 3))
+SUM_BANKS = (6, 2, 5, 0)
 ROW_SPLIT = 1536
 FLOPS = 2 * K * H * S + 2 * H * S * U
 
@@ -119,9 +121,10 @@ def tile_picked_yrbf_sum_p_kernel(
             nc.scalar.activation(*views(0), ACT.Copy)
             nc.vector.tensor_copy(*views(1))
 
-        def quantize_weights(o):
-            values = w_bf[o][:].rearrange("p c n -> p (c n)")
-            nc.vector.quantize_mx(out=w_codes[o][:].bitcast(FP8X4), scales=w_scale[o][:], in_=values)
+        def quantize_weights(o, first, last):
+            cols = slice(2 * P * first, 2 * P * last)
+            values = w_bf[o][:, first:last, :].rearrange("p c n -> p (c n)")
+            nc.vector.quantize_mx(out=w_codes[o][:, cols].bitcast(FP8X4), scales=w_scale[o][:, cols], in_=values)
 
         round_weights(0)
         e_scale_rows = sbuf("e_scale_rows", [P, D, P], U8)
@@ -135,21 +138,22 @@ def tile_picked_yrbf_sum_p_kernel(
         neg_alpha = sbuf("neg_alpha", [P, D], F32)
         for cols, row in ((neg_half, HALF_ROW), (neg_alpha, ALPHA_ROW)):
             nc.sync.dma_start(cols[:], rows_picked[row : row + 1, :].rearrange("o (v d) -> o v d", d=D))
-        quantize_weights(0)
+        quantize_weights(0, 0, 2)
 
         round_weights(1)
+        quantize_weights(1, 1, 2)
         gather_x(1, 0, 1)
-        quantize_weights(1)
+        quantize_weights(1, 0, 1)
         own_rows = sbuf("own_rows", [P, S], F32, at=0)
         gather_x(1, 1, 2, at=4 * S)
         gather_x(1, 2, BLOCKS, at=8 * S)
 
-        own_ps = psum.tile([P, BLOCKS, P], F32, name="own_ps", tag="h3")
+        own_ps = psum.tile([P, BLOCKS, P], F32, name="own_ps", tag="bank3")
         for s in range(BLOCKS):
             nc.tensor.transpose(own_ps[:, s, :], own_cols[:, s : s + 1].to_broadcast([P, P]), ident[:])
         nc.scalar.copy(own_rows[:].rearrange("m (p s) -> m p s", s=BLOCKS), own_ps[:].rearrange("m s p -> m p s"))
 
-        h_ps = [psum.tile([P, PACK, P], F32, name="h_ps%d" % tb, tag="h%d" % tb) for tb in range(BLOCKS)]
+        h_ps = [psum.tile([P, PACK, P], F32, name="h_ps%d" % tb, tag="bank%d" % (tb % 3)) for tb in range(BLOCKS)]
 
         def project(tb, r, o):
             samples = slice(P * tb, P * (tb + 1))
@@ -161,34 +165,38 @@ def tile_picked_yrbf_sum_p_kernel(
                 rhs=x_codes[o, tb].bitcast(FP8X4),
                 rhs_scale=x_scale[4 * o : P, samples],
                 start=(o, r) == (0, 0),
-                stop=(o, r) == (PASSES - 1, PACK - 1),
+                stop=(o, r) == (PASSES - 1, 1),
             )
 
         h_bf = [sbuf("h_bf%d" % th, [P, HALF, PACK], BF16) for th in range(2)]
 
         def second_pass(tb):
-            for r in range(PACK):
+            for r in (2, 3, 0, 1):
                 project(tb, r, 1)
             nc.scalar.copy(h_bf[tb // 2][:, P * (tb % 2) : P * (tb % 2 + 1), :], h_ps[tb][:].rearrange("p r t -> p t r"))
 
-        for tb in range(BLOCKS):
-            if tb == BLOCKS - 1:
-                second_pass(0)
+        for tb in range(BLOCKS - 1):
             for r in range(PACK):
                 project(tb, r, 0)
-        for tb in range(1, BLOCKS):
+        for tb in range(BLOCKS - 1):
             second_pass(tb)
+        for r in range(PACK):
+            project(BLOCKS - 1, r, 0)
+        second_pass(BLOCKS - 1)
 
         e_codes = sbuf("e_codes", [P, D, P], U32)
         nc.vector.tensor_copy(e_codes[:].rearrange("p d v -> p v d"), e_table[:].bitcast(U32).indirect(sv_sb[:]))
 
-        y_first = psum.tile([P, HALF], F32, name="y_first", tag="h0")
-        y_ps = [psum.tile([P, 2, HALF], F32, name="y_ps%d" % bank, tag="y%d" % bank) for bank in range(D)]
+        y_first = psum.tile([P, HALF], F32, name="y_first", tag="bank1")
+        y_ps = {}
 
         def y_of(th, first, last):
             if (th, first) == (0, 0):
                 return y_first[:].unsqueeze(1)
-            return y_ps[2 * th + first // 2][:, first % 2 : first % 2 + last - first, :]
+            pair = first // 2
+            if (th, pair) not in y_ps:
+                y_ps[th, pair] = psum.tile([P, 2, HALF], F32, name="y_ps%d%d" % (th, pair), tag="bank%d" % Y_BANKS[th][pair])
+            return y_ps[th, pair][:, first % 2 : first % 2 + last - first, :]
 
         def products(first, last, codes_at=None, scale_after=None):
             th, cols = first // 2, slice(P * (first % 2), P * (first % 2 + last - first))
@@ -198,8 +206,8 @@ def tile_picked_yrbf_sum_p_kernel(
                 out=codes[:].bitcast(FP8X4), scales=scale[:], in_=h_bf[th][:, cols, :].rearrange("p t r -> p (t r)")
             )
 
-            def multiply():
-                for d in range(D):
+            def multiply(pairs):
+                for d in range(2 * pairs.start, 2 * pairs.stop):
                     nc.tensor.matmul_mx(
                         out=y_of(th, d, d + 1)[:, 0, cols],
                         lhsT=e_codes[:, d, :].bitcast(FP8X4),
@@ -224,17 +232,20 @@ def tile_picked_yrbf_sum_p_kernel(
 
         first_half = products(0, 2, codes_at=PICKED_AT)
         third_block = products(2, 3, codes_at=PICKED_AT + 4 * HALF)
-        first_half()
-        third_block()
+        first_half(range(2))
         add_own(0, 0, 1)
-        products(3, 4, scale_after="h_scale0")()
+        last_block = products(3, 4, scale_after="h_scale0")
         add_own(0, 1, 2)
+        third_block(range(1))
+        last_block(range(1))
         add_own(0, 2, 4)
+        third_block(range(1, 2))
+        last_block(range(1, 2))
         add_own(1, 0, 2)
         add_own(1, 2, 3)
         add_own(1, 3, 4)
 
-        sums = [psum.tile([P, P], F32, name="sum%d" % tb, tag="h%d" % tb) for tb in range(BLOCKS)]
+        sums = [psum.tile([P, P], F32, name="sum%d" % tb, tag="bank%d" % SUM_BANKS[tb]) for tb in range(BLOCKS)]
 
         def weighted(d, first, last):
             name = "%d%d" % (d, first)

@@ -25,7 +25,7 @@ HALF = S // 2
 POOL_TERMS = 3
 HALF_ROW, ALPHA_ROW = 16, 80
 E_ROWS = range(32, 96, 4)
-PICKED_AT = 4 * PACK * H
+PICKED_AT = 4 * PACK * H + 4 * HALF
 Y_BANKS = ((3, 4), (1, 3))
 SUM_BANKS = (6, 2, 5, 0)
 ROW_SPLIT = 1536
@@ -127,12 +127,12 @@ def tile_picked_yrbf_sum_p_kernel(
             nc.vector.quantize_mx(out=w_codes[o][:, cols].bitcast(FP8X4), scales=w_scale[o][:, cols], in_=values)
 
         round_weights(0)
-        e_scale_rows = sbuf("e_scale_rows", [P, D, P], U8)
+        e_scale_rows = sbuf("e_scale_rows", [P, D, P], U8, at=PICKED_AT)
         nc.vector.tensor_copy(e_scale_rows[:].rearrange("p d v -> p v d"), e_scale_table[:].indirect(sv_sb[:]))
         for q in range(QUADS):
             rows = e_scale_rows[E_ROWS[4 * q] : E_ROWS[4 * q + 3] + 1 : E_ROWS.step, :, :]
             nc.sync.dma_start(e_scale[32 * q : 32 * q + 4, :, :].bitcast(I32), rows.bitcast(I32))
-        rows_picked = sbuf("rows_picked", [P, U], F32, at=PICKED_AT)
+        rows_picked = sbuf("rows_picked", [P, U], F32)
         nc.scalar.activation(rows_picked[:], row_table[:].indirect(sv_sb[:]), ACT.Copy, scale=-1.0)
         neg_half = sbuf("neg_half", [P, D], F32)
         neg_alpha = sbuf("neg_alpha", [P, D], F32)
@@ -230,8 +230,8 @@ def tile_picked_yrbf_sum_p_kernel(
             for d in range(first, last):
                 args[th, d] = arg[:, d - first, :]
 
-        first_half = products(0, 2, codes_at=PICKED_AT)
-        third_block = products(2, 3, codes_at=PICKED_AT + 4 * HALF)
+        first_half = products(0, 2, codes_at=PICKED_AT + 64 - 4 * HALF)
+        third_block = products(2, 3, codes_at=PICKED_AT + 64)
         first_half(range(2))
         add_own(0, 0, 1)
         last_block = products(3, 4, scale_after="h_scale0")
@@ -243,7 +243,6 @@ def tile_picked_yrbf_sum_p_kernel(
         last_block(range(1, 2))
         add_own(1, 0, 2)
         add_own(1, 2, 3)
-        add_own(1, 3, 4)
 
         sums = [psum.tile([P, P], F32, name="sum%d" % tb, tag="bank%d" % SUM_BANKS[tb]) for tb in range(BLOCKS)]
 
@@ -264,6 +263,7 @@ def tile_picked_yrbf_sum_p_kernel(
 
         for d in range(D):
             weighted(d, 0, 2)
+        add_own(1, 3, 4)
         for d in range(D - 1):
             weighted(d, 2, BLOCKS)
         weighted(D - 1, 2, 3)

@@ -26,8 +26,8 @@ POOL_TERMS = 3
 HALF_ROW, ALPHA_ROW = 16, 80
 E_ROWS = range(32, 96, 4)
 PICKED_AT = 4 * PACK * H + 4 * HALF
-Y_BANKS = ((3, 4), (1, 3))
-SUM_BANKS = (6, 2, 5, 0)
+Y_BANKS = (4, 5, 6, 7)
+SUM_BANKS = (3, 1, 2, 0)
 ROW_SPLIT = 1536
 FLOPS = 2 * K * H * S + 2 * H * S * U
 
@@ -187,62 +187,33 @@ def tile_picked_yrbf_sum_p_kernel(
         e_codes = sbuf("e_codes", [P, D, P], U32)
         nc.vector.tensor_copy(e_codes[:].rearrange("p d v -> p v d"), e_table[:].bitcast(U32).indirect(sv_sb[:]))
 
-        y_first = psum.tile([P, HALF], F32, name="y_first", tag="bank1")
-        y_ps = {}
+        h_codes = [sbuf("h_codes%d" % th, [P, HALF], U32, at=PICKED_AT + 64 - 4 * HALF * (1 - th)) for th in range(2)]
+        h_scale = [sbuf("h_scale%d" % th, [P, HALF], U8) for th in range(2)]
 
-        def y_of(th, first, last):
-            if (th, first) == (0, 0):
-                return y_first[:].unsqueeze(1)
-            pair = first // 2
-            if (th, pair) not in y_ps:
-                y_ps[th, pair] = psum.tile([P, 2, HALF], F32, name="y_ps%d%d" % (th, pair), tag="bank%d" % Y_BANKS[th][pair])
-            return y_ps[th, pair][:, first % 2 : first % 2 + last - first, :]
+        def quantize_hidden(th, cols):
+            values = h_bf[th][:, cols, :].rearrange("p t r -> p (t r)")
+            nc.vector.quantize_mx(out=h_codes[th][:, cols].bitcast(FP8X4), scales=h_scale[th][:, cols], in_=values)
 
-        def products(first, last, codes_at=None, scale_after=None):
-            th, cols = first // 2, slice(P * (first % 2), P * (first % 2 + last - first))
-            codes = sbuf("h_codes%d" % first, [P, P * (last - first)], U32, at=codes_at)
-            scale = sbuf("h_scale%d" % first, [P, P * (last - first)], U8, after=scale_after)
-            nc.vector.quantize_mx(
-                out=codes[:].bitcast(FP8X4), scales=scale[:], in_=h_bf[th][:, cols, :].rearrange("p t r -> p (t r)")
-            )
-
-            def multiply(pairs):
-                for d in range(2 * pairs.start, 2 * pairs.stop):
-                    nc.tensor.matmul_mx(
-                        out=y_of(th, d, d + 1)[:, 0, cols],
-                        lhsT=e_codes[:, d, :].bitcast(FP8X4),
-                        lhsT_scale=e_scale[:, d, :],
-                        rhs=codes[:].bitcast(FP8X4),
-                        rhs_scale=scale[:],
-                        start=True,
-                        stop=True,
-                    )
-
-            return multiply
+        quantize_hidden(0, slice(0, HALF))
+        quantize_hidden(1, slice(0, P))
+        quantize_hidden(1, slice(P, HALF))
 
         args = {}
-
-        def add_own(th, first, last):
-            count = last - first
-            arg = sbuf("arg%d%d" % (th, first), [P, count, HALF], F32)
-            own_view = own_rows[:, HALF * th : HALF * (th + 1)].unsqueeze(1).to_broadcast([P, count, HALF])
-            nc.vector.scalar_tensor_tensor(arg[:], y_of(th, first, last), 0.5, own_view, ALU.mult, ALU.add)
-            for d in range(first, last):
-                args[th, d] = arg[:, d - first, :]
-
-        first_half = products(0, 2, codes_at=PICKED_AT + 64 - 4 * HALF)
-        third_block = products(2, 3, codes_at=PICKED_AT + 64)
-        first_half(range(2))
-        add_own(0, 0, 1)
-        last_block = products(3, 4, scale_after="h_scale0")
-        add_own(0, 1, 2)
-        third_block(range(1))
-        last_block(range(1))
-        add_own(0, 2, 4)
-        third_block(range(1, 2))
-        last_block(range(1, 2))
-        add_own(1, 0, 2)
-        add_own(1, 2, 3)
+        for th in range(2):
+            for d in range(D):
+                y = psum.tile([P, HALF], F32, name="y%d%d" % (th, d), tag="bank%d" % Y_BANKS[d])
+                nc.tensor.matmul_mx(
+                    out=y[:],
+                    lhsT=e_codes[:, d, :].bitcast(FP8X4),
+                    lhsT_scale=e_scale[:, d, :],
+                    rhs=h_codes[th][:].bitcast(FP8X4),
+                    rhs_scale=h_scale[th][:],
+                    start=True,
+                    stop=True,
+                )
+                args[th, d] = sbuf("arg%d%d" % (th, d), [P, HALF], F32)
+                own_half = own_rows[:, HALF * th : HALF * (th + 1)]
+                nc.vector.scalar_tensor_tensor(args[th, d][:], y[:], 0.5, own_half, ALU.mult, ALU.add)
 
         sums = [psum.tile([P, P], F32, name="sum%d" % tb, tag="bank%d" % SUM_BANKS[tb]) for tb in range(BLOCKS)]
 
@@ -257,17 +228,22 @@ def tile_picked_yrbf_sum_p_kernel(
                 nc.gpsimd.tensor_scalar(term[:], value[:], neg_alpha[:, d : d + 1], 0.0, ALU.mult, ALU.add)
             else:
                 nc.vector.tensor_scalar(term[:], value[:], neg_alpha[:, d : d + 1], None, ALU.mult)
-            for tb in range(first, last):
-                block = term[:, P * (tb - first) : P * (tb - first + 1)]
-                nc.tensor.matmul(sums[tb][:], block, ident[:], start=(d == 0), stop=(d == D - 1), is_transpose=True)
+            return term
 
-        for d in range(D):
-            weighted(d, 0, 2)
-        add_own(1, 3, 4)
-        for d in range(D - 1):
-            weighted(d, 2, BLOCKS)
-        weighted(D - 1, 2, 3)
-        weighted(D - 1, 3, BLOCKS)
+        def add_transposed(term, first, start, stop):
+            for s in range(term.shape[1] // P):
+                block = term[:, P * s : P * (s + 1)]
+                nc.tensor.matmul(sums[first + s][:], block, ident[:], start=start, stop=stop, is_transpose=True)
+
+        terms = [weighted(d, 0, 2) for d in range(D)]
+        for d in (0, 1, 3):
+            add_transposed(terms[d], 0, d == 0, False)
+        add_transposed(weighted(0, 2, BLOCKS), 2, True, False)
+        add_transposed(terms[2], 0, False, True)
+        for d in range(1, D - 1):
+            add_transposed(weighted(d, 2, BLOCKS), 2, False, False)
+        for tb in range(2, BLOCKS):
+            add_transposed(weighted(D - 1, tb, tb + 1), tb, False, True)
 
         first_out = sbuf("first_out", [P, 2, P], F32, after="arg13")
         for tb in range(2):

@@ -86,9 +86,9 @@ def tile_picked_yrbf_sum_p_kernel(
         load_weights(0)
         e_rows = e_scale_table[E_ROWS.start : E_ROWS.stop : E_ROWS.step, :]
         nc.sync.dma_start(e_rows.bitcast(I32), e_scales[0].bitcast(I32))
+        load_weights(1)
         nc.sync.dma_start(row_table[HALF_ROW : HALF_ROW + 1, :], half[0:1, :])
         nc.sync.dma_start(row_table[ALPHA_ROW : ALPHA_ROW + 1, :], alpha[0:1, :])
-        load_weights(1)
         load_words(x_table[1], x_words[1])
         load_words(e_table, e_words[0])
         make_identity(nc, ident[:])
@@ -132,26 +132,26 @@ def tile_picked_yrbf_sum_p_kernel(
         for q in range(QUADS):
             rows = e_scale_rows[E_ROWS[4 * q] : E_ROWS[4 * q + 3] + 1 : E_ROWS.step, :, :]
             nc.sync.dma_start(e_scale[32 * q : 32 * q + 4, :, :].bitcast(I32), rows.bitcast(I32))
-        rows_picked = sbuf("rows_picked", [P, U], F32)
-        nc.scalar.activation(rows_picked[:], row_table[:].indirect(sv_sb[:]), ACT.Copy, scale=-1.0)
-        neg_half = sbuf("neg_half", [P, D], F32)
-        neg_alpha = sbuf("neg_alpha", [P, D], F32)
-        for cols, row in ((neg_half, HALF_ROW), (neg_alpha, ALPHA_ROW)):
-            nc.sync.dma_start(cols[:], rows_picked[row : row + 1, :].rearrange("o (v d) -> o v d", d=D))
         quantize_weights(0, 0, 2)
+
+        own_rows = sbuf("own_rows", [P, S], F32)
+        own_ps = psum.tile([P, BLOCKS, P], F32, name="own_ps", tag="bank3")
+        for s in range(BLOCKS):
+            nc.tensor.transpose(own_ps[:, s, :], own_cols[:, s : s + 1].to_broadcast([P, P]), ident[:])
+        nc.scalar.copy(own_rows[:].rearrange("m (p s) -> m p s", s=BLOCKS), own_ps[:].rearrange("m s p -> m p s"))
 
         round_weights(1)
         quantize_weights(1, 1, 2)
         gather_x(1, 0, 1)
         quantize_weights(1, 0, 1)
-        own_rows = sbuf("own_rows", [P, S], F32, at=0)
         gather_x(1, 1, 2, at=4 * S)
         gather_x(1, 2, BLOCKS, at=8 * S)
-
-        own_ps = psum.tile([P, BLOCKS, P], F32, name="own_ps", tag="bank3")
-        for s in range(BLOCKS):
-            nc.tensor.transpose(own_ps[:, s, :], own_cols[:, s : s + 1].to_broadcast([P, P]), ident[:])
-        nc.scalar.copy(own_rows[:].rearrange("m (p s) -> m p s", s=BLOCKS), own_ps[:].rearrange("m s p -> m p s"))
+        rows_picked = sbuf("rows_picked", [P, U], F32, at=0)
+        nc.scalar.activation(rows_picked[:], row_table[:].indirect(sv_sb[:]), ACT.Copy, scale=-1.0)
+        neg_half = sbuf("neg_half", [P, D], F32)
+        neg_alpha = sbuf("neg_alpha", [P, D], F32)
+        for cols, row in ((neg_half, HALF_ROW), (neg_alpha, ALPHA_ROW)):
+            nc.sync.dma_start(cols[:], rows_picked[row : row + 1, :].rearrange("o (v d) -> o v d", d=D))
 
         h_ps = [psum.tile([P, PACK, P], F32, name="h_ps%d" % tb, tag="bank%d" % (tb % 3)) for tb in range(BLOCKS)]
 
@@ -187,33 +187,46 @@ def tile_picked_yrbf_sum_p_kernel(
         e_codes = sbuf("e_codes", [P, D, P], U32)
         nc.vector.tensor_copy(e_codes[:].rearrange("p d v -> p v d"), e_table[:].bitcast(U32).indirect(sv_sb[:]))
 
-        h_codes = [sbuf("h_codes%d" % th, [P, HALF], U32, at=PICKED_AT + 64 - 4 * HALF * (1 - th)) for th in range(2)]
-        h_scale = [sbuf("h_scale%d" % th, [P, HALF], U8) for th in range(2)]
+        def quantize_hidden(first, last, codes_at=None, scale_after=None):
+            samples = P * (last - first)
+            codes = sbuf("h_codes%d" % first, [P, samples], U32, at=codes_at)
+            scale = sbuf("h_scale%d" % first, [P, samples], U8, after=scale_after)
+            values = h_bf[first // 2][:, P * (first % 2) : P * (first % 2) + samples, :].rearrange("p t r -> p (t r)")
+            nc.vector.quantize_mx(out=codes[:].bitcast(FP8X4), scales=scale[:], in_=values)
+            return codes, scale
 
-        def quantize_hidden(th, cols):
-            values = h_bf[th][:, cols, :].rearrange("p t r -> p (t r)")
-            nc.vector.quantize_mx(out=h_codes[th][:, cols].bitcast(FP8X4), scales=h_scale[th][:, cols], in_=values)
-
-        quantize_hidden(0, slice(0, HALF))
-        quantize_hidden(1, slice(0, P))
-        quantize_hidden(1, slice(P, HALF))
-
-        args = {}
-        for th in range(2):
-            for d in range(D):
-                y = psum.tile([P, HALF], F32, name="y%d%d" % (th, d), tag="bank%d" % Y_BANKS[d])
+        def product(th, d, pieces):
+            y = psum.tile([P, HALF], F32, name="y%d%d" % (th, d), tag="bank%d" % Y_BANKS[d])
+            start = 0
+            for codes, scale in pieces:
                 nc.tensor.matmul_mx(
-                    out=y[:],
+                    out=y[:, start : start + codes.shape[1]],
                     lhsT=e_codes[:, d, :].bitcast(FP8X4),
                     lhsT_scale=e_scale[:, d, :],
-                    rhs=h_codes[th][:].bitcast(FP8X4),
-                    rhs_scale=h_scale[th][:],
+                    rhs=codes[:].bitcast(FP8X4),
+                    rhs_scale=scale[:],
                     start=True,
                     stop=True,
                 )
-                args[th, d] = sbuf("arg%d%d" % (th, d), [P, HALF], F32)
-                own_half = own_rows[:, HALF * th : HALF * (th + 1)]
-                nc.vector.scalar_tensor_tensor(args[th, d][:], y[:], 0.5, own_half, ALU.mult, ALU.add)
+                start = start + codes.shape[1]
+            return y
+
+        args = {}
+
+        def add_own(th, d, y):
+            args[th, d] = sbuf("arg%d%d" % (th, d), [P, HALF], F32)
+            own_half = own_rows[:, HALF * th : HALF * (th + 1)]
+            nc.vector.scalar_tensor_tensor(args[th, d][:], y[:], 0.5, own_half, ALU.mult, ALU.add)
+
+        first_half = quantize_hidden(0, 2, codes_at=PICKED_AT + 64 - 4 * HALF)
+        third_block = quantize_hidden(2, 3, codes_at=PICKED_AT + 64)
+        first_y = [product(0, d, [first_half]) for d in range(D)]
+        add_own(0, 0, first_y[0])
+        last_block = quantize_hidden(3, 4, scale_after="h_scale0")
+        for d in range(1, D):
+            add_own(0, d, first_y[d])
+        for d in range(D):
+            add_own(1, d, product(1, d, [third_block, last_block]))
 
         sums = [psum.tile([P, P], F32, name="sum%d" % tb, tag="bank%d" % SUM_BANKS[tb]) for tb in range(BLOCKS)]
 

@@ -22,7 +22,7 @@ H, W, U, D = 512, 2048, 512, 4
 PASSES = K // (P * PACK)
 BLOCKS = S // P
 HALF = S // 2
-POOL_TERMS = 3
+POOL_TERMS = 2
 HALF_ROW, ALPHA_ROW = 16, 80
 E_ROWS = range(32, 96, 4)
 PICKED_AT = 4 * PACK * H + 4 * HALF
@@ -216,7 +216,7 @@ def tile_picked_yrbf_sum_p_kernel(
         def add_own(th, d, y):
             args[th, d] = sbuf("arg%d%d" % (th, d), [P, HALF], F32)
             own_half = own_rows[:, HALF * th : HALF * (th + 1)]
-            nc.vector.scalar_tensor_tensor(args[th, d][:], y[:], 0.5, own_half, ALU.mult, ALU.add)
+            nc.vector.scalar_tensor_tensor(args[th, d][:], own_half, 2.0, y[:], ALU.mult, ALU.add)
 
         first_half = quantize_hidden(0, 2, codes_at=PICKED_AT + 64 - 4 * HALF)
         third_block = quantize_hidden(2, 3, codes_at=PICKED_AT + 64)
@@ -235,7 +235,7 @@ def tile_picked_yrbf_sum_p_kernel(
             th = first // 2
             arg = args[th, d][:, P * (first % 2) : P * (first % 2 + last - first)]
             value = sbuf("value" + name, [P, P * (last - first)], F32)
-            nc.scalar.activation(value[:], arg, ACT.Exp, bias=neg_half[:, d : d + 1])
+            nc.scalar.activation(value[:], arg, ACT.Exp, bias=neg_half[:, d : d + 1], scale=0.5)
             term = sbuf("term" + name, [P, P * (last - first)], F32)
             if D * th + d < POOL_TERMS:
                 nc.gpsimd.tensor_scalar(term[:], value[:], neg_alpha[:, d : d + 1], 0.0, ALU.mult, ALU.add)
@@ -248,13 +248,10 @@ def tile_picked_yrbf_sum_p_kernel(
                 block = term[:, P * s : P * (s + 1)]
                 nc.tensor.matmul(sums[first + s][:], block, ident[:], start=start, stop=stop, is_transpose=True)
 
-        terms = [weighted(d, 0, 2) for d in range(D)]
-        for d in (0, 1, 3):
-            add_transposed(terms[d], 0, d == 0, False)
-        add_transposed(weighted(0, 2, BLOCKS), 2, True, False)
-        add_transposed(terms[2], 0, False, True)
-        for d in range(1, D - 1):
-            add_transposed(weighted(d, 2, BLOCKS), 2, False, False)
+        for d in range(D):
+            add_transposed(weighted(d, 0, 2), 0, d == 0, d == D - 1)
+        for d in range(D - 1):
+            add_transposed(weighted(d, 2, BLOCKS), 2, d == 0, False)
         for tb in range(2, BLOCKS):
             add_transposed(weighted(D - 1, tb, tb + 1), tb, False, True)
 

@@ -81,9 +81,10 @@ def tile_picked_yrbf_sum_p_kernel(
 
         load_words(x_table[0], x_words[0])
         nc.sync.dma_start(offs_sb[:], offs)
-        nc.sync.dma_start(sv_sb[:], sv)
+        nc.sync.dma_start(own_cols[:], own.rearrange("(p s) o -> p (s o)", s=BLOCKS))
         load_scales(x_scale_table, x_scales, 0)
         load_weights(0)
+        nc.sync.dma_start(sv_sb[:], sv)
         e_rows = e_scale_table[E_ROWS.start : E_ROWS.stop : E_ROWS.step, :]
         nc.sync.dma_start(e_rows.bitcast(I32), e_scales[0].bitcast(I32))
         load_weights(1)
@@ -92,7 +93,12 @@ def tile_picked_yrbf_sum_p_kernel(
         load_words(x_table[1], x_words[1])
         load_words(e_table, e_words[0])
         make_identity(nc, ident[:])
-        nc.gpsimd.dma_start(own_cols[:], own.rearrange("(p s) o -> p (s o)", s=BLOCKS))
+
+        own_rows = sbuf("own_rows", [P, S], F32)
+        own_ps = psum.tile([P, BLOCKS, P], F32, name="own_ps", tag="bank3")
+        for s in range(BLOCKS):
+            nc.tensor.transpose(own_ps[:, s, :], own_cols[:, s : s + 1].to_broadcast([P, P]), ident[:])
+        nc.scalar.copy(own_rows[:].rearrange("m (p s) -> m p s", s=BLOCKS), own_ps[:].rearrange("m s p -> m p s"))
 
         x_scale = sbuf("x_scale", [P, S], U8)
         nc.vector.tensor_copy(x_scale[:], x_scale_table[:].indirect(offs_sb[:]))
@@ -111,36 +117,33 @@ def tile_picked_yrbf_sum_p_kernel(
         w_scale = [sbuf("w_scale%d" % o, [P, H], U8) for o in range(PASSES)]
         w_bf = [sbuf("w_bf%d" % o, [P, 2, 2 * H], BF16) for o in range(PASSES)]
 
-        def round_weights(o):
-            def views(c):
+        def round_weights(o, split):
+            def views(c, first, last):
                 return (
-                    w_bf[o][:, c, :].rearrange("p (r m j) -> p m j r", r=2, j=PACK),
-                    w_raw[o][:].rearrange("p j (m r) -> p m j r", r=PACK)[:, :, :, 2 * c : 2 * c + 2],
+                    w_bf[o][:, c, :].rearrange("p (r m j) -> p m j r", r=2, j=PACK)[:, first:last],
+                    w_raw[o][:].rearrange("p j (m r) -> p m j r", r=PACK)[:, first:last, :, 2 * c : 2 * c + 2],
                 )
 
-            nc.scalar.activation(*views(0), ACT.Copy)
-            nc.vector.tensor_copy(*views(1))
+            nc.scalar.activation(*views(0, 0, P), ACT.Copy)
+            if split:
+                nc.scalar.activation(*views(1, 0, split), ACT.Copy)
+            nc.vector.tensor_copy(*views(1, split, P))
 
         def quantize_weights(o, first, last):
             cols = slice(2 * P * first, 2 * P * last)
             values = w_bf[o][:, first:last, :].rearrange("p c n -> p (c n)")
             nc.vector.quantize_mx(out=w_codes[o][:, cols].bitcast(FP8X4), scales=w_scale[o][:, cols], in_=values)
 
-        round_weights(0)
+        round_weights(0, P // 4)
         e_scale_rows = sbuf("e_scale_rows", [P, D, P], U8, at=PICKED_AT)
         nc.vector.tensor_copy(e_scale_rows[:].rearrange("p d v -> p v d"), e_scale_table[:].indirect(sv_sb[:]))
         for q in range(QUADS):
             rows = e_scale_rows[E_ROWS[4 * q] : E_ROWS[4 * q + 3] + 1 : E_ROWS.step, :, :]
             nc.sync.dma_start(e_scale[32 * q : 32 * q + 4, :, :].bitcast(I32), rows.bitcast(I32))
-        quantize_weights(0, 0, 2)
+        quantize_weights(0, 0, 1)
+        quantize_weights(0, 1, 2)
 
-        own_rows = sbuf("own_rows", [P, S], F32)
-        own_ps = psum.tile([P, BLOCKS, P], F32, name="own_ps", tag="bank3")
-        for s in range(BLOCKS):
-            nc.tensor.transpose(own_ps[:, s, :], own_cols[:, s : s + 1].to_broadcast([P, P]), ident[:])
-        nc.scalar.copy(own_rows[:].rearrange("m (p s) -> m p s", s=BLOCKS), own_ps[:].rearrange("m s p -> m p s"))
-
-        round_weights(1)
+        round_weights(1, 0)
         quantize_weights(1, 1, 2)
         gather_x(1, 0, 1)
         quantize_weights(1, 0, 1)
@@ -184,9 +187,6 @@ def tile_picked_yrbf_sum_p_kernel(
             project(BLOCKS - 1, r, 0)
         second_pass(BLOCKS - 1)
 
-        e_codes = sbuf("e_codes", [P, D, P], U32)
-        nc.vector.tensor_copy(e_codes[:].rearrange("p d v -> p v d"), e_table[:].bitcast(U32).indirect(sv_sb[:]))
-
         def quantize_hidden(first, last, codes_at=None, scale_after=None):
             samples = P * (last - first)
             codes = sbuf("h_codes%d" % first, [P, samples], U32, at=codes_at)
@@ -194,6 +194,9 @@ def tile_picked_yrbf_sum_p_kernel(
             values = h_bf[first // 2][:, P * (first % 2) : P * (first % 2) + samples, :].rearrange("p t r -> p (t r)")
             nc.vector.quantize_mx(out=codes[:].bitcast(FP8X4), scales=scale[:], in_=values)
             return codes, scale
+
+        e_codes = sbuf("e_codes", [P, D, P], U32)
+        nc.vector.tensor_copy(e_codes[:].rearrange("p d v -> p v d"), e_table[:].bitcast(U32).indirect(sv_sb[:]))
 
         def product(th, d, pieces):
             y = psum.tile([P, HALF], F32, name="y%d%d" % (th, d), tag="bank%d" % Y_BANKS[d])

@@ -54,11 +54,13 @@ def tile_picked_yrbf_sum_p_kernel(
         x_table = [sbuf("x_table%d" % o, [P, T], I32) for o in range(PASSES)]
         e_table = sbuf("e_table", [P, W], I32)
         w_raw = [sbuf("w_raw0", [P, PACK, H], F32), sbuf("w_raw1", [P, PACK, H], F32, at=0)]
+        own_blocks = sbuf("own_blocks", [P, P], F32)
         own_cols = sbuf("own_cols", [P, BLOCKS], F32)
         ident = sbuf("ident", [P, P], F32)
         zero = sbuf("zero", [P, 1], F32)
         e_scale = sbuf("e_scale", [P, D, P], U8)
 
+        nc.vector.memset(own_blocks[:], 0.0)
         nc.vector.memset(x_scale_table[:].bitcast(I32), 0)
         nc.vector.memset(zero[:], 0.0)
         nc.vector.memset(e_scale_table[:].bitcast(I32), 0)
@@ -81,7 +83,7 @@ def tile_picked_yrbf_sum_p_kernel(
 
         load_words(x_table[0], x_words[0])
         nc.sync.dma_start(offs_sb[:], offs)
-        nc.sync.dma_start(own_cols[:], own.rearrange("(p s) o -> p (s o)", s=BLOCKS))
+        nc.sync.dma_start(own_blocks[0:BLOCKS, :], own.rearrange("(s c) o -> s (c o)", s=BLOCKS))
         load_scales(x_scale_table, x_scales, 0)
         load_weights(0)
         nc.sync.dma_start(sv_sb[:], sv)
@@ -94,11 +96,14 @@ def tile_picked_yrbf_sum_p_kernel(
         load_words(e_table, e_words[0])
         make_identity(nc, ident[:])
 
+        own_turned = psum.tile([P, P], F32, name="own_turned", tag="bank2")
+        nc.tensor.transpose(own_turned[:], own_blocks[:], ident[:])
+        nc.scalar.copy(own_cols[:], own_turned[:, 0:BLOCKS])
         own_rows = sbuf("own_rows", [P, S], F32)
         own_ps = psum.tile([P, BLOCKS, P], F32, name="own_ps", tag="bank3")
         for s in range(BLOCKS):
             nc.tensor.transpose(own_ps[:, s, :], own_cols[:, s : s + 1].to_broadcast([P, P]), ident[:])
-        nc.scalar.copy(own_rows[:].rearrange("m (p s) -> m p s", s=BLOCKS), own_ps[:].rearrange("m s p -> m p s"))
+        nc.scalar.copy(own_rows[:], own_ps[:].rearrange("m s p -> m (s p)"))
 
         x_scale = sbuf("x_scale", [P, S], U8)
         nc.vector.tensor_copy(x_scale[:], x_scale_table[:].indirect(offs_sb[:]))

@@ -23,12 +23,11 @@ PASSES = K // (P * PACK)
 BLOCKS = S // P
 HALF = S // 2
 POOL_TERMS = 2
-HALF_ROW, ALPHA_ROW = 16, 80
+HALF_ROW, ALPHA_ROW = 63, 127
 E_ROWS = range(32, 96, 4)
-PICKED_AT = 4 * PACK * H + 4 * HALF
+PICKED_AT = 4 * PACK * H
 Y_BANKS = (4, 5, 6, 7)
 SUM_BANKS = (3, 1, 2, 0)
-ROW_SPLIT = 1536
 FLOPS = 2 * K * H * S + 2 * H * S * U
 
 
@@ -60,13 +59,14 @@ def tile_picked_yrbf_sum_p_kernel(
         zero = sbuf("zero", [P, 1], F32)
         e_scale = sbuf("e_scale", [P, D, P], U8)
 
-        nc.vector.memset(own_blocks[:], 0.0)
-        nc.vector.memset(x_scale_table[:].bitcast(I32), 0)
         nc.vector.memset(zero[:], 0.0)
+        nc.vector.memset(x_scale_table[:].bitcast(I32), 0)
+        nc.vector.memset(own_blocks[:], 0.0)
         nc.vector.memset(e_scale_table[:].bitcast(I32), 0)
-        nc.vector.memset(row_table[:, 0:ROW_SPLIT], 0.0)
+        nc.vector.memset(row_table[0:HALF_ROW, :], 0.0)
         nc.vector.memset(e_scale[:].bitcast(I32), 0)
-        nc.scalar.activation(row_table[:, ROW_SPLIT:W], zero[:].to_broadcast([P, W - ROW_SPLIT]), ACT.Copy)
+        upper = slice(HALF_ROW + 1, ALPHA_ROW)
+        nc.scalar.activation(row_table[upper, :], zero[upper, :].to_broadcast([ALPHA_ROW - HALF_ROW - 1, W]), ACT.Copy)
 
         def load_words(tile, words):
             nc.sync.dma_start(tile[:], words.rearrange("p c j -> p (c j)").bitcast(I32))
@@ -81,29 +81,27 @@ def tile_picked_yrbf_sum_p_kernel(
             rows = w1[P * PACK * o : P * PACK * (o + 1), :].rearrange("(p j) c -> p (j c)", j=PACK)
             nc.sync.dma_start(w_raw[o][:].rearrange("p j c -> p (j c)"), rows)
 
-        load_words(x_table[0], x_words[0])
         nc.sync.dma_start(offs_sb[:], offs)
-        nc.sync.dma_start(own_blocks[0:BLOCKS, :], own.rearrange("(s c) o -> s (c o)", s=BLOCKS))
-        load_scales(x_scale_table, x_scales, 0)
-        load_weights(0)
         nc.sync.dma_start(sv_sb[:], sv)
+        load_words(x_table[0], x_words[0])
+        load_scales(x_scale_table, x_scales, 0)
+        nc.sync.dma_start(row_table[HALF_ROW : HALF_ROW + 1, :], half[0:1, :])
+        nc.sync.dma_start(row_table[ALPHA_ROW : ALPHA_ROW + 1, :], alpha[0:1, :])
+        load_weights(0)
+        nc.sync.dma_start(own_blocks[0:BLOCKS, :], own.rearrange("(s c) o -> s (c o)", s=BLOCKS))
         e_rows = e_scale_table[E_ROWS.start : E_ROWS.stop : E_ROWS.step, :]
         nc.sync.dma_start(e_rows.bitcast(I32), e_scales[0].bitcast(I32))
         load_weights(1)
-        nc.sync.dma_start(row_table[HALF_ROW : HALF_ROW + 1, :], half[0:1, :])
-        nc.sync.dma_start(row_table[ALPHA_ROW : ALPHA_ROW + 1, :], alpha[0:1, :])
         load_words(x_table[1], x_words[1])
         load_words(e_table, e_words[0])
         make_identity(nc, ident[:])
 
-        own_turned = psum.tile([P, P], F32, name="own_turned", tag="bank2")
-        nc.tensor.transpose(own_turned[:], own_blocks[:], ident[:])
-        nc.scalar.copy(own_cols[:], own_turned[:, 0:BLOCKS])
-        own_rows = sbuf("own_rows", [P, S], F32)
-        own_ps = psum.tile([P, BLOCKS, P], F32, name="own_ps", tag="bank3")
-        for s in range(BLOCKS):
-            nc.tensor.transpose(own_ps[:, s, :], own_cols[:, s : s + 1].to_broadcast([P, P]), ident[:])
-        nc.scalar.copy(own_rows[:], own_ps[:].rearrange("m s p -> m (s p)"))
+        rows_picked = sbuf("rows_picked", [P, U], F32)
+        nc.scalar.activation(rows_picked[:], row_table[:].indirect(sv_sb[:]), ACT.Copy, scale=-1.0)
+        neg_half = sbuf("neg_half", [P, D], F32)
+        neg_alpha = sbuf("neg_alpha", [P, D], F32)
+        for cols, row in ((neg_half, HALF_ROW), (neg_alpha, ALPHA_ROW)):
+            nc.sync.dma_start(cols[:], rows_picked[row : row + 1, :].rearrange("o (v d) -> o v d", d=D))
 
         x_scale = sbuf("x_scale", [P, S], U8)
         nc.vector.tensor_copy(x_scale[:], x_scale_table[:].indirect(offs_sb[:]))
@@ -140,6 +138,15 @@ def tile_picked_yrbf_sum_p_kernel(
             nc.vector.quantize_mx(out=w_codes[o][:, cols].bitcast(FP8X4), scales=w_scale[o][:, cols], in_=values)
 
         round_weights(0, P // 4)
+        own_turned = psum.tile([P, P], F32, name="own_turned", tag="bank2")
+        nc.tensor.transpose(own_turned[:], own_blocks[:], ident[:])
+        nc.vector.tensor_copy(own_cols[:], own_turned[:, 0:BLOCKS])
+        own_rows = sbuf("own_rows", [P, S], F32)
+        own_ps = psum.tile([P, BLOCKS, P], F32, name="own_ps", tag="bank3")
+        for s in range(BLOCKS):
+            nc.tensor.transpose(own_ps[:, s, :], own_cols[:, s : s + 1].to_broadcast([P, P]), ident[:])
+        nc.scalar.copy(own_rows[:], own_ps[:].rearrange("m s p -> m (s p)"))
+
         e_scale_rows = sbuf("e_scale_rows", [P, D, P], U8, at=PICKED_AT)
         nc.vector.tensor_copy(e_scale_rows[:].rearrange("p d v -> p v d"), e_scale_table[:].indirect(sv_sb[:]))
         for q in range(QUADS):
@@ -154,16 +161,10 @@ def tile_picked_yrbf_sum_p_kernel(
         quantize_weights(1, 0, 1)
         gather_x(1, 1, 2, at=4 * S)
         gather_x(1, 2, BLOCKS, at=8 * S)
-        rows_picked = sbuf("rows_picked", [P, U], F32, at=0)
-        nc.scalar.activation(rows_picked[:], row_table[:].indirect(sv_sb[:]), ACT.Copy, scale=-1.0)
-        neg_half = sbuf("neg_half", [P, D], F32)
-        neg_alpha = sbuf("neg_alpha", [P, D], F32)
-        for cols, row in ((neg_half, HALF_ROW), (neg_alpha, ALPHA_ROW)):
-            nc.sync.dma_start(cols[:], rows_picked[row : row + 1, :].rearrange("o (v d) -> o v d", d=D))
 
-        h_ps = [psum.tile([P, PACK, P], F32, name="h_ps%d" % tb, tag="bank%d" % (tb % 3)) for tb in range(BLOCKS)]
+        h_ps = [psum.tile([P, PACK, P], F32, name="h_ps%d" % tb, tag="bank%d" % tb) for tb in range(BLOCKS)]
 
-        def project(tb, r, o):
+        def project(tb, r, o, stop=False):
             samples = slice(P * tb, P * (tb + 1))
             hidden = slice(P * r, P * (r + 1))
             nc.tensor.matmul_mx(
@@ -173,29 +174,27 @@ def tile_picked_yrbf_sum_p_kernel(
                 rhs=x_codes[o, tb].bitcast(FP8X4),
                 rhs_scale=x_scale[4 * o : P, samples],
                 start=(o, r) == (0, 0),
-                stop=(o, r) == (PASSES - 1, 1),
+                stop=stop,
             )
 
         h_bf = [sbuf("h_bf%d" % th, [P, HALF, PACK], BF16) for th in range(2)]
 
         def second_pass(tb):
-            for r in (2, 3, 0, 1):
-                project(tb, r, 1)
+            order = (2, 3, 0, 1) if tb == 0 else (0, 1, 2, 3)
+            for r in order:
+                project(tb, r, 1, r == order[-1])
             nc.scalar.copy(h_bf[tb // 2][:, P * (tb % 2) : P * (tb % 2 + 1), :], h_ps[tb][:].rearrange("p r t -> p t r"))
 
-        for tb in range(BLOCKS - 1):
+        for tb in range(BLOCKS):
             for r in range(PACK):
                 project(tb, r, 0)
-        for tb in range(BLOCKS - 1):
+        for tb in range(BLOCKS):
             second_pass(tb)
-        for r in range(PACK):
-            project(BLOCKS - 1, r, 0)
-        second_pass(BLOCKS - 1)
 
-        def quantize_hidden(first, last, codes_at=None, scale_after=None):
+        def quantize_hidden(first, last):
             samples = P * (last - first)
-            codes = sbuf("h_codes%d" % first, [P, samples], U32, at=codes_at)
-            scale = sbuf("h_scale%d" % first, [P, samples], U8, after=scale_after)
+            codes = sbuf("h_codes%d" % first, [P, samples], U32)
+            scale = sbuf("h_scale%d" % first, [P, samples], U8, at=PICKED_AT + P * first)
             values = h_bf[first // 2][:, P * (first % 2) : P * (first % 2) + samples, :].rearrange("p t r -> p (t r)")
             nc.vector.quantize_mx(out=codes[:].bitcast(FP8X4), scales=scale[:], in_=values)
             return codes, scale
@@ -226,13 +225,11 @@ def tile_picked_yrbf_sum_p_kernel(
             own_half = own_rows[:, HALF * th : HALF * (th + 1)]
             nc.vector.scalar_tensor_tensor(args[th, d][:], own_half, 2.0, y[:], ALU.mult, ALU.add)
 
-        first_half = quantize_hidden(0, 2, codes_at=PICKED_AT + 64 - 4 * HALF)
-        third_block = quantize_hidden(2, 3, codes_at=PICKED_AT + 64)
-        first_y = [product(0, d, [first_half]) for d in range(D)]
-        add_own(0, 0, first_y[0])
-        last_block = quantize_hidden(3, 4, scale_after="h_scale0")
-        for d in range(1, D):
-            add_own(0, d, first_y[d])
+        first_half = quantize_hidden(0, 2)
+        third_block = quantize_hidden(2, 3)
+        last_block = quantize_hidden(3, 4)
+        for d in range(D):
+            add_own(0, d, product(0, d, [first_half]))
         for d in range(D):
             add_own(1, d, product(1, d, [third_block, last_block]))
 

@@ -113,8 +113,9 @@ def tile_picked_yrbf_sum_p_kernel(
             nc.vector.tensor_copy(codes[:], x_table[o][:].bitcast(U32).indirect(entries))
             for tb in range(first, last):
                 x_codes[o, tb] = codes[:, P * (tb - first) : P * (tb - first + 1)]
+            return codes
 
-        gather_x(0, 0, BLOCKS)
+        x_first = gather_x(0, 0, BLOCKS)
 
         w_codes = [sbuf("w_codes%d" % o, [P, H], U32) for o in range(PASSES)]
         w_scale = [sbuf("w_scale%d" % o, [P, H], U8) for o in range(PASSES)]
@@ -232,6 +233,17 @@ def tile_picked_yrbf_sum_p_kernel(
             add_own(0, d, product(0, d, [first_half]))
         for d in range(D):
             add_own(1, d, product(1, d, [third_block, last_block]))
+
+        unread = psum.tile([P, S], F32, name="unread", tag="bank%d" % Y_BANKS[0])
+        nc.tensor.matmul_mx(
+            out=unread[:],
+            lhsT=w_codes[0][:, 0:P].bitcast(FP8X4),
+            lhsT_scale=w_scale[0][:, 0:P],
+            rhs=x_first[:].bitcast(FP8X4),
+            rhs_scale=x_scale[:],
+            start=True,
+            stop=True,
+        )
 
         sums = [psum.tile([P, P], F32, name="sum%d" % tb, tag="bank%d" % SUM_BANKS[tb]) for tb in range(BLOCKS)]
 

@@ -26,6 +26,12 @@ POOL_TERMS = 2
 HALF_ROW, ALPHA_ROW = 63, 127
 E_ROWS = range(32, 96, 4)
 PICKED_AT = 4 * PACK * H
+LAP = 64
+E_WORDS_AT = PICKED_AT + U
+X_SCALES_AT = E_WORDS_AT + 4 * W - LAP
+X_FIRST_AT = X_SCALES_AT + T
+X_SECOND_AT = X_FIRST_AT + 4 * S
+E_SCALES_AT = X_SECOND_AT + 4 * T
 Y_BANKS = (4, 5, 6, 7)
 SUM_BANKS = (3, 1, 2, 0)
 FLOPS = 2 * K * H * S + 2 * H * S * U
@@ -47,23 +53,25 @@ def tile_picked_yrbf_sum_p_kernel(
 
         offs_sb = keep.tile([P, S // LIST_ROWS], U16, name="offs_sb")
         sv_sb = keep.tile([P, U // LIST_ROWS], U16, name="sv_sb")
-        x_scale_table = sbuf("x_scale_table", [P, T], U8)
-        e_scale_table = sbuf("e_scale_table", [P, W], U8)
+        x_scale_table = sbuf("x_scale_table", [P, T + 4 * S + LAP], U8, at=X_SCALES_AT)
+        e_scale_table = sbuf("e_scale_table", [P, W], U8, at=E_SCALES_AT)
         row_table = sbuf("row_table", [P, W], F32)
-        x_table = [sbuf("x_table%d" % o, [P, T], I32) for o in range(PASSES)]
-        e_table = sbuf("e_table", [P, W], I32)
+        x_table = [sbuf("x_table0", [P, T], I32), sbuf("x_table1", [P, T], I32, at=X_SECOND_AT)]
+        e_table = sbuf("e_table", [P, W], I32, at=E_WORDS_AT)
         w_raw = [sbuf("w_raw0", [P, PACK, H], F32), sbuf("w_raw1", [P, PACK, H], F32, at=0)]
         own_blocks = sbuf("own_blocks", [P, P], F32)
         own_cols = sbuf("own_cols", [P, BLOCKS], F32)
         ident = sbuf("ident", [P, P], F32)
         zero = sbuf("zero", [P, 1], F32)
         e_scale = sbuf("e_scale", [P, D, P], U8)
+        x_scale = sbuf("x_scale", [P, PASSES, S], U8)
 
-        nc.vector.memset(zero[:], 0.0)
-        nc.vector.memset(x_scale_table[:].bitcast(I32), 0)
-        nc.vector.memset(own_blocks[:], 0.0)
+        nc.vector.memset(x_scale_table[:, 0:T].bitcast(I32), 0)
         nc.vector.memset(e_scale_table[:].bitcast(I32), 0)
+        nc.gpsimd.memset(zero[:], 0.0)
+        nc.vector.memset(own_blocks[:], 0.0)
         nc.vector.memset(row_table[0:HALF_ROW, :], 0.0)
+        nc.vector.memset(x_scale[:].rearrange("p o s -> p (o s)").bitcast(I32), 0)
         nc.vector.memset(e_scale[:].bitcast(I32), 0)
         upper = slice(HALF_ROW + 1, ALPHA_ROW)
         nc.scalar.activation(row_table[upper, :], zero[upper, :].to_broadcast([ALPHA_ROW - HALF_ROW - 1, W]), ACT.Copy)
@@ -71,40 +79,45 @@ def tile_picked_yrbf_sum_p_kernel(
         def load_words(tile, words):
             nc.sync.dma_start(tile[:], words.rearrange("p c j -> p (c j)").bitcast(I32))
 
-        def load_scales(tile, scales, first):
-            passes = scales.shape[0]
-            for q in range(QUADS):
-                rows = tile[32 * q + first : 32 * q + first + 4 * passes, :]
-                nc.sync.dma_start(rows.bitcast(I32), scales[:, 4 * q : 4 * q + 4, :].bitcast(I32))
-
         def load_weights(o):
             rows = w1[P * PACK * o : P * PACK * (o + 1), :].rearrange("(p j) c -> p (j c)", j=PACK)
             nc.sync.dma_start(w_raw[o][:].rearrange("p j c -> p (j c)"), rows)
 
         nc.sync.dma_start(offs_sb[:], offs)
-        nc.sync.dma_start(sv_sb[:], sv)
         load_words(x_table[0], x_words[0])
-        load_scales(x_scale_table, x_scales, 0)
+        nc.sync.dma_start(sv_sb[:], sv)
+        x_rows = x_scale_table[0:P:4, 0:T]
+        nc.sync.dma_start(x_rows.bitcast(I32), x_scales.rearrange("o b c -> b o c").bitcast(I32))
+        e_rows = e_scale_table[E_ROWS.start : E_ROWS.stop : E_ROWS.step, :]
+        nc.sync.dma_start(e_rows.bitcast(I32), e_scales[0].bitcast(I32))
         nc.sync.dma_start(row_table[HALF_ROW : HALF_ROW + 1, :], half[0:1, :])
         nc.sync.dma_start(row_table[ALPHA_ROW : ALPHA_ROW + 1, :], alpha[0:1, :])
         load_weights(0)
         nc.sync.dma_start(own_blocks[0:BLOCKS, :], own.rearrange("(s c) o -> s (c o)", s=BLOCKS))
-        e_rows = e_scale_table[E_ROWS.start : E_ROWS.stop : E_ROWS.step, :]
-        nc.sync.dma_start(e_rows.bitcast(I32), e_scales[0].bitcast(I32))
         load_weights(1)
+
+        x_scale_rows = sbuf("x_scale_rows", [P, S], U8)
+        nc.vector.tensor_copy(x_scale_rows[:], x_scale_table[:, 0:T].indirect(offs_sb[:]))
+        for q in range(QUADS):
+            rows = x_scale_rows[32 * q : 32 * (q + 1) : 4, :]
+            nc.sync.dma_start(x_scale[32 * q : 32 * q + 4, :, :].bitcast(I32), rows.bitcast(I32))
         load_words(x_table[1], x_words[1])
         load_words(e_table, e_words[0])
+
+        e_scale_rows = sbuf("e_scale_rows", [P, D, P], U8, at=PICKED_AT)
+        nc.vector.tensor_copy(e_scale_rows[:].rearrange("p d v -> p v d"), e_scale_table[:].indirect(sv_sb[:]))
+        for q in range(QUADS):
+            rows = e_scale_rows[E_ROWS[4 * q] : E_ROWS[4 * q + 3] + 1 : E_ROWS.step, :, :]
+            nc.sync.dma_start(e_scale[32 * q : 32 * q + 4, :, :].bitcast(I32), rows.bitcast(I32))
         make_identity(nc, ident[:])
 
         rows_picked = sbuf("rows_picked", [P, U], F32)
         nc.scalar.activation(rows_picked[:], row_table[:].indirect(sv_sb[:]), ACT.Copy, scale=-1.0)
-        neg_half = sbuf("neg_half", [P, D], F32)
-        neg_alpha = sbuf("neg_alpha", [P, D], F32)
+        neg_half = sbuf("neg_half", [P, D], F32, at=E_SCALES_AT + 2 * LAP)
+        neg_alpha = sbuf("neg_alpha", [P, D], F32, at=E_SCALES_AT + 3 * LAP)
         for cols, row in ((neg_half, HALF_ROW), (neg_alpha, ALPHA_ROW)):
             nc.sync.dma_start(cols[:], rows_picked[row : row + 1, :].rearrange("o (v d) -> o v d", d=D))
 
-        x_scale = sbuf("x_scale", [P, S], U8)
-        nc.vector.tensor_copy(x_scale[:], x_scale_table[:].indirect(offs_sb[:]))
         x_codes = {}
 
         def gather_x(o, first, last, at=None):
@@ -115,7 +128,7 @@ def tile_picked_yrbf_sum_p_kernel(
                 x_codes[o, tb] = codes[:, P * (tb - first) : P * (tb - first + 1)]
             return codes
 
-        x_first = gather_x(0, 0, BLOCKS)
+        x_first = gather_x(0, 0, BLOCKS, at=X_FIRST_AT)
 
         w_codes = [sbuf("w_codes%d" % o, [P, H], U32) for o in range(PASSES)]
         w_scale = [sbuf("w_scale%d" % o, [P, H], U8) for o in range(PASSES)]
@@ -139,24 +152,19 @@ def tile_picked_yrbf_sum_p_kernel(
             nc.vector.quantize_mx(out=w_codes[o][:, cols].bitcast(FP8X4), scales=w_scale[o][:, cols], in_=values)
 
         round_weights(0, P // 4)
-        own_turned = psum.tile([P, P], F32, name="own_turned", tag="bank2")
+        own_turned = psum.tile([P, P], F32, name="own_turned", tag="bank6")
         nc.tensor.transpose(own_turned[:], own_blocks[:], ident[:])
-        nc.vector.tensor_copy(own_cols[:], own_turned[:, 0:BLOCKS])
-        own_rows = sbuf("own_rows", [P, S], F32)
-        own_ps = psum.tile([P, BLOCKS, P], F32, name="own_ps", tag="bank3")
+        nc.scalar.copy(own_cols[:], own_turned[:, 0:BLOCKS])
+        own_rows = sbuf("own_rows", [P, S], F32, at=0)
+        own_ps = psum.tile([P, BLOCKS, P], F32, name="own_ps", tag="bank7")
         for s in range(BLOCKS):
             nc.tensor.transpose(own_ps[:, s, :], own_cols[:, s : s + 1].to_broadcast([P, P]), ident[:])
-        nc.scalar.copy(own_rows[:], own_ps[:].rearrange("m s p -> m (s p)"))
 
-        e_scale_rows = sbuf("e_scale_rows", [P, D, P], U8, at=PICKED_AT)
-        nc.vector.tensor_copy(e_scale_rows[:].rearrange("p d v -> p v d"), e_scale_table[:].indirect(sv_sb[:]))
-        for q in range(QUADS):
-            rows = e_scale_rows[E_ROWS[4 * q] : E_ROWS[4 * q + 3] + 1 : E_ROWS.step, :, :]
-            nc.sync.dma_start(e_scale[32 * q : 32 * q + 4, :, :].bitcast(I32), rows.bitcast(I32))
         quantize_weights(0, 0, 1)
         quantize_weights(0, 1, 2)
 
         round_weights(1, 0)
+        nc.scalar.copy(own_rows[:], own_ps[:].rearrange("m s p -> m (s p)"))
         quantize_weights(1, 1, 2)
         gather_x(1, 0, 1)
         quantize_weights(1, 0, 1)
@@ -173,7 +181,7 @@ def tile_picked_yrbf_sum_p_kernel(
                 lhsT=w_codes[o][:, hidden].bitcast(FP8X4),
                 lhsT_scale=w_scale[o][:, hidden],
                 rhs=x_codes[o, tb].bitcast(FP8X4),
-                rhs_scale=x_scale[4 * o : P, samples],
+                rhs_scale=x_scale[:, o, samples],
                 start=(o, r) == (0, 0),
                 stop=stop,
             )
@@ -240,7 +248,7 @@ def tile_picked_yrbf_sum_p_kernel(
             lhsT=w_codes[0][:, 0:P].bitcast(FP8X4),
             lhsT_scale=w_scale[0][:, 0:P],
             rhs=x_first[:].bitcast(FP8X4),
-            rhs_scale=x_scale[:],
+            rhs_scale=x_scale[:, 0, :],
             start=True,
             stop=True,
         )
@@ -276,9 +284,7 @@ def tile_picked_yrbf_sum_p_kernel(
         for tb in range(2):
             nc.scalar.activation(first_out[:, tb, :], sums[tb][:], ACT.Copy, scale=-1.0)
         nc.sync.dma_start(out[0:HALF, :].rearrange("(s p) v -> p s v", s=2), first_out[:])
-        third_out = sbuf("third_out", [P, P], F32)
-        nc.scalar.activation(third_out[:], sums[2][:], ACT.Copy, scale=-1.0)
-        nc.sync.dma_start(out[2 * P : 3 * P, :], third_out[:])
-        last_out = sbuf("last_out", [P, P], F32)
-        nc.vector.tensor_scalar(last_out[:], sums[3][:], -1.0, None, ALU.mult)
-        nc.sync.dma_start(out[3 * P : S, :], last_out[:])
+        last_out = sbuf("last_out", [P, 2, P], F32)
+        nc.scalar.activation(last_out[:, 0, :], sums[2][:], ACT.Copy, scale=-1.0)
+        nc.vector.tensor_scalar(last_out[:, 1, :], sums[3][:], -1.0, None, ALU.mult)
+        nc.sync.dma_start(out[HALF:S, :].rearrange("(s p) v -> p s v", s=2), last_out[:])

@@ -24,8 +24,9 @@ BLOCKS = S // P
 HALF = S // 2
 POOL_TERMS = 2
 HALF_ROW, ALPHA_ROW = 63, 127
-E_ROWS = range(32, 96, 4)
+E_ROWS = range(0, P, 8)
 PICKED_AT = 4 * PACK * H
+X_PLANE = 4
 LAP = 64
 E_WORDS_AT = PICKED_AT + U
 X_SCALES_AT = E_WORDS_AT + 4 * W - LAP
@@ -83,11 +84,11 @@ def tile_picked_yrbf_sum_p_kernel(
             rows = w1[P * PACK * o : P * PACK * (o + 1), :].rearrange("(p j) c -> p (j c)", j=PACK)
             nc.sync.dma_start(w_raw[o][:].rearrange("p j c -> p (j c)"), rows)
 
-        nc.sync.dma_start(offs_sb[:], offs)
         load_words(x_table[0], x_words[0])
-        nc.sync.dma_start(sv_sb[:], sv)
+        nc.sync.dma_start(offs_sb[:], offs)
         x_rows = x_scale_table[0:P:4, 0:T]
         nc.sync.dma_start(x_rows.bitcast(I32), x_scales.rearrange("o b c -> b o c").bitcast(I32))
+        nc.sync.dma_start(sv_sb[:], sv)
         e_rows = e_scale_table[E_ROWS.start : E_ROWS.stop : E_ROWS.step, :]
         nc.sync.dma_start(e_rows.bitcast(I32), e_scales[0].bitcast(I32))
         nc.sync.dma_start(row_table[HALF_ROW : HALF_ROW + 1, :], half[0:1, :])
@@ -100,7 +101,7 @@ def tile_picked_yrbf_sum_p_kernel(
         nc.vector.tensor_copy(x_scale_rows[:], x_scale_table[:, 0:T].indirect(offs_sb[:]))
         for q in range(QUADS):
             rows = x_scale_rows[32 * q : 32 * (q + 1) : 4, :]
-            nc.sync.dma_start(x_scale[32 * q : 32 * q + 4, :, :].bitcast(I32), rows.bitcast(I32))
+            nc.sync.dma_start(x_scale[32 * q + X_PLANE : 32 * q + X_PLANE + 4, :, :].bitcast(I32), rows.bitcast(I32))
         load_words(x_table[1], x_words[1])
         load_words(e_table, e_words[0])
 
@@ -181,7 +182,7 @@ def tile_picked_yrbf_sum_p_kernel(
                 lhsT=w_codes[o][:, hidden].bitcast(FP8X4),
                 lhsT_scale=w_scale[o][:, hidden],
                 rhs=x_codes[o, tb].bitcast(FP8X4),
-                rhs_scale=x_scale[:, o, samples],
+                rhs_scale=x_scale[X_PLANE:P, o, samples],
                 start=(o, r) == (0, 0),
                 stop=stop,
             )
@@ -248,7 +249,7 @@ def tile_picked_yrbf_sum_p_kernel(
             lhsT=w_codes[0][:, 0:P].bitcast(FP8X4),
             lhsT_scale=w_scale[0][:, 0:P],
             rhs=x_first[:].bitcast(FP8X4),
-            rhs_scale=x_scale[:, 0, :],
+            rhs_scale=x_scale[X_PLANE:P, 0, :],
             start=True,
             stop=True,
         )

from contextlib import ExitStack

import concourse.mybir as mybir
from concourse.masks import make_identity

F32 = mybir.dt.float32
BF16 = mybir.dt.bfloat16
I32 = mybir.dt.int32
U32 = mybir.dt.uint32
U16 = mybir.dt.uint16
U8 = mybir.dt.uint8
FP8X4 = mybir.dt.float8_e4m3fn_x4
ALU = mybir.AluOpType
ACT = mybir.ActivationFunctionType

P = 128
PACK = 4
QUADS = 4
LIST_ROWS = 16
K, T, S = 1024, 1024, 512
H, W, U, D = 512, 2048, 512, 4
PASSES = K // (P * PACK)
BLOCKS = S // P
HALF = S // 2
POOL_TERMS = 2
HALF_ROW, ALPHA_ROW = 63, 127
E_ROWS = range(0, P, 8)
PICKED_AT = 4 * PACK * H
X_PLANE = 4
LAP = 64
E_WORDS_AT = PICKED_AT + U
X_SCALES_AT = E_WORDS_AT + 4 * W - LAP
X_FIRST_AT = X_SCALES_AT + T
X_SECOND_AT = X_FIRST_AT + 4 * S
E_SCALES_AT = X_SECOND_AT + 4 * T
Y_BANKS = (4, 5, 6, 7)
SUM_BANKS = (3, 1, 2, 0)
FLOPS = 2 * K * H * S + 2 * H * S * U


def tile_picked_yrbf_sum_p_kernel(
    tc, x_words, x_scales, w1, e_words, e_scales, half, own, alpha, offs, sv, out
):
    nc = tc.nc
    with ExitStack() as ctx:
        keep = ctx.enter_context(tc.tile_pool(name="keep", bufs=1))
        psum = ctx.enter_context(tc.psum_pool(name="psum", bufs=1))
        shared = ctx.enter_context(tc.tile_pool(name="shared", bufs=1))

        def sbuf(name, shape, dtype, after=None, at=None):
            if at is not None:
                return shared.tile(shape, dtype, name=name, offset=at, align_bytes=64)
            return keep.tile(shape, dtype, name=name, tag=after or name, align_bytes=64)

        offs_sb = keep.tile([P, S // LIST_ROWS], U16, name="offs_sb")
        sv_sb = keep.tile([P, U // LIST_ROWS], U16, name="sv_sb")
        x_scale_table = sbuf("x_scale_table", [P, T + 4 * S + LAP], U8, at=X_SCALES_AT)
        e_scale_table = sbuf("e_scale_table", [P, W], U8, at=E_SCALES_AT)
        row_table = sbuf("row_table", [P, W], F32)
        x_table = [sbuf("x_table0", [P, T], I32), sbuf("x_table1", [P, T], I32, at=X_SECOND_AT)]
        e_table = sbuf("e_table", [P, W], I32, at=E_WORDS_AT)
        w_raw = [sbuf("w_raw0", [P, PACK, H], F32), sbuf("w_raw1", [P, PACK, H], F32, at=0)]
        own_blocks = sbuf("own_blocks", [P, P], F32)
        own_cols = sbuf("own_cols", [P, BLOCKS], F32)
        ident = sbuf("ident", [P, P], F32)
        zero = sbuf("zero", [P, 1], F32)
        e_scale = sbuf("e_scale", [P, D, P], U8)
        x_scale = sbuf("x_scale", [P, PASSES, S], U8)

        nc.vector.memset(x_scale_table[:, 0:T].bitcast(I32), 0)
        nc.vector.memset(e_scale_table[:].bitcast(I32), 0)
        nc.gpsimd.memset(zero[:], 0.0)
        nc.vector.memset(own_blocks[:], 0.0)
        nc.vector.memset(row_table[0:HALF_ROW, :], 0.0)
        nc.vector.memset(x_scale[:].rearrange("p o s -> p (o s)").bitcast(I32), 0)
        nc.vector.memset(e_scale[:].bitcast(I32), 0)
        upper = slice(HALF_ROW + 1, ALPHA_ROW)
        nc.scalar.activation(row_table[upper, :], zero[upper, :].to_broadcast([ALPHA_ROW - HALF_ROW - 1, W]), ACT.Copy)

        def load_words(tile, words):
            nc.sync.dma_start(tile[:], words.rearrange("p c j -> p (c j)").bitcast(I32))

        def load_weights(o):
            rows = w1[P * PACK * o : P * PACK * (o + 1), :].rearrange("(p j) c -> p (j c)", j=PACK)
            nc.sync.dma_start(w_raw[o][:].rearrange("p j c -> p (j c)"), rows)

        load_words(x_table[0], x_words[0])
        nc.sync.dma_start(offs_sb[:], offs)
        x_rows = x_scale_table[0:P:4, 0:T]
        nc.sync.dma_start(x_rows.bitcast(I32), x_scales.rearrange("o b c -> b o c").bitcast(I32))
        nc.sync.dma_start(sv_sb[:], sv)
        e_rows = e_scale_table[E_ROWS.start : E_ROWS.stop : E_ROWS.step, :]
        nc.sync.dma_start(e_rows.bitcast(I32), e_scales[0].bitcast(I32))
        nc.sync.dma_start(row_table[HALF_ROW : HALF_ROW + 1, :], half[0:1, :])
        nc.sync.dma_start(row_table[ALPHA_ROW : ALPHA_ROW + 1, :], alpha[0:1, :])
        load_weights(0)
        nc.sync.dma_start(own_blocks[0:BLOCKS, :], own.rearrange("(s c) o -> s (c o)", s=BLOCKS))
        load_weights(1)

        x_scale_rows = sbuf("x_scale_rows", [P, S], U8)
        nc.vector.tensor_copy(x_scale_rows[:], x_scale_table[:, 0:T].indirect(offs_sb[:]))
        for q in range(QUADS):
            rows = x_scale_rows[32 * q : 32 * (q + 1) : 4, :]
            nc.sync.dma_start(x_scale[32 * q + X_PLANE : 32 * q + X_PLANE + 4, :, :].bitcast(I32), rows.bitcast(I32))
        load_words(x_table[1], x_words[1])
        load_words(e_table, e_words[0])

        e_scale_rows = sbuf("e_scale_rows", [P, D, P], U8, at=PICKED_AT)
        nc.vector.tensor_copy(e_scale_rows[:].rearrange("p d v -> p v d"), e_scale_table[:].indirect(sv_sb[:]))
        for q in range(QUADS):
            rows = e_scale_rows[E_ROWS[4 * q] : E_ROWS[4 * q + 3] + 1 : E_ROWS.step, :, :]
            nc.sync.dma_start(e_scale[32 * q : 32 * q + 4, :, :].bitcast(I32), rows.bitcast(I32))
        make_identity(nc, ident[:])

        rows_picked = sbuf("rows_picked", [P, U], F32)
        nc.scalar.activation(rows_picked[:], row_table[:].indirect(sv_sb[:]), ACT.Copy, scale=-1.0)
        neg_half = sbuf("neg_half", [P, D], F32, at=E_SCALES_AT + 2 * LAP)
        neg_alpha = sbuf("neg_alpha", [P, D], F32, at=E_SCALES_AT + 3 * LAP)
        for cols, row in ((neg_half, HALF_ROW), (neg_alpha, ALPHA_ROW)):
            nc.sync.dma_start(cols[:], rows_picked[row : row + 1, :].rearrange("o (v d) -> o v d", d=D))

        x_codes = {}

        def gather_x(o, first, last, at=None):
            codes = sbuf("x_codes%d%d" % (o, first), [P, P * (last - first)], U32, at=at)
            entries = offs_sb[:, first * P // LIST_ROWS : last * P // LIST_ROWS]
            nc.vector.tensor_copy(codes[:], x_table[o][:].bitcast(U32).indirect(entries))
            for tb in range(first, last):
                x_codes[o, tb] = codes[:, P * (tb - first) : P * (tb - first + 1)]
            return codes

        x_first = gather_x(0, 0, BLOCKS, at=X_FIRST_AT)

        w_codes = [sbuf("w_codes%d" % o, [P, H], U32) for o in range(PASSES)]
        w_scale = [sbuf("w_scale%d" % o, [P, H], U8) for o in range(PASSES)]
        w_bf = [sbuf("w_bf%d" % o, [P, 2, 2 * H], BF16) for o in range(PASSES)]

        def round_weights(o, split):
            def views(c, first, last):
                return (
                    w_bf[o][:, c, :].rearrange("p (r m j) -> p m j r", r=2, j=PACK)[:, first:last],
                    w_raw[o][:].rearrange("p j (m r) -> p m j r", r=PACK)[:, first:last, :, 2 * c : 2 * c + 2],
                )

            nc.scalar.activation(*views(0, 0, P), ACT.Copy)
            if split:
                nc.scalar.activation(*views(1, 0, split), ACT.Copy)
            nc.vector.tensor_copy(*views(1, split, P))

        def quantize_weights(o, first, last):
            cols = slice(2 * P * first, 2 * P * last)
            values = w_bf[o][:, first:last, :].rearrange("p c n -> p (c n)")
            nc.vector.quantize_mx(out=w_codes[o][:, cols].bitcast(FP8X4), scales=w_scale[o][:, cols], in_=values)

        round_weights(0, P // 4)
        own_turned = psum.tile([P, P], F32, name="own_turned", tag="bank6")
        nc.tensor.transpose(own_turned[:], own_blocks[:], ident[:])
        nc.scalar.copy(own_cols[:], own_turned[:, 0:BLOCKS])
        own_rows = sbuf("own_rows", [P, S], F32, at=0)
        own_ps = psum.tile([P, BLOCKS, P], F32, name="own_ps", tag="bank7")
        for s in range(BLOCKS):
            nc.tensor.transpose(own_ps[:, s, :], own_cols[:, s : s + 1].to_broadcast([P, P]), ident[:])

        quantize_weights(0, 0, 1)
        quantize_weights(0, 1, 2)

        round_weights(1, 0)
        nc.scalar.copy(own_rows[:], own_ps[:].rearrange("m s p -> m (s p)"))
        quantize_weights(1, 1, 2)
        gather_x(1, 0, 1)
        quantize_weights(1, 0, 1)
        gather_x(1, 1, 2, at=4 * S)
        gather_x(1, 2, BLOCKS, at=8 * S)

        h_ps = [psum.tile([P, PACK, P], F32, name="h_ps%d" % tb, tag="bank%d" % tb) for tb in range(BLOCKS)]

        def project(tb, r, o, stop=False):
            samples = slice(P * tb, P * (tb + 1))
            hidden = slice(P * r, P * (r + 1))
            nc.tensor.matmul_mx(
                out=h_ps[tb][:, r, :],
                lhsT=w_codes[o][:, hidden].bitcast(FP8X4),
                lhsT_scale=w_scale[o][:, hidden],
                rhs=x_codes[o, tb].bitcast(FP8X4),
                rhs_scale=x_scale[X_PLANE:P, o, samples],
                start=(o, r) == (0, 0),
                stop=stop,
            )

        h_bf = [sbuf("h_bf%d" % th, [P, HALF, PACK], BF16) for th in range(2)]

        def second_pass(tb):
            order = (2, 3, 0, 1) if tb == 0 else (0, 1, 2, 3)
            for r in order:
                project(tb, r, 1, r == order[-1])
            nc.scalar.copy(h_bf[tb // 2][:, P * (tb % 2) : P * (tb % 2 + 1), :], h_ps[tb][:].rearrange("p r t -> p t r"))

        for tb in range(BLOCKS):
            for r in range(PACK):
                project(tb, r, 0)
        for tb in range(BLOCKS):
            second_pass(tb)

        def quantize_hidden(first, last):
            samples = P * (last - first)
            codes = sbuf("h_codes%d" % first, [P, samples], U32)
            scale = sbuf("h_scale%d" % first, [P, samples], U8, at=PICKED_AT + P * first)
            values = h_bf[first // 2][:, P * (first % 2) : P * (first % 2) + samples, :].rearrange("p t r -> p (t r)")
            nc.vector.quantize_mx(out=codes[:].bitcast(FP8X4), scales=scale[:], in_=values)
            return codes, scale

        e_codes = sbuf("e_codes", [P, D, P], U32)
        nc.vector.tensor_copy(e_codes[:].rearrange("p d v -> p v d"), e_table[:].bitcast(U32).indirect(sv_sb[:]))

        def product(th, d, pieces):
            y = psum.tile([P, HALF], F32, name="y%d%d" % (th, d), tag="bank%d" % Y_BANKS[d])
            start = 0
            for codes, scale in pieces:
                nc.tensor.matmul_mx(
                    out=y[:, start : start + codes.shape[1]],
                    lhsT=e_codes[:, d, :].bitcast(FP8X4),
                    lhsT_scale=e_scale[:, d, :],
                    rhs=codes[:].bitcast(FP8X4),
                    rhs_scale=scale[:],
                    start=True,
                    stop=True,
                )
                start = start + codes.shape[1]
            return y

        args = {}

        def add_own(th, d, y):
            args[th, d] = sbuf("arg%d%d" % (th, d), [P, HALF], F32)
            own_half = own_rows[:, HALF * th : HALF * (th + 1)]
            nc.vector.scalar_tensor_tensor(args[th, d][:], own_half, 2.0, y[:], ALU.mult, ALU.add)

        first_half = quantize_hidden(0, 2)
        third_block = quantize_hidden(2, 3)
        last_block = quantize_hidden(3, 4)
        for d in range(D):
            add_own(0, d, product(0, d, [first_half]))
        for d in range(D):
            add_own(1, d, product(1, d, [third_block, last_block]))

        unread = psum.tile([P, S], F32, name="unread", tag="bank%d" % Y_BANKS[0])
        nc.tensor.matmul_mx(
            out=unread[:],
            lhsT=w_codes[0][:, 0:P].bitcast(FP8X4),
            lhsT_scale=w_scale[0][:, 0:P],
            rhs=x_first[:].bitcast(FP8X4),
            rhs_scale=x_scale[X_PLANE:P, 0, :],
            start=True,
            stop=True,
        )

        sums = [psum.tile([P, P], F32, name="sum%d" % tb, tag="bank%d" % SUM_BANKS[tb]) for tb in range(BLOCKS)]

        def weighted(d, first, last):
            name = "%d%d" % (d, first)
            th = first // 2
            arg = args[th, d][:, P * (first % 2) : P * (first % 2 + last - first)]
            value = sbuf("value" + name, [P, P * (last - first)], F32)
            nc.scalar.activation(value[:], arg, ACT.Exp, bias=neg_half[:, d : d + 1], scale=0.5)
            term = sbuf("term" + name, [P, P * (last - first)], F32)
            if D * th + d < POOL_TERMS:
                nc.gpsimd.tensor_scalar(term[:], value[:], neg_alpha[:, d : d + 1], 0.0, ALU.mult, ALU.add)
            else:
                nc.vector.tensor_scalar(term[:], value[:], neg_alpha[:, d : d + 1], None, ALU.mult)
            return term

        def add_transposed(term, first, start, stop):
            for s in range(term.shape[1] // P):
                block = term[:, P * s : P * (s + 1)]
                nc.tensor.matmul(sums[first + s][:], block, ident[:], start=start, stop=stop, is_transpose=True)

        for d in range(D):
            add_transposed(weighted(d, 0, 2), 0, d == 0, d == D - 1)
        for d in range(D - 1):
            add_transposed(weighted(d, 2, BLOCKS), 2, d == 0, False)
        for tb in range(2, BLOCKS):
            add_transposed(weighted(D - 1, tb, tb + 1), tb, False, True)

        first_out = sbuf("first_out", [P, 2, P], F32, after="arg13")
        for tb in range(2):
            nc.scalar.activation(first_out[:, tb, :], sums[tb][:], ACT.Copy, scale=-1.0)
        nc.sync.dma_start(out[0:HALF, :].rearrange("(s p) v -> p s v", s=2), first_out[:])
        last_out = sbuf("last_out", [P, 2, P], F32)
        nc.scalar.activation(last_out[:, 0, :], sums[2][:], ACT.Copy, scale=-1.0)
        nc.vector.tensor_scalar(last_out[:, 1, :], sums[3][:], -1.0, None, ALU.mult)
        nc.sync.dma_start(out[HALF:S, :].rearrange("(s p) v -> p s v", s=2), last_out[:])
